import numpy as np, ml_dtypes
CORES = [242,247,114,119]
N = 4
BF = ml_dtypes.bfloat16
def gentries(a):
    return np.ascontiguousarray(a.reshape(8, 16, -1).transpose(0, 2, 1)).reshape(8, -1)
def gtable(e):
    e = np.asarray(e); return np.ascontiguousarray(e.reshape(8, -1, 16).transpose(0, 2, 1)).reshape(128, -1).astype(np.int32)
V, G, NB, RO, HP = 768, 384, 1, 5, 3
H = NB * G
S = V + H
def vals(rng, n):
    p = rng.choice(np.array([0.5, 1.0, 1.0, 2.0]), (N, 8, 1, n)) * rng.choice(np.array([0.7, 1.0, 1.4]), (N, 8, 16, 1))
    return np.minimum((256 * rng.random((N, 8, 16, n)) ** p).astype(np.int64), 255)
def parts(rng):
    m = rng.choice(np.array([2, 4, 16, 16]), (N, 8, 1, V))
    e = np.take_along_axis(rng.integers(0, S, (N, 8, 16, V)), (rng.random((N, 8, 16, V)) * m).astype(np.int64), axis=2)
    share = np.where(rng.random((N, 8, 1, V)) < 0.03125, 1.0, rng.choice(np.array([0.0, 0.0, 0.1, 0.3]), (N, 8, 1, V)))
    e = e + S * (rng.random((N, 8, 16, V)) < share)
    u = rng.integers(0, 16 * V, (N, 8, 16, V)); s = rng.integers(0, V // 4, (N, 8, H))
    h = rng.choice(np.array([200, 600, 1000, 1300, 1600]), (N, 8, RO)) + rng.integers(0, 200, (N, 8, RO))
    return e, u, vals(rng, V), vals(rng, V), vals(rng, S), s, h
def pack(e, u, x, b, y, s, h):
    flat = lambda a: np.ascontiguousarray(a.reshape(N, 128, a.shape[-1]))
    return {"ent": flat(e).astype(np.int32), "usr": flat(u).astype(np.int32), "xa": flat(x).astype(np.float32).astype(BF), "bn": flat(b).astype(np.float32).astype(BF),
            "yc": flat(y).astype(np.float32).astype(BF), "snd": np.stack([gtable(a) for a in s]), "th": np.ascontiguousarray(h).astype(np.int32)}
def setup_inputs(rng):
    return pack(*parts(rng))
def setup_inputs_spread(rng):
    e, u, x, b, y, s, h = parts(rng)
    def uneven(n):
        v = np.minimum((np.exp2(8 * rng.random((N, 8, 1, n))) * rng.random((N, 8, 16, n))).astype(np.int64), 255)
        return np.where(rng.random((N, 8, 1, n)) < 0.5, v, 255 - v)
    src = np.minimum((S * rng.random((N, 8, 16, V)) ** rng.choice(np.array([0.3, 1.0, 3.0]), (N, 8, 1, 1))).astype(np.int64), S - 1)
    e = src + S * (e >= S)
    w = np.minimum((V * rng.random((N, 8, 16, V)) ** rng.choice(np.array([0.5, 1.0, 2.0]), (N, 8, 1, 1))).astype(np.int64), V - 1)
    u = 16 * w + rng.integers(0, 16, (N, 8, 16, V))
    h = np.minimum(np.exp2(12 * rng.random((N, 8, RO))).astype(np.int64) - 1, 4080)
    return pack(e, u, uneven(V), uneven(V), uneven(S), s, h)
def setup_inputs_ends(rng):
    def two(n):
        mode = rng.integers(0, 3, (N, 8, 1, n)); bits = rng.integers(0, 2, (N, 8, 16, n))
        return 255 * np.where(mode == 0, 0, np.where(mode == 1, 1, bits))
    def mix(top, share, other):
        return np.where(rng.random((N, 8, 16, V)) < share, top * rng.integers(0, 2, (N, 8, 16, V)), other)
    x, b, y = two(V), two(V), two(S); v = np.arange(V)
    near = rng.choice(np.array([0, V - 1, V, S - 1, S, S + V - 1, S + V]), (N, 8, 16, V))
    e = mix(2 * S - 1, 0.75, np.where(rng.random((N, 8, 16, V)) < 0.5, near, rng.integers(0, 2 * S, (N, 8, 16, V))))
    u = mix(16 * V - 1, 0.75, rng.integers(0, 16 * V, (N, 8, 16, V)))
    none = v % 8 == 2; one = rng.integers(0, 16, (N, 8, 1, V))
    e = np.where(none, 2 * S - 1, np.where(np.arange(16)[:, None] == one, 0, e))
    top = np.where(np.arange(8) % 2 == 0, 255, 0)[None, :, None]
    x[:, :, :, 0] = top; y[:, :, :, 0] = top; b[:, :, :, 0] = 0; e[:, :, :, 0] = 0
    u[:, :4, 0, 0] = 0; u[:, 4:, 0, 0] = 16 * V - 1
    far = list(range(1, 8)) + list(range(V - 8, V))
    x[:, :, :, far] = 255 - top[..., None]; b[:, :, :, far] = 0; e[:, :, :, far] = 0; u[:, :, 0, far] = 16 * V - 1
    lone = list(range(12, 16)) + list(range(V - 12, V - 8))
    x[:, :, :, lone] = 255 - top[..., None]; e[:, :, :15, lone] = 2 * S - 1; e[:, :, 15, lone] = 0
    still = list(range(8, 12))
    x[:, :, :, still] = top[..., None]; b[:, :, :, still] = 0; e[:, :, :, still] = 0; u[:, :, 0, still] = 0
    s = (V // 4 - 1) * rng.integers(0, 2, (N, 8, H))
    h = 4080 * rng.integers(0, 2, (N, 8, RO)); h[:, 0, 0] = 0; h[:, 1, 0] = 0; h[:, 6, 0] = 4080; h[:, 7, 0] = 4080; h[N - 1, :, 1] = 4080
    return pack(e, u, x, b, y, s, h)
def setup_inputs_corners(rng):
    e, u, x, b, y, s, h = parts(rng); v = np.arange(V)
    src = rng.integers(0, S, (N, 8, 16, V)); src[:, 3] = v; src[:, 5] = rng.integers(V, S, (N, 16, V))
    src[:, 6] = rng.choice(np.array([0, V - 1, V, S - 1]), (N, 16, V))
    cl = rng.choice(np.array([0, 1, 2, 15, 16]), (N, 8, 1, V)); cl[:, 5] = 16
    o = np.argsort(rng.random((N, 8, 16, V)), axis=2); o[:, 0] = np.arange(15, -1, -1)[:, None]; o[:, 7] = np.arange(16)[:, None]
    gone = o >= cl; gone[:, 4, 15] = True
    q = rng.integers(0, 16, (N, 8, 16, V))
    u[:, 1] = 16 * np.where(v < V // 2, v, v ^ 1) + q[:, 1]; u[:, 2] = 16 * ((v + 1) % V) + q[:, 2]
    u[:, 3] = 16 * rng.choice(np.array([0, V - 1]), (N, 16, V)) + q[:, 3]; u[:, 4] = 16 * (u[:, 4] >> 4) + 15
    e = src + S * gone
    for a in range(N):
        turn = np.roll(np.arange(8), a); e[a] = e[a][turn]; u[a] = u[a][turn]
    e[1, :, :, 2::4] = e[1, :, :, 2::4] % S + S
    s[:, ::2] = rng.choice(np.array([0, V // 4 - 1]), (N, 4, H))
    h = rng.choice(np.array([0, 1, 300, 1000, 1400, 4079, 4080]), (N, 8, RO))
    return pack(e, u, x, b, y, s, h)
def setup_inputs_limits(rng):
    e, u, x, b, y, s, h = parts(rng); m = V // 4; a = np.arange(N)[:, None]; g = np.arange(8)[None, :]; k = np.arange(16)[:, None]; p = rng.permutation(N)
    base = np.where((a + g) % 2 == 0, rng.integers(2048, 3824, (N, 8)), rng.integers(64, 1700, (N, 8)))
    eff = base[..., None] + np.argsort(rng.random((N, 8, m)), axis=2)
    d = (eff[:, :, None] + np.argsort(rng.random((N, 8, 16, m)), axis=2)) // 16
    mv = (rng.random((N, 8, 8, m)) * (np.minimum(255 - d[:, :, :8], d[:, :, 8:]) + 1)).astype(np.int64)
    d = np.concatenate([d[:, :, :8] + mv, d[:, :, 8:] - mv], axis=2)
    fv = (rng.random(d.shape) * (np.minimum(128, 255 - d) + 1)).astype(np.int64)
    x[..., 3::4] = np.where((fv >= d) & (rng.random(d.shape) < 0.5), fv - d, fv + d)
    b[..., 3::4] = np.where((fv < 128) & (rng.random(d.shape) < 0.5), 127 - fv, 127 + fv)
    w = 4 * np.argsort(rng.random((N, 8, 4, m)), axis=3) + 3
    u = 16 * w.transpose(0, 1, 3, 2).reshape(N, 8, 1, V) + rng.integers(8, 16, (N, 8, 16, V))
    e = np.where(k == rng.integers(0, 16, (N, 8, 1, V)), e % S, e)
    o = np.argsort(rng.random((N, 8, S)), axis=2); lo, hi = o[..., 0], o[..., 1]
    y[a, g, :, lo] = 0; y[a, g, :, hi] = 255; lo = lo[..., None]; hi = hi[..., None]
    c = rng.integers(0, 2, (N, 8, m)) == 1
    e[..., 3::4] = e[..., 3::4] % S + S * (k < 8)
    e[:, :, 0, 3::4] = S + np.where(c, lo, hi); e[:, :, 7, 3::4] = S + np.where(c, hi, lo)
    h = base[..., None] + rng.integers(32, m - 64, (N, 8, RO))
    h = h - (h & 15) + rng.choice(np.array([0, 1, 2, 3, 4, 5, 10, 11, 12, 13, 14, 15]), h.shape)
    h[p[:2], :, 0] = 4080; h[p[2:], rng.integers(0, 8, N - 2), 0] = 4080; h[p[1], :, 1] = 0
    few = 4 * rng.permutation(m)[:int(rng.integers(1, 32))]; ez = e[p[1], int(rng.integers(0, 8))]
    ez[:, few] = ez[:, few] % S + S
    e[p[1], ::2, :, 1::4] = e[p[1], ::2, :, 1::4] % S + S
    return pack(e, u, x, b, y, s, h)
def setup_inputs_ties(rng):
    e, u, x, b, y, s, h = parts(rng)
    base = rng.choice(np.array([0, 100, 252]), (N, 8, 1, 1)); base[:, 0] = 252; base[:, 7] = 0
    x = base + rng.integers(0, 4, (N, 8, 16, V)); y = base + rng.integers(0, 4, (N, 8, 16, S)); b = rng.integers(0, 4, (N, 8, 16, V))
    x[:, :, :, 1::4] = x[:, :, :, 0::4]; x[:, :, :, 3::4] = x[:, :, :, 2::4]
    h = rng.integers(0, 40, (N, 8, RO))
    return pack(e, u, x, b, y, s, h)
def check_inputs(d):
    bad = []
    for k, lo, hi in (("ent", 0, 2 * S - 1), ("usr", 0, 16 * V - 1), ("xa", 0, 255), ("bn", 0, 255), ("yc", 0, 255), ("snd", 0, V // 4 - 1), ("th", 0, 4080)):
        v = np.asarray(d[k]).astype(np.float64)
        if not np.all((v >= lo) & (v <= hi)): bad.append("range of " + k)
        elif np.any(v != np.floor(v)): bad.append("whole numbers of " + k)
    return bad
def mid(a, b):
    return np.abs(((np.maximum.reduce(a, axis=3) + np.minimum.reduce(a, axis=3)) >> 1) - b)
def nodes(a, dtype):
    return np.ascontiguousarray(np.asarray(a).astype(np.float32).astype(dtype).reshape(N, 8, 16, -1).transpose(0, 1, 3, 2))
def reference(ent, usr, xa, bn, yc, snd, th):
    e, u = nodes(ent, np.int64), nodes(usr, np.int64); x, b, y = nodes(xa, np.int32), nodes(bn, np.int32), nodes(yc, np.int32)
    sl = np.stack([gentries(a) for a in snd]).astype(np.int64).reshape(N, 8, NB, 4, G // 4) * 4 + np.arange(4)[:, None]
    sl = sl.reshape(N, 8, NB, G); hh = th.astype(np.int64)
    r3 = np.arange(N)[:, None, None]; g3 = np.arange(8)[None, :, None]; r4 = r3[..., None]; g4 = g3[..., None]; sixteen = np.arange(16)
    gone = np.zeros(N, np.int64)
    for t in range(RO):
        w = [x]
        for n in range(1, NB + 1):
            q = (np.arange(N) + n) % N
            w.append(x[q][r3, g3, sl[q, :, n - 1]])
        w = np.concatenate(w + [y], axis=2)
        own = np.arange(t % 4, V, 4)
        eo = e[:, :, own]; xo = x[:, :, own]; bo = b[:, :, own]
        src = w[r4, g4, eo]
        score = np.add.reduce(np.abs(src - xo[:, :, :, None]), axis=4); clean = eo < S; some = np.any(clean, axis=3)
        k = np.argmin(np.where(clean, score, 9999), axis=3)
        hit = (sixteen == k[..., None]) & some[..., None]
        ek = np.take_along_axis(eo, k[..., None], 3)[..., 0]
        cv = w[r3, g3, np.where(some, ek + S, 0)]
        f0 = mid(src, bo); z = mid(np.where(hit[..., None], cv[:, :, :, None], src), bo); z0 = z
        c = np.broadcast_to(own, some.shape); dead = np.zeros(some.shape, bool)
        for hop in range(HP):
            p = u[r3, g3, c, np.add.reduce(z, axis=3) & 15]
            c = p >> 4; at = sixteen == (p & 15)[..., None]; ew = e[r3, g3, c]
            dead = dead | np.any(at & (ew >= S), axis=3)
            z = mid(np.where(at[..., None], z[:, :, :, None], w[r4, g4, ew]), b[r3, g3, c])
        D = np.where(dead, 0, np.add.reduce(np.abs(z - x[r3, g3, c]), axis=3))
        stay = some & (D <= hh[:, :, t][..., None] + (gone & 31)[:, None, None])
        e[:, :, own] = np.where(stay[..., None] & hit, eo + S, eo)
        x[:, :, own] = np.where(stay[..., None], z0, f0)
        gone = np.add.reduce(stay.astype(np.int64), axis=(1, 2))
    return {"ye": np.ascontiguousarray(e.transpose(0, 1, 3, 2)).reshape(N, 128, V).astype(np.float32), "yx": np.ascontiguousarray(x.transpose(0, 1, 3, 2)).reshape(N, 128, V).astype(np.float32).astype(BF)}

@@ -1,0 +1,605 @@
+import numpy as np
+from concourse.mybir import AluOpType as OP, ActivationFunctionType as AF, AxisListType as AX
+
+V, NG, NBT, PARTS = 768, 384, 96, 2
+ZC = 288
+XO = ZC
+XG = ZC + V
+YO = XG + NG
+XE = ZC + 2304
+MAGIC = 12582912.0
+BF2 = "bfloat16"
+SCRATCH = {}
+WHERE = {}
+
+
+def _buf(name, cols, dtype=BF2, where="sbuf", rows=128, pool=True):
+    if not pool or where != "sbuf" or rows != 128 or cols > 144:
+        SCRATCH[name] = (where, [rows, cols], dtype)
+        WHERE[name] = (name, 0, cols, dtype)
+        return
+    p = "pool_" + dtype
+    lo = SCRATCH[p][1][1] if p in SCRATCH else 0
+    SCRATCH[p] = ("sbuf", [128, lo + (cols + 15) // 16 * 16], dtype)
+    WHERE[name] = (p, lo, cols, dtype)
+
+
+for _b in range(2):
+    _buf("xw%d" % _b, XE)
+    for _n in ("ga", "gb", "mt", "mx", "mn", "m0", "n0"):
+        _buf("%s%d" % (_n, _b), 16 * NBT)
+    for _n in ("f0", "hit", "pq", "bw", "xv", "z3", "da", "st", "sd", "hs", "da1", "da2", "da3"):
+        _buf("%s%d" % (_n, _b), NBT)
+    _buf("pw%d" % _b, NBT, "float16")
+    for _n in ("hot", "aa", "ll", "of", "kt", "r1", "mb", "mbt"):
+        _buf("%s%d" % (_n, _b), NBT, "float32")
+    _buf("rm%d" % _b, 112, "float32")
+    _buf("ri%d" % _b, NBT)
+    _buf("ou%d" % _b, NBT, "uint16")
+    _buf("eu%d" % _b, NBT, "uint16")
+    _buf("wl%d" % _b, 8, "uint16")
+for _n in ("enti", "usri", "uw", "uq"):
+    _buf(_n, V, "int32")
+_buf("entt", V, "float32")
+_buf("yef", V, "float32")
+_buf("ct", V)
+_buf("bt", V)
+_buf("sndi", 24, "int32", "sbuf", 128, False)
+_buf("sndu", 24, "uint16")
+_buf("thi", 5, "int32", "sbuf", 8)
+_buf("thf", 5, "float32", "sbuf", 8)
+for _n, _w in (("tha", 5), ("thc", 5), ("rr", 1), ("pf", 4), ("bc", 4), ("py", 1), ("mgc", 1), ("nzc", 1),
+               ("rg", NBT), ("idf", 128)):
+    _buf(_n, _w, "float32")
+for _n, _w in (("rri", 1), ("rrj", 1), ("ji", NBT), ("jj", NBT), ("pi", 4), ("pj", 4), ("bi", 4)):
+    _buf(_n, _w, "int32")
+_buf("gs0", NG)
+for _n in range(4):
+    _buf("gt%d" % _n, NBT, BF2, "sbuf", 128, False)
+    _buf("land%d" % _n, NBT, BF2, "sbuf", 128, False)
+for _n in ("one", "idn", "half", "neg", "i256", "i1152", "b16", "b1", "b4096", "dead"):
+    _buf(_n, 128)
+for _n in ("one144", "blkh", "blk", "wsel", "w32", "w16", "wn16"):
+    _buf(_n, 144)
+_buf("blkf", 128, "float16")
+for _n in ("oe", "ee0", "ee"):
+    _buf(_n, 128, "float32", "sbuf", 8)
+for _n in ("kc", "yc96", "jc", "mask", "cm", "cq"):
+    _buf(_n, NBT)
+_buf("ab1", 16 * NBT)
+_buf("rx", 16 * NBT)
+_buf("rn", 16 * NBT)
+for _n in range(8):
+    _buf("p%d" % _n, 512, "float32", "psum")
+LOADS = ["snd", "xa", "ent", "yc", "bn", "usr", "th"]
+SEMAPHORES = ["sv", "ss", "st", "sg", "loc", "o0", "o1", "o2", "o3"] + ["ld_" + n for n in LOADS] + ["arr%d" % t for t in range(5)]
+QS = {"v": "sv", "s": "ss", "t": "st", "g": "sg"}
+PLAN = {}
+
+
+def _overlap(a, b):
+    if a[1] >= b[2] or b[1] >= a[2]:
+        return False
+    return not (a[3] > 1 and a[3] == b[3] and (a[1] - b[1]) % a[3])
+
+
+def _bank(r):
+    return r[0][0] == "p" and r[0][1:].isdigit()
+
+
+def _edges(ops):
+    hist = {}
+    for i, o in enumerate(ops):
+        pre = {}
+        both = [(False, r) for r in o["rd"]] + [(True, r) for r in o["wr"]]
+        for wr, r in both:
+            for (r2, j, w2) in hist.get(r[0], ()):
+                if j == i or not (_bank(r) or ((wr or w2) and _overlap(r, r2))):
+                    continue
+                pre[j] = pre.get(j, False) or ops[j]["q"] != o["q"] or (w2 and (not wr or o["q"] != "t")) or ops[j]["dma"]
+        for j in o["after"]:
+            pre[j] = True
+        for wr, r in both:
+            h = hist.setdefault(r[0], [])
+            if _bank(r):
+                if h and ops[h[-1][1]]["q"] != o["q"]:
+                    h[:] = [e for e in h if e[1] == i or ops[e[1]]["q"] != o["q"]]
+            elif wr:
+                h[:] = [e for e in h if e[1] == i or not (r == e[0] or (r[3] == 1 and r[1] <= e[0][1] and e[0][2] <= r[2]))]
+            h.append((r, i, wr))
+        o["pre"] = pre
+
+
+def _cost(o, m):
+    f, n, gath = o["cost"]
+    return f * m[0] + max(64, n * (m[2] if gath else 1)) * 1.0e-3 * m[1] if n else f
+
+
+def _schedule(ops, succ, m, slack, noise):
+    n = len(ops)
+    cost = [_cost(o, m) for o in ops]
+    pri = [0.0] * n
+    for i in range(n - 1, -1, -1):
+        x = 0.0
+        for j in succ[i]:
+            x = max(x, pri[j] + (m[3] if ops[j]["pre"][i] else 0.0))
+        pri[i] = x + cost[i] + ops[i]["lag"] * m[4]
+    pri = [pri[i] + float(noise[i]) for i in range(n)]
+    left = [len(o["pre"]) for o in ops]
+    rdy = [0.0] * n
+    cand = {}
+    for i in range(n):
+        if left[i] == 0:
+            cand.setdefault(ops[i]["q"], []).append(i)
+    free = {}
+    order = []
+    while True:
+        q = None
+        for k in cand:
+            if cand[k]:
+                s = max(free.get(k, 0.0), min(rdy[i] for i in cand[k]))
+                if q is None or s < s0:
+                    q, s0 = k, s
+        if q is None:
+            return order
+        pick = None
+        for i in cand[q]:
+            if rdy[i] <= s0 + slack and (pick is None or pri[i] > pri[pick]):
+                pick = i
+        cand[q].remove(pick)
+        order.append(pick)
+        st = max(s0, rdy[pick])
+        free[q] = st + cost[pick]
+        for j in succ[pick]:
+            e = free[q] + ops[pick]["lag"] * m[4] + m[3] if ops[j]["pre"][pick] else st
+            rdy[j] = max(rdy[j], e)
+            left[j] -= 1
+            if left[j] == 0:
+                cand.setdefault(ops[j]["q"], []).append(j)
+
+
+def _length(ops, order, m):
+    free, fin, top = {}, [0.0] * len(ops), 0.0
+    for i in order:
+        o = ops[i]
+        t = free.get(o["q"], 0.0)
+        for j in o["pre"]:
+            if o["pre"][j]:
+                t = max(t, fin[j] + m[3])
+        free[o["q"]] = t + _cost(o, m)
+        fin[i] = free[o["q"]] + o["lag"] * m[4]
+        top = max(top, fin[i])
+    return top
+
+
+MODELS = [(1.0, 1.04, 1.56, 0.06, 1.0), (0.4, 0.9, 1.2, 0.06, 1.0), (0.5, 1.2, 2.0, 0.1, 1.3), (1.0, 0.9, 1.3, 0.2, 1.3)]
+STEPS = 1600
+
+
+def _plan(ops):
+    succ = [[] for _ in ops]
+    for i, o in enumerate(ops):
+        for j in o["pre"]:
+            succ[j].append(i)
+    keys = 1 + max(o["key"] for o in ops)
+    rng = np.random.RandomState(5)
+    cur = np.full(keys + 1, 2.0)
+    cur[keys] = 0.0
+    best = None
+    for step in range(STEPS):
+        c = cur.copy()
+        if step:
+            if rng.rand() < 0.5:
+                for _i in range((1, 2, 4, 10, 25)[rng.randint(5)]):
+                    c[rng.randint(keys)] = 0.25 * rng.randint(26)
+            else:
+                a, w = rng.randint(keys), (3, 8, 20, 60)[rng.randint(4)]
+                hi = min(keys, a + w)
+                c[a:hi] = np.clip(c[a:hi] + 0.25 * rng.randint(-6, 7), 0.0, 6.25)
+        order = _schedule(ops, succ, MODELS[0], 0.12, [float(c[o["key"]]) for o in ops])
+        score = []
+        for m in range(len(MODELS)):
+            score.append(_length(ops, order, MODELS[m]))
+            if best and m == 0 and score[0] > 1.006 * best[1][0]:
+                break
+        if len(score) < len(MODELS):
+            continue
+        if not best:
+            base = score
+        x = sum(a / b for a, b in zip(score, base))
+        if not best or x <= best[0]:
+            best, cur = (x, score, order), c
+    return best[2]
+
+
+def rank_program(g, core, T, topo):
+    rank = T.rank_of(core)
+    if rank is None:
+        return
+    ops = []
+    start = []
+    eng = {"v": g.vector, "s": g.scalar, "t": g.tensor, "g": g, "y": g.sync}
+
+    def add(q, fn, rd, wr, cost, lag=0.0, sem=None, amount=1, dma=False, after=()):
+        ops.append({"q": q, "fn": fn, "key": len(ops) - start[0] if start else -1, "rd": rd, "wr": wr, "cost": cost, "lag": lag, "sem": sem, "amount": amount,
+                    "dma": dma, "after": list(after), "remote": False})
+        return len(ops) - 1
+
+    def A(name, lo=0, hi=None, step=1):
+        buf, o, cols, _d = WHERE[name]
+        if hi is None:
+            hi = cols
+        ap = T[buf][:, o + lo:o + hi] if step == 1 else T[buf][:, o + lo:o + hi:step]
+        return (ap, [(name, lo, hi, step)], (hi - lo + step - 1) // step, False)
+
+    def IND(w, off):
+        return (w[0].indirect(off[0]), w[1] + off[1], 16 * off[2], True)
+
+    def regs(*xs):
+        out = []
+        for x in xs:
+            if isinstance(x, tuple):
+                out += x[1]
+        return out
+
+    def val(x):
+        return x[0] if isinstance(x, tuple) else x
+
+    def kind(x):
+        return WHERE[x[1][0][0]][3]
+
+    def half(*xs):
+        return 0.5 if all(kind(x) in ("bfloat16", "float16", "uint16") for x in xs) else 1
+
+    def vc(n, gath=False):
+        return (0.055, n, gath)
+
+    def tt(out, a, b, op):
+        n = out[2] * (1 if a[3] or _bank(a[1][0]) or _bank(b[1][0]) else 2)
+        return add("v", lambda e: e.tensor_tensor(out=out[0], in0=a[0], in1=b[0], op=op), regs(a, b), regs(out), vc(n, a[3]))
+
+    def ts(out, a, s1, s2, op0, op1=None):
+        if op1 is None:
+            fn = lambda e: e.tensor_scalar(out=out[0], in0=a[0], scalar1=val(s1), scalar2=None, op0=op0)
+        else:
+            fn = lambda e: e.tensor_scalar(out=out[0], in0=a[0], scalar1=val(s1), scalar2=val(s2), op0=op0, op1=op1)
+        return add("v", fn, regs(a, s1, s2), regs(out), vc(out[2] * half(out, a)))
+
+    def vcp(out, a):
+        return add("v", lambda e: e.tensor_copy(out=out[0], in_=a[0]), regs(a), regs(out),
+                   vc(out[2], True) if a[3] else vc(out[2] * half(out, a)))
+
+    def scan(out, d0, d1, op0, op1):
+        return add("v", lambda e: e.tensor_tensor_scan(out=out[0], data0=d0[0], data1=d1[0], initial=0.0, op0=op0, op1=op1),
+                   regs(d0, d1), regs(out), vc(out[2] * half(out, d0, d1)))
+
+    def vtr(out, a):
+        return add("v", lambda e: e.transpose(out=out[0], in_=a[0]), regs(a), regs(out), vc(out[2]))
+
+    def fill(out, x):
+        return add("v", lambda e: e.memset(out[0], x), [], regs(out), vc(out[2] * half(out)))
+
+    def act(out, a, func, bias=None):
+        if bias is None:
+            fn = lambda e: e.activation(out=out[0], in_=a[0], func=func)
+        else:
+            fn = lambda e: e.activation(out=out[0], in_=a[0], func=func, bias=val(bias))
+        return add("s", fn, regs(a, bias), regs(out), (0.065, out[2], a[3]))
+
+    def mm(out, l, r, start, stop):
+        return add("t", lambda e: e.matmul(out[0], l[0], r[0], start, stop), regs(l, r), regs(out),
+                   (0.03, max(64, r[2]) * (4 if kind(r) == "float32" else 1), False))
+
+    def sel(out, a, pattern, op, base, cm):
+        return add("g", lambda e: e.affine_select(out=out[0], in_=a[0], pattern=pattern, compare_op=op, fill=0.0, base=base,
+                                                 channel_multiplier=cm), regs(a), regs(out), (0.2, 2 * out[2], False))
+
+    def iota(out, pattern, base, cm):
+        if kind(out) != "int32":
+            fn = lambda e: e.iota(out[0], pattern=pattern, base=base, channel_multiplier=cm, allow_small_or_imprecise_dtypes=True)
+        else:
+            fn = lambda e: e.iota(out[0], pattern=pattern, base=base, channel_multiplier=cm)
+        return add("g", fn, [], regs(out), (0.15, 2 * out[2], False))
+
+    def load(q, name, out):
+        return add(q, lambda e: e.dma_start(out=out[0], in_=T[name][:, :]), [], regs(out), (0.1, 0, False), 2.2,
+                   "ld_" + name, 16, True)
+
+    dst = T.cores[(rank - 1) % len(T.cores)]
+    src = T.cores[(rank + 1) % len(T.cores)]
+    rid, pid = topo.addr(dst, core)
+    es = topo.engines(core, dst)[:8]
+    mask = sum(1 << e for e in es)
+    n_in = len(topo.engines(src, core)[:8])
+
+    def send(slot, a, land):
+        j = add("g", lambda e: e.remote_dma(land[0], a[0], T.sem["arr%d" % slot], T.sem.loc, pid, rid, mask),
+                regs(a), [], (0.3, 0, False))
+        ops[j]["remote"] = True
+        add("x", None, [], regs(land), (0.0, 0, False), 2.5, "arr%d" % slot, n_in, True, (j,))
+
+    own0 = A("xw0", XO, XO + V)
+    load("y", "snd", A("sndi"))
+    load("s", "xa", own0)
+    load("y", "ent", A("enti"))
+    load("y", "yc", A("xw0", YO, XE))
+    load("s", "bn", A("bt"))
+    load("y", "usr", A("usri"))
+    load("s", "th", A("thi"))
+    for c in range(4):
+        ts(A("sndu", 6 * c, 6 * c + 6), A("sndi", 6 * c, 6 * c + 6), 4, c, OP.mult, OP.add)
+    act(A("gs0"), IND(own0, A("sndu")), AF.Copy)
+    send(4, A("gs0"), A("xw0", XG, XG + NG))
+
+    fill(A("one"), 1.0)
+    fill(A("one144"), 1.0)
+    fill(A("oe"), 1.0)
+    sel(A("idn"), A("one"), [[-1, 128]], OP.is_equal, 0, 1)
+    sel(A("blkh"), A("one144"), [[-16, 9], [0, 16]], OP.is_ge, 0, 1)
+    sel(A("blk"), A("blkh"), [[16, 9], [0, 16]], OP.is_ge, 15, -1)
+    sel(A("wsel"), A("blk"), [[0, 9], [1, 16]], OP.is_equal, -15, 0)
+    sel(A("ee0"), A("oe"), [[1, 128]], OP.is_ge, 0, -16)
+    sel(A("ee"), A("ee0"), [[-1, 128]], OP.is_ge, 15, 16)
+    iota(A("ji"), [[1, NBT]], 128, -1)
+    iota(A("jc"), [[1, NBT]], 0, 0)
+    iota(A("pi"), [[0, 4]], 0, 1)
+    iota(A("bi"), [[NBT, 4]], 0, 0)
+    for name, of, x in (("half", "idn", 0.5), ("neg", "idn", -1.0), ("i256", "idn", 256.0), ("i1152", "idn", 1152.0),
+                        ("idf", "idn", 1.0), ("w32", "wsel", 32.0), ("w16", "wsel", 16.0),
+                        ("wn16", "wsel", -16.0)):
+        ts(A(name), A(of), x, None, OP.mult)
+    for name, x in (("b16", 0.0625), ("b1", 1.0), ("b4096", 4096.0), ("dead", -8192.0), ("blkf", 1.0)):
+        ts(A(name), A("blk", 0, 128), x, None, OP.mult)
+    ts(A("pj"), A("pi"), 15, None, OP.bitwise_and)
+    vcp(A("pf"), A("pj"))
+    ts(A("py"), A("pf", 0, 1), -0.0625, None, OP.mult)
+    ts(A("bc"), A("pf"), -4096.0, None, OP.mult)
+    tt(A("bc"), A("bc"), A("bi"), OP.add)
+    ts(A("jj"), A("ji"), 15, None, OP.bitwise_and)
+    ts(A("mask"), A("jj"), 0, -4096.0, OP.not_equal, OP.mult)
+    ts(A("kc"), A("one", 0, NBT), A("pf", 0, 1), None, OP.mult)
+    ts(A("yc96"), A("one", 0, NBT), A("py"), None, OP.mult)
+    for name, x, y in (("cm", MAGIC, None), ("cq", -0.25, None), ("rx", 1.0, 0.0), ("rn", 0.0, 512.0), ("rg", 0.0, 1048576.0),
+                       ("rm0", 0.0, None), ("rm1", 0.0, None), ("mgc", -MAGIC, None), ("nzc", -float(ZC), None)):
+        fill(A(name), x)
+        if y is not None:
+            fill(A(name, 0, WHERE[name][2], 16), y)
+    ts(A("entt"), A("enti"), float(ZC), None, OP.add)
+    ts(A("ct"), A("enti"), 1152.0, 1024.0, OP.is_ge, OP.mult)
+    ts(A("uw"), A("usri"), 4, None, OP.logical_shift_right)
+    ts(A("uq"), A("usri"), 15, None, OP.bitwise_and)
+    vcp(A("thf"), A("thi"))
+    mm(A("p0", 0, 5), A("ee"), A("thf"), True, True)
+    vcp(A("tha"), A("p0", 0, 5))
+    vcp(A("thc", 0, 1), A("tha", 0, 1))
+    act(A("xw1", XO, XO + V), own0, AF.Copy)
+    act(A("xw1", YO, XE), A("xw0", YO, XE), AF.Copy)
+    act(A("xw1", XG, XG + NG), A("xw0", XG, XG + NG), AF.Copy)
+
+    I = A("idn")
+    RXL = A("rx", 0, NBT)
+
+    def sl(b, t, base=0):
+        return base + 384 * b + t % 4, base + 384 * (b + 1), 4
+
+    def xcopy(b, t):
+        for m in range(4):
+            mm(A("p%d" % (4 + b), m, 384, 4), I, A("xw%d" % b, *sl(b, t, XO)), True, True)
+
+    def scans(G, X, N, parts):
+        w = 16 * NBT // parts
+        for m in range(parts):
+            lo, hi = w * m, w * m + w
+            scan(A(X, lo, hi), A("rx", lo, hi), A(G, lo, hi), OP.mult, OP.max)
+            scan(A(N, lo, hi), A("rn", lo, hi), A(G, lo, hi), OP.add, OP.min)
+
+    def gather(out, win, off, vec=()):
+        w = NBT // PARTS
+        for m in range(PARTS):
+            o, i = A(out, 16 * w * m, 16 * w * m + 16 * w), IND(win, A(off, w * m, w * m + w))
+            if m in vec:
+                vcp(o, i)
+            else:
+                act(o, i, AF.Copy)
+
+    def fin(bank, bv, X, N, out):
+        p = A(bank, 0, NBT)
+        mm(p, I, A("cq"), True, False)
+        mm(p, A("neg"), bv, False, False)
+        mm(p, A("half"), A(X, 15, 16 * NBT, 16), False, False)
+        mm(p, A("half"), A(N, 15, 16 * NBT, 16), False, False)
+        mm(p, I, A("cm"), False, True)
+        act(out, p, AF.Abs, A("mgc"))
+
+    for b in range(2):
+        xcopy(b, 0)
+    for t in range(5):
+        last = t == 4
+        start[:] = [len(ops)]
+        for b in range(2):
+            s = str(b)
+            vcp(A("eu" + s), A("entt", *sl(b, t)))
+            gather("ga" + s, A("xw" + s), "eu" + s, (1,) if b == 0 else ())
+        if last:
+            act(A("yef"), A("entt"), AF.Identity, A("nzc"))
+            start[0] += 1
+        for b in range(2):
+            s = str(b)
+            b0, b1 = "p%d" % (2 * b), "p%d" % (2 * b + 1)
+            xb, fb = "p%d" % (4 + b), "p%d" % (6 + b)
+            K = A(b0, 0, NBT)
+            mm(K, A("i256"), A("ct", *sl(b, t)), True, False)
+            mm(K, I, A("kc"), False, False)
+            for k in range(4):
+                tt(A("mt" + s, 384 * k, 384 * k + 384), A(xb, 0, 384), A("ga" + s, k, 1536, 4), OP.subtract if b else OP.max)
+            if b:
+                for lo in range(0, 16 * NBT, 4 * NBT):
+                    act(A("ab1", lo, lo + 4 * NBT), A("mt1", lo, lo + 4 * NBT), AF.Abs)
+            else:
+                for k in range(16):
+                    mm(K, A("wn16", 15 - k, 143 - k), A("ga0", k, 1536, 16), False, False)
+            for k in sorted(range(16), key=lambda k: k % 4):
+                lo = 384 * (k % 4)
+                mm(K, A("w16" if b else "w32", 15 - k, 143 - k), A("ab1" if b else "mt0", lo + k // 4, lo + 384, 4), False, k == 15)
+            vtr(A("kt" + s), K)
+            scan(A("r1" + s), A("rg"), A("kt" + s), OP.add, OP.min)
+            ts(A("rm" + s, 15, NBT, 16), A("r1" + s, 15, NBT, 16), 262143.0, None, OP.min)
+            scan(A("mb" + s), RXL, A("rm" + s, 15, 15 + NBT), OP.mult, OP.add)
+            vtr(A("mbt" + s), A("mb" + s))
+            tt(A("hit" + s), K, A("mbt" + s), OP.is_equal)
+            E = A(b1, 0, NBT)
+            mm(E, A("idf"), A("entt", *sl(b, t)), True, False)
+            mm(E, A("i1152"), A("hit" + s), False, True)
+            vcp(A("ou" + s), E)
+            gather("gb" + s, A("xw" + s), "ou" + s)
+            scans("ga" + s, "m0" + s, "n0" + s, 1)
+            fin(fb, A("bt", *sl(b, t)), "m0" + s, "n0" + s, A("f0" + s))
+            scans("gb" + s, "mx" + s, "mn" + s, PARTS)
+            z = A("xw" + s, 0, NBT)
+            fin(b0, A("bt", *sl(b, t)), "mx" + s, "mn" + s, z)
+            dz = A(fb, NBT, 2 * NBT)
+            mm(dz, A("neg"), A("f0" + s), True, False)
+            mm(dz, I, z, False, True)
+        if not last:
+            for b in range(2):
+                xcopy(b, t + 1)
+        else:
+            start[0] -= 8
+        for h in range(1, 4):
+            for b in range(2):
+                s = str(b)
+                b0, b1 = "p%d" % (2 * b), "p%d" % (2 * b + 1)
+                z = A("xw" + s, NBT * (h - 1), NBT * h)
+                wl = A("wl" + s, 0, 6)
+                Y = A(b1, 0, NBT)
+                mm(Y, I, A("yc96"), True, False)
+                mm(Y, A("b16"), z, False, True)
+                R = A(b1, NBT, 2 * NBT)
+                mm(R, I, A("yc96"), True, False)
+                mm(R, A("b16"), z, False, False)
+                mm(R, I, A("cm"), False, True)
+                act(A("ri" + s), R, AF.Identity, A("mgc"))
+                tt(A("hot" + s), Y, A("ri" + s), OP.is_equal)
+                for tab, out in (("uw", "pw"), ("uq", "pq")):
+                    tt(A(out + s), A(tab, *sl(b, t)) if h == 1 else IND(A(tab), wl), A("hot" + s), OP.mult)
+                W = A(b0, 0, NBT)
+                mm(W, I, A("mask"), True, False)
+                mm(W, A("blkf"), A("pw" + s), False, True)
+                Q = A(b1, 0, NBT)
+                mm(Q, I, A("jc"), True, False)
+                mm(Q, A("b4096"), A("pq" + s), False, True)
+                act(A("aa" + s), Q, AF.Abs, A("bc", h - 1, h))
+                scan(A("ll" + s), RXL, W, OP.mult, OP.max)
+                vcp(wl, A("ll" + s, 15, NBT, 16))
+                tt(A("of" + s), IND(A("entt"), wl), A("aa" + s), OP.min)
+                vcp(A("ou" + s), A("of" + s))
+                tt(A("da%d%s" % (h, s)), IND(A("ct"), wl), A("aa" + s), OP.is_gt)
+                act(A("bw" + s), IND(A("bt"), wl), AF.Copy)
+                gather("gb" + s, A("xw" + s), "ou" + s)
+                if h == 3:
+                    act(A("xv" + s), IND(A("xw" + s, XO, XO + V), wl), AF.Copy)
+                scans("gb" + s, "mx" + s, "mn" + s, PARTS)
+                fin(b0, A("bw" + s), "mx" + s, "mn" + s,
+                    A("xw" + s, NBT * h, NBT * (h + 1)) if h < 3 else A("z3" + s))
+        for b in range(2):
+            s = str(b)
+            b0, b1, fb = "p%d" % (2 * b), "p%d" % (2 * b + 1), "p%d" % (6 + b)
+            d = A(b1, 0, NBT)
+            mm(d, A("neg"), A("xv" + s), True, False)
+            mm(d, I, A("z3" + s), False, True)
+            act(A("da" + s), d, AF.Abs)
+            D = A(b0, 0, NBT)
+            for h in range(1, 4):
+                mm(D, A("dead"), A("da%d%s" % (h, s)), h == 1, False)
+            mm(D, A("b1"), A("da" + s), False, True)
+            ts(A("st" + s), D, A("thc", t, t + 1), None, OP.is_le)
+            tt(A("sd" + s), A(fb, NBT, 2 * NBT), A("st" + s), OP.mult)
+            xn = A(b1, 0, NBT)
+            mm(xn, I, A("f0" + s), True, False)
+            mm(xn, I, A("sd" + s), False, True)
+        for b in range(2):
+            xn = A("p%d" % (2 * b + 1), 0, NBT)
+            if b == 0:
+                act(A("xw0", *sl(b, t, XO)), xn, AF.Copy)
+            else:
+                vcp(A("xw0", *sl(b, t, XO)), xn)
+        if not last:
+            vcp(A("gt%d" % t), IND(own0, A("sndu", 6 * t, 6 * t + 6)))
+            send(t, A("gt%d" % t), A("land%d" % t))
+        for b in range(2):
+            s = str(b)
+            b0, b1 = "p%d" % (2 * b), "p%d" % (2 * b + 1)
+            tt(A("hs" + s), A("st" + s), A("hit" + s), OP.mult)
+            E = A(b0, 0, NBT)
+            mm(E, A("idf"), A("entt", *sl(b, t)), True, False)
+            mm(E, A("i1152"), A("hs" + s), False, True)
+            if last:
+                act(A("yef", *sl(b, t)), E, AF.Identity, A("nzc"))
+                cols = slice(384 * b, 384 * b + 384)
+                xc = slice(XO + 384 * b, XO + 384 * b + 384)
+                add("y", lambda e, cols=cols: e.dma_start(out=T.ye[:, cols], in_=T.yef[:, cols]),
+                    [("yef", cols.start, cols.stop, 1)], [], (0.1, 0, False), 2.0, "o%d" % b, 16, True)
+                add("y", lambda e, cols=cols, xc=xc: e.dma_start(out=T.yx[:, cols], in_=T.xw0[:, xc]),
+                    [("xw0", xc.start, xc.stop, 1)], [], (0.1, 0, False), 2.0, "o%d" % (2 + b), 16, True)
+            else:
+                act(A("entt", *sl(b, t)), E, AF.Copy)
+                ts(A("ct", *sl(b, t)), A("entt", *sl(b, t)), 1440.0, 1024.0, OP.is_ge, OP.mult)
+                act(A("xw1", *sl(b, t, XO)), A("p%d" % (2 * b + 1), 0, NBT), AF.Copy)
+        if not last:
+            C = A("p0", 0, NBT)
+            mm(C, A("one"), A("hs0"), True, False)
+            mm(C, A("one"), A("hs1"), False, True)
+            rr, c0 = A("rr"), A("p0", 0, NBT)
+            add("v", lambda e, rr=rr, c0=c0: e.tensor_reduce(out=rr[0], in_=c0[0], axis=AX.X, op=OP.add),
+                regs(c0), regs(rr), vc(NBT))
+            vcp(A("rri"), A("rr"))
+            ts(A("rrj"), A("rri"), 31, None, OP.bitwise_and)
+            tt(A("thc", t + 1, t + 2), A("rrj"), A("tha", t + 1, t + 2), OP.add)
+            for b in range(2):
+                vcp(A("xw%d" % b, XG + NBT * t, XG + NBT * (t + 1)), A("land%d" % t))
+
+    _edges(ops)
+    if "order" not in PLAN:
+        PLAN["order"] = _plan(ops)
+    needed = [False] * len(ops)
+    for o in ops:
+        for j in o["pre"]:
+            needed[j] = needed[j] or o["pre"][j]
+    know = {}
+    count = {}
+    remotes = 0
+    for i in PLAN["order"]:
+        o = ops[i]
+        q = o["q"]
+        if q == "x":
+            count[o["sem"]] = o["amount"]
+            o["done"] = (o["sem"], o["amount"])
+            o["snap"] = {}
+            continue
+        kq = know.setdefault(q, {})
+        want = sorted((j for j in o["pre"] if o["pre"][j]), key=lambda j: -j)
+        for j in want:
+            sm, c = ops[j]["done"]
+            if kq.get(sm, 0) < c:
+                same = [j2 for j2 in want if ops[j2]["done"][0] == sm]
+                c = max(ops[j2]["done"][1] for j2 in same)
+                eng[q].wait_ge(T.sem[sm], c)
+                kq[sm] = c
+                for j2 in same:
+                    for a in ops[j2]["snap"]:
+                        kq[a] = max(kq.get(a, 0), ops[j2]["snap"][a])
+        ins = o["fn"](eng[q])
+        o["snap"] = dict(kq)
+        if o["remote"]:
+            remotes += 1
+            continue
+        if o["sem"] or needed[i]:
+            sm = o["sem"] or QS[q]
+            count[sm] = count.get(sm, 0) + o["amount"]
+            ins.then_inc(T.sem[sm], o["amount"])
+            o["done"] = (sm, count[sm])
+            if not o["sem"]:
+                o["snap"][sm] = count[sm]
+    for sm in sorted(count):
+        g.wait_ge(T.sem[sm], count[sm])
+    g.wait_ge(T.sem.loc, remotes * len(es))

@@ -1,12 +1,25 @@
+import math
 import numpy as np
 from concourse.mybir import AluOpType as OP, ActivationFunctionType as AF, AxisListType as AX
 
-V, NG, NBT, PARTS = 768, 384, 96, 2
-ZC = 288
-XO = ZC
-XG = ZC + V
-YO = XG + NG
-XE = ZC + 2304
+V, NG, NJ = 768, 384, 192
+NS = [96, 96]
+U0 = [sum(NS[:b]) for b in range(len(NS))]
+NB = len(NS)
+JUDGE_GATHER = ["sv", "ss", "ss"]
+FORM = ["xp", "dd", "pp"]
+ON_VECTOR = [[m for m in range(2) if f[m] == "x"] for f in FORM]
+REGATHER = ["ss", "ss", "ss"]
+HOP_GATHER = ["sss", "sss", "ss"]
+HOT = "sss"
+BANKS = [("p0", "p1", "p2"), ("p3", "p4", "p5")]
+XBANKS = [("p2", "p7"), ("p5", "p4"), ()]
+DBANKS = [("p1", "p6"), (), ()]
+KEEP = "p6"
+ZO, XO = 1152, 1664
+XG = XO + V
+XE = XG + NG
+GAP = XO - ZO
 MAGIC = 12582912.0
 BF2 = "bfloat16"
 SCRATCH = {}
@@ -14,7 +27,7 @@ WHERE = {}
 
 
 def _buf(name, cols, dtype=BF2, where="sbuf", rows=128, pool=True):
-    if not pool or where != "sbuf" or rows != 128 or cols > 144:
+    if not pool or where != "sbuf" or rows != 128 or cols > 288:
         SCRATCH[name] = (where, [rows, cols], dtype)
         WHERE[name] = (name, 0, cols, dtype)
         return
@@ -24,55 +37,69 @@ def _buf(name, cols, dtype=BF2, where="sbuf", rows=128, pool=True):
     WHERE[name] = (p, lo, cols, dtype)
 
 
-for _b in range(2):
+for _b, _w in enumerate(NS):
     _buf("xw%d" % _b, XE)
     for _n in ("ga", "gb", "mt", "mx", "mn", "m0", "n0"):
-        _buf("%s%d" % (_n, _b), 16 * NBT)
-    for _n in ("f0", "hit", "pq", "bw", "xv", "z3", "da", "st", "sd", "hs", "da1", "da2", "da3"):
-        _buf("%s%d" % (_n, _b), NBT)
-    _buf("pw%d" % _b, NBT, "float16")
-    for _n in ("hot", "aa", "ll", "of", "kt", "r1", "mb", "mbt"):
-        _buf("%s%d" % (_n, _b), NBT, "float32")
-    _buf("rm%d" % _b, 112, "float32")
-    _buf("ri%d" % _b, NBT)
-    _buf("ou%d" % _b, NBT, "uint16")
-    _buf("eu%d" % _b, NBT, "uint16")
+        _buf("%s%d" % (_n, _b), 16 * _w)
+    for _n in ("hot", "pq", "bw", "xv", "z3", "mz"):
+        _buf("%s%d" % (_n, _b), _w)
+    _buf("pw%d" % _b, _w, "float16")
+    _buf("cl%d" % _b, 3 * _w, "float16")
+    for _n in ("ca", "cb"):
+        _buf("%s%d" % (_n, _b), _w, "float16")
+    for _n in ("aa", "ll", "of"):
+        _buf("%s%d" % (_n, _b), _w, "float32")
+    _buf("r1%d" % _b, 144, "float32")
+    _buf("mb%d" % _b, 128, "float32")
+    _buf("ht%d" % _b, 128)
+    _buf("bc%d" % _b, 4, "float32")
+    _buf("bi%d" % _b, 4, "int32")
+    _buf("ou%d" % _b, 4 * _w, "uint16")
     _buf("wl%d" % _b, 8, "uint16")
+for _n in range(5):
+    _buf("eu%d" % _n, NJ, "uint16")
+    _buf("ct%d" % _n, NJ)
+    _buf("eh%d" % _n, NJ, "float16")
+for _n in range(2):
+    _buf("xr%d" % _n, 8 * NJ)
+for _n in ("f0", "st", "sd", "hs"):
+    _buf(_n, NJ)
 for _n in ("enti", "usri", "uw", "uq"):
     _buf(_n, V, "int32")
-_buf("entt", V, "float32")
-_buf("yef", V, "float32")
-_buf("ct", V)
+for _n in ("entt", "yef", "e1", "e2"):
+    _buf(_n, V, "float32")
 _buf("bt", V)
 _buf("sndi", 24, "int32", "sbuf", 128, False)
 _buf("sndu", 24, "uint16")
+_buf("sndl", 24, "uint16")
 _buf("thi", 5, "int32", "sbuf", 8)
 _buf("thf", 5, "float32", "sbuf", 8)
-for _n, _w in (("tha", 5), ("thc", 5), ("rr", 1), ("pf", 4), ("bc", 4), ("py", 1), ("mgc", 1), ("nzc", 1),
-               ("rg", NBT), ("idf", 128)):
+for _n, _w in (("tha", 5), ("thc", 5), ("rr", 1), ("pf", 4), ("bk", 4), ("py", 1), ("p1c", 1), ("mgc", 1), ("nxo", 1), ("pg", 1),
+               ("top", 128), ("idf", 128)):
     _buf(_n, _w, "float32")
-for _n, _w in (("rri", 1), ("rrj", 1), ("ji", NBT), ("jj", NBT), ("pi", 4), ("pj", 4), ("bi", 4)):
+for _n, _w in (("rri", 1), ("rrj", 1), ("ji", 96), ("jj", 96), ("pi", 4), ("pj", 4), ("pk", 1)):
     _buf(_n, _w, "int32")
 _buf("gs0", NG)
+_buf("f0g", 96)
 for _n in range(4):
-    _buf("gt%d" % _n, NBT, BF2, "sbuf", 128, False)
-    _buf("land%d" % _n, NBT, BF2, "sbuf", 128, False)
-for _n in ("one", "idn", "half", "neg", "i256", "i1152", "b16", "b1", "b4096", "dead"):
+    _buf("gt%d" % _n, 96, BF2, "sbuf", 128, False)
+    _buf("land%d" % _n, 96, BF2, "sbuf", 128, False)
+for _n in ("one", "idn", "half", "neg", "ict", "ik", "ig", "ixo", "i1152", "blkh", "blk", "b16", "nb16", "nb1", "b2", "b8k",
+           "w16", "wn16", "w32", "wx0", "wx1"):
     _buf(_n, 128)
-for _n in ("one144", "blkh", "blk", "wsel", "w32", "w16", "wn16"):
-    _buf(_n, 144)
-_buf("blkf", 128, "float16")
+for _n in ("idh", "blkf", "i8k", "f8k", "nf8k"):
+    _buf(_n, 128, "float16")
 for _n in ("oe", "ee0", "ee"):
     _buf(_n, 128, "float32", "sbuf", 8)
-for _n in ("kc", "yc96", "jc", "mask", "cm", "cq"):
-    _buf(_n, NBT)
-_buf("ab1", 16 * NBT)
-_buf("rx", 16 * NBT)
-_buf("rn", 16 * NBT)
+for _n in ("yc96", "jc", "mask", "cm", "cq", "cm2"):
+    _buf(_n, 96)
+_buf("rx", 16 * max(NS))
+_buf("rn", 16 * max(NS))
 for _n in range(8):
     _buf("p%d" % _n, 512, "float32", "psum")
 LOADS = ["snd", "xa", "ent", "yc", "bn", "usr", "th"]
-SEMAPHORES = ["sv", "ss", "st", "sg", "loc", "o0", "o1", "o2", "o3"] + ["ld_" + n for n in LOADS] + ["arr%d" % t for t in range(5)]
+SEMAPHORES = (["sv", "ss", "st", "sg", "loc"] + ["o%d" % n for n in range(2 * NB)] + ["ld_" + n for n in LOADS]
+              + ["ld_y%d" % b for b in range(NB)] + ["ld_x%d" % b for b in range(NB)] + ["arr%d" % t for t in range(5)])
 QS = {"v": "sv", "s": "ss", "t": "st", "g": "sg"}
 PLAN = {}
 
@@ -115,7 +142,7 @@ def _cost(o, m):
     return f * m[0] + max(64, n * (m[2] if gath else 1)) * 1.0e-3 * m[1] if n else f
 
 
-def _schedule(ops, succ, m, slack, noise):
+def _schedule(ops, succ, m, slack=0.12):
     n = len(ops)
     cost = [_cost(o, m) for o in ops]
     pri = [0.0] * n
@@ -124,7 +151,6 @@ def _schedule(ops, succ, m, slack, noise):
         for j in succ[i]:
             x = max(x, pri[j] + (m[3] if ops[j]["pre"][i] else 0.0))
         pri[i] = x + cost[i] + ops[i]["lag"] * m[4]
-    pri = [pri[i] + float(noise[i]) for i in range(n)]
     left = [len(o["pre"]) for o in ops]
     rdy = [0.0] * n
     cand = {}
@@ -172,8 +198,8 @@ def _length(ops, order, m):
     return top
 
 
-MODELS = [(1.0, 1.04, 1.56, 0.06, 1.0), (0.4, 0.9, 1.2, 0.06, 1.0), (0.5, 1.2, 2.0, 0.1, 1.3), (1.0, 0.9, 1.3, 0.2, 1.3)]
-STEPS = 1600
+MODELS = [(1.0, 0.9, 1.56, 0.1, 1.0), (1.0, 0.83, 1.2, 0.06, 1.0), (1.3, 1.2, 2.0, 0.1, 1.3), (1.0, 0.9, 1.3, 0.2, 1.3)]
+STEPS = 1200
 
 
 def _plan(ops):
@@ -212,24 +238,138 @@ def _plan(ops):
     return best[2]
 
 
+MODELS = [(1.0, 0.87, 1.56, 0.1, 1.0), (1.2, 1.15, 1.8, 0.15, 1.2)]
+STEPS = 6000
+
+
+def _plan(ops):
+    n = len(ops)
+    names = sorted(set(o["q"] for o in ops))
+    queue = [names.index(o["q"]) for o in ops]
+    key = [o["key"] for o in ops]
+    wait = [[j for j in o["pre"] if o["pre"][j]] for o in ops]
+    costs = [[_cost(o, m) for o in ops] for m in MODELS]
+    lags = [[o["lag"] * m[4] + m[3] for o in ops] for m in MODELS]
+    succ = [[] for _ in ops]
+    for i, o in enumerate(ops):
+        for j in o["pre"]:
+            succ[j].append((i, o["pre"][j]))
+    path = [0.0] * n
+    for i in range(n - 1, -1, -1):
+        path[i] = costs[0][i] + max([path[j] + (lags[0][i] if w else 0.0) for j, w in succ[i]] + [lags[0][i]])
+    count = [len(o["pre"]) for o in ops]
+
+    def schedule(bonus, patience):
+        cost, lag = costs[0], lags[0]
+        pri = [path[i] + bonus[key[i]] for i in range(n)]
+        left, rdy = list(count), [0.0] * n
+        cand = [[] for _ in names]
+        for i in range(n):
+            if not left[i]:
+                cand[queue[i]].append(i)
+        free, soon = [0.0] * len(names), [0.0 if c else 1e9 for c in cand]
+        order, top = [], 0.0
+        for _i in range(n):
+            s0 = min(soon)
+            q = soon.index(s0)
+            c = cand[q]
+            pick, p = -1, -1e9
+            for i in c:
+                if pri[i] > p and rdy[i] <= s0 + patience[key[i]]:
+                    pick, p = i, pri[i]
+            c.remove(pick)
+            order.append(pick)
+            st = rdy[pick] if rdy[pick] > s0 else s0
+            end = free[q] = st + cost[pick]
+            done = end + lag[pick]
+            if done > top:
+                top = done
+            soon[q] = max(end, min([rdy[i] for i in c])) if c else 1e9
+            for j, w in succ[pick]:
+                e = done if w else st
+                if e > rdy[j]:
+                    rdy[j] = e
+                left[j] -= 1
+                if not left[j]:
+                    r = queue[j]
+                    cand[r].append(j)
+                    e = max(free[r], rdy[j])
+                    if e < soon[r]:
+                        soon[r] = e
+        return order, top
+
+    def length(order, m):
+        cost, lag = costs[m], lags[m]
+        free, fin = [0.0] * len(names), [0.0] * n
+        for i in order:
+            t = free[queue[i]]
+            for j in wait[i]:
+                if fin[j] > t:
+                    t = fin[j]
+            t += cost[i]
+            free[queue[i]] = t
+            fin[i] = t + lag[i]
+        return max(fin)
+
+    keys = 1 + max(key)
+    batch = [0] * keys
+    for o in ops:
+        batch[o["key"]] = o["batch"]
+    rng = np.random.RandomState(5)
+    cur = best = None
+    for step in range(STEPS):
+        if step < 4:
+            c = ([-(0.5 + 0.25 * step) * b for b in batch], [0.1] * keys)
+        else:
+            c = (list(cur[1][0]), list(cur[1][1]))
+            for _i in range((1, 1, 2, 4)[rng.randint(4)]):
+                a = key[rng.randint(n)]
+                if rng.rand() < 0.3:
+                    c[1][a] = 0.1 * rng.randint(7)
+                else:
+                    x = (0.3, 1.0, 3.0)[rng.randint(3)] * rng.randn()
+                    for k in range(a, min(keys, a + (1, 1, 3, 8, 20)[rng.randint(5)])):
+                        c[0][k] += x
+        order, top = schedule(*c)
+        bar = 1e9 if step < 4 else cur[0] - 0.001 * (1 - step / STEPS) * math.log(rng.rand())
+        if step == 0:
+            unit = [top] + [length(order, m) for m in range(1, len(MODELS))]
+        if cur and top / unit[0] > bar - cur[0] + cur[2] + 0.004:
+            continue
+        x = top / unit[0] + sum(length(order, m) / unit[m] for m in range(1, len(MODELS)))
+        if cur is None or x <= (cur[0] if step < 4 else bar):
+            cur = (x, c, top / unit[0])
+            if best is None or x < best[0]:
+                best = (x, order)
+    return best[1]
+
+
 def rank_program(g, core, T, topo):
     rank = T.rank_of(core)
     if rank is None:
         return
     ops = []
-    start = []
+    names = {}
+    step = [None, 0]
+    now = [0]
     eng = {"v": g.vector, "s": g.scalar, "t": g.tensor, "g": g, "y": g.sync}
 
+    def label(*x):
+        step[:] = [x or None, 0]
+
     def add(q, fn, rd, wr, cost, lag=0.0, sem=None, amount=1, dma=False, after=()):
-        ops.append({"q": q, "fn": fn, "key": len(ops) - start[0] if start else -1, "rd": rd, "wr": wr, "cost": cost, "lag": lag, "sem": sem, "amount": amount,
+        key = names.setdefault((step[0], step[1]), len(names))
+        step[1] += 1
+        ops.append({"q": q, "fn": fn, "key": key, "batch": step[0][-1] if step[0] and len(step[0]) > 1 else 0, "rd": rd, "wr": wr, "cost": cost, "lag": lag, "sem": sem, "amount": amount,
                     "dma": dma, "after": list(after), "remote": False})
         return len(ops) - 1
 
-    def A(name, lo=0, hi=None, step=1):
+    def A(name, lo=0, hi=None, step=1, rows=None):
         buf, o, cols, _d = WHERE[name]
         if hi is None:
             hi = cols
-        ap = T[buf][:, o + lo:o + hi] if step == 1 else T[buf][:, o + lo:o + hi:step]
+        c = slice(o + lo, o + hi) if step == 1 else slice(o + lo, o + hi, step)
+        ap = T[buf][:, c] if rows is None else T[buf][0:rows, c]
         return (ap, [(name, lo, hi, step)], (hi - lo + step - 1) // step, False)
 
     def IND(w, off):
@@ -273,37 +413,41 @@ def rank_program(g, core, T, topo):
         return add("v", lambda e: e.tensor_tensor_scan(out=out[0], data0=d0[0], data1=d1[0], initial=0.0, op0=op0, op1=op1),
                    regs(d0, d1), regs(out), vc(out[2] * half(out, d0, d1)))
 
-    def vtr(out, a):
-        return add("v", lambda e: e.transpose(out=out[0], in_=a[0]), regs(a), regs(out), vc(out[2]))
-
     def fill(out, x):
         return add("v", lambda e: e.memset(out[0], x), [], regs(out), vc(out[2] * half(out)))
 
-    def act(out, a, func, bias=None):
+    def act(out, a, func, bias=None, scale=1.0):
         if bias is None:
             fn = lambda e: e.activation(out=out[0], in_=a[0], func=func)
         else:
-            fn = lambda e: e.activation(out=out[0], in_=a[0], func=func, bias=val(bias))
+            fn = lambda e: e.activation(out=out[0], in_=a[0], func=func, bias=val(bias), scale=scale)
         return add("s", fn, regs(a, bias), regs(out), (0.065, out[2], a[3]))
+
+    def copy(q, out, a):
+        return vcp(out, a) if q == "v" else act(out, a, AF.Copy)
 
     def mm(out, l, r, start, stop):
         return add("t", lambda e: e.matmul(out[0], l[0], r[0], start, stop), regs(l, r), regs(out),
                    (0.03, max(64, r[2]) * (4 if kind(r) == "float32" else 1), False))
 
+    def mms(out, pairs, start=True, stop=True):
+        for i, (l, r) in enumerate(pairs):
+            mm(out, l, r, start and i == 0, stop and i == len(pairs) - 1)
+
     def sel(out, a, pattern, op, base, cm):
         return add("g", lambda e: e.affine_select(out=out[0], in_=a[0], pattern=pattern, compare_op=op, fill=0.0, base=base,
-                                                 channel_multiplier=cm), regs(a), regs(out), (0.2, 2 * out[2], False))
+                                                 channel_multiplier=cm), regs(a), regs(out), (0.17, 2 * out[2], False))
 
     def iota(out, pattern, base, cm):
         if kind(out) != "int32":
             fn = lambda e: e.iota(out[0], pattern=pattern, base=base, channel_multiplier=cm, allow_small_or_imprecise_dtypes=True)
         else:
             fn = lambda e: e.iota(out[0], pattern=pattern, base=base, channel_multiplier=cm)
-        return add("g", fn, [], regs(out), (0.15, 2 * out[2], False))
+        return add("g", fn, [], regs(out), (0.13, 2 * out[2], False))
 
-    def load(q, name, out):
+    def load(q, name, out, sem=None):
         return add(q, lambda e: e.dma_start(out=out[0], in_=T[name][:, :]), [], regs(out), (0.1, 0, False), 2.2,
-                   "ld_" + name, 16, True)
+                   sem or "ld_" + name, 16, True)
 
     dst = T.cores[(rank - 1) % len(T.cores)]
     src = T.cores[(rank + 1) % len(T.cores)]
@@ -318,245 +462,268 @@ def rank_program(g, core, T, topo):
         ops[j]["remote"] = True
         add("x", None, [], regs(land), (0.0, 0, False), 2.5, "arr%d" % slot, n_in, True, (j,))
 
-    own0 = A("xw0", XO, XO + V)
+    def cls(t, b=None, base=0):
+        lo, n = (0, NJ) if b is None else (U0[b], NS[b])
+        return base + 4 * lo + t % 4, base + 4 * (lo + n), 4
+
+    def part(name, b, times=1):
+        return A(name, times * U0[b], times * (U0[b] + NS[b]))
+
+    own0 = A("xw0", XO, XG)
     load("y", "snd", A("sndi"))
     load("s", "xa", own0)
     load("y", "ent", A("enti"))
-    load("y", "yc", A("xw0", YO, XE))
-    load("s", "bn", A("bt"))
-    load("y", "usr", A("usri"))
-    load("s", "th", A("thi"))
+    load("s", "yc", A("xw0", 0, ZO))
+    load("y", "bn", A("bt"))
+    load("s", "usr", A("usri"))
+    load("y", "th", A("thi"))
+    for b in range(1, NB):
+        load("y", "xa", A("xw%d" % b, XO, XG), "ld_x%d" % b)
+        load("s", "yc", A("xw%d" % b, 0, ZO), "ld_y%d" % b)
     for c in range(4):
         ts(A("sndu", 6 * c, 6 * c + 6), A("sndi", 6 * c, 6 * c + 6), 4, c, OP.mult, OP.add)
     act(A("gs0"), IND(own0, A("sndu")), AF.Copy)
-    send(4, A("gs0"), A("xw0", XG, XG + NG))
+    send(4, A("gs0"), A("xw0", XG, XE))
+    vcp(A("sndl"), A("sndi"))
 
     fill(A("one"), 1.0)
-    fill(A("one144"), 1.0)
     fill(A("oe"), 1.0)
     sel(A("idn"), A("one"), [[-1, 128]], OP.is_equal, 0, 1)
-    sel(A("blkh"), A("one144"), [[-16, 9], [0, 16]], OP.is_ge, 0, 1)
-    sel(A("blk"), A("blkh"), [[16, 9], [0, 16]], OP.is_ge, 15, -1)
-    sel(A("wsel"), A("blk"), [[0, 9], [1, 16]], OP.is_equal, -15, 0)
+    sel(A("blkh"), A("one"), [[-16, 8], [0, 16]], OP.is_ge, 0, 1)
+    sel(A("blk"), A("blkh"), [[16, 8], [0, 16]], OP.is_ge, 15, -1)
     sel(A("ee0"), A("oe"), [[1, 128]], OP.is_ge, 0, -16)
     sel(A("ee"), A("ee0"), [[-1, 128]], OP.is_ge, 15, 16)
-    iota(A("ji"), [[1, NBT]], 128, -1)
-    iota(A("jc"), [[1, NBT]], 0, 0)
+    iota(A("ji"), [[1, 96]], 128, -1)
+    iota(A("jc"), [[1, 96]], 0, 0)
     iota(A("pi"), [[0, 4]], 0, 1)
-    iota(A("bi"), [[NBT, 4]], 0, 0)
-    for name, of, x in (("half", "idn", 0.5), ("neg", "idn", -1.0), ("i256", "idn", 256.0), ("i1152", "idn", 1152.0),
-                        ("idf", "idn", 1.0), ("w32", "wsel", 32.0), ("w16", "wsel", 16.0),
-                        ("wn16", "wsel", -16.0)):
-        ts(A(name), A(of), x, None, OP.mult)
-    for name, x in (("b16", 0.0625), ("b1", 1.0), ("b4096", 4096.0), ("dead", -8192.0), ("blkf", 1.0)):
-        ts(A(name), A("blk", 0, 128), x, None, OP.mult)
+    fill(A("top"), 0.0)
+    ts(A("top", 0, 128, 16), A("jc", 0, 8), 131072.0, 65535.0, OP.mult, OP.add)
     ts(A("pj"), A("pi"), 15, None, OP.bitwise_and)
     vcp(A("pf"), A("pj"))
-    ts(A("py"), A("pf", 0, 1), -0.0625, None, OP.mult)
-    ts(A("bc"), A("pf"), -4096.0, None, OP.mult)
-    tt(A("bc"), A("bc"), A("bi"), OP.add)
+    ts(A("pk"), A("pi", 0, 1), 112, None, OP.bitwise_and)
+    ts(A("pg"), A("pk"), 8192.0, None, OP.mult)
+    for name, of, x in (("half", "idn", 0.5), ("neg", "idn", -1.0), ("ict", "idn", 65536.0), ("i1152", "idn", 1152.0),
+                        ("ixo", "idn", -float(XO)), ("idf", "idn", 1.0), ("idh", "idn", 1.0), ("i8k", "idn", 8192.0), ("ik", "idn", A("pf", 0, 1)),
+                        ("ig", "idn", A("pg")), ("b16", "blk", 0.0625), ("nb16", "blk", -0.0625), ("nb1", "blk", -1.0),
+                        ("b2", "blk", 2.0), ("b8k", "blk", 8192.0), ("blkf", "blk", 1.0), ("f8k", "blk", 8192.0),
+                        ("nf8k", "blk", -8192.0), ("w16", "blk", 16.0), ("wn16", "blk", -16.0), ("w32", "blk", 32.0)):
+        ts(A(name), A(of), x, None, OP.mult)
+    for m in sorted(set(m for b in range(NB) for m in ON_VECTOR[b])):
+        vcp(A("wx%d" % m), A("wn16"))
+        fill(A("wx%d" % m, 1 - m, 128, 2), 0.0)
+    ts(A("py"), A("pf", 0, 1), -0.0625, -15.0 / 32, OP.mult, OP.add)
+    if HOT[0] == "s":
+        ts(A("p1c"), A("pf", 0, 1), 1.0, None, OP.add)
+    else:
+        ts(A("p1c"), A("pf", 0, 1), -0.0625, None, OP.mult)
+    ts(A("bk"), A("pf"), -8192.0, None, OP.mult)
+    for b, n in enumerate(NS):
+        iota(A("bi%d" % b), [[n, 4]], ZO, 0)
+        tt(A("bc%d" % b), A("bk"), A("bi%d" % b), OP.add)
+        c0 = (48 * (ZO - 1) + 3 * n + 3) % GAP
+        ts(A("ca%d" % b), A("jc", 0, n), 3.0, c0 - (GAP - 1) / 2, OP.mult, OP.add)
+        ts(A("cb%d" % b), A("jc", 0, n), -3.0, -float(c0), OP.mult, OP.add)
+        fill(A("r1%d" % b, 128, 144), 1048576.0)
     ts(A("jj"), A("ji"), 15, None, OP.bitwise_and)
     ts(A("mask"), A("jj"), 0, -4096.0, OP.not_equal, OP.mult)
-    ts(A("kc"), A("one", 0, NBT), A("pf", 0, 1), None, OP.mult)
-    ts(A("yc96"), A("one", 0, NBT), A("py"), None, OP.mult)
-    for name, x, y in (("cm", MAGIC, None), ("cq", -0.25, None), ("rx", 1.0, 0.0), ("rn", 0.0, 512.0), ("rg", 0.0, 1048576.0),
-                       ("rm0", 0.0, None), ("rm1", 0.0, None), ("mgc", -MAGIC, None), ("nzc", -float(ZC), None)):
+    ts(A("yc96"), A("one", 0, 96), A("py"), None, OP.mult)
+    for name, x, y in (("cm", MAGIC, None), ("cm2", MAGIC * 8192 * GAP, None), ("cq", -0.25, None), ("rx", 1.0, 0.0),
+                       ("rn", 0.0, 512.0), ("mgc", -MAGIC, None), ("nxo", -float(XO), None)):
         fill(A(name), x)
         if y is not None:
             fill(A(name, 0, WHERE[name][2], 16), y)
-    ts(A("entt"), A("enti"), float(ZC), None, OP.add)
-    ts(A("ct"), A("enti"), 1152.0, 1024.0, OP.is_ge, OP.mult)
+    I, NEG = A("idn"), A("neg")
+
+    def lists(t):
+        vcp(A("eu%d" % t), A("entt", *cls(t)))
+        ts(A("ct%d" % t), A("eu%d" % t), float(ZO), None, OP.is_lt)
+        ts(A("eh%d" % t), A("eu%d" % t), -1024.0, None, OP.add)
+
+    def repeat(t):
+        for r in range(8):
+            sel(A("xr%d" % (t % 2), r, 8 * NJ, 8), A("xw0", *cls(t, None, XO)), [[0, NJ]], OP.is_ge, 0, 0)
+
+    for c in range(4):
+        ts(A("e1", *cls(c)), A("enti", *cls(c)), float(ZO), -float(XE), OP.is_ge, OP.mult)
+        ts(A("e2", *cls(c)), A("enti", *cls(c)), float(XO), None, OP.add)
+        tt(A("entt", *cls(c)), A("e1", *cls(c)), A("e2", *cls(c)), OP.add)
+        act(A("yef", *cls(c)), A("e2", *cls(c)), AF.Identity, A("nxo"))
+        lists(c)
     ts(A("uw"), A("usri"), 4, None, OP.logical_shift_right)
     ts(A("uq"), A("usri"), 15, None, OP.bitwise_and)
     vcp(A("thf"), A("thi"))
     mm(A("p0", 0, 5), A("ee"), A("thf"), True, True)
     vcp(A("tha"), A("p0", 0, 5))
     vcp(A("thc", 0, 1), A("tha", 0, 1))
-    act(A("xw1", XO, XO + V), own0, AF.Copy)
-    act(A("xw1", YO, XE), A("xw0", YO, XE), AF.Copy)
-    act(A("xw1", XG, XG + NG), A("xw0", XG, XG + NG), AF.Copy)
+    for b in range(1, NB):
+        act(A("xw%d" % b, XG, XE), A("xw0", XG, XE), AF.Copy)
+    repeat(0)
 
-    I = A("idn")
-    RXL = A("rx", 0, NBT)
-
-    def sl(b, t, base=0):
-        return base + 384 * b + t % 4, base + 384 * (b + 1), 4
-
-    def xcopy(b, t):
-        for m in range(4):
-            mm(A("p%d" % (4 + b), m, 384, 4), I, A("xw%d" % b, *sl(b, t, XO)), True, True)
-
-    def scans(G, X, N, parts):
-        w = 16 * NBT // parts
+    def scans(G, X, N, n, parts):
+        w = 16 * n // parts
         for m in range(parts):
             lo, hi = w * m, w * m + w
             scan(A(X, lo, hi), A("rx", lo, hi), A(G, lo, hi), OP.mult, OP.max)
             scan(A(N, lo, hi), A("rn", lo, hi), A(G, lo, hi), OP.add, OP.min)
 
-    def gather(out, win, off, vec=()):
-        w = NBT // PARTS
-        for m in range(PARTS):
-            o, i = A(out, 16 * w * m, 16 * w * m + 16 * w), IND(win, A(off, w * m, w * m + w))
-            if m in vec:
-                vcp(o, i)
-            else:
-                act(o, i, AF.Copy)
+    def gather(out, win, off, lo, n, queues):
+        w = n // len(queues)
+        for m, q in enumerate(queues):
+            copy(q, A(out, 16 * w * m, 16 * w * m + 16 * w), IND(win, A(off, lo + w * m, lo + w * m + w)))
 
     def fin(bank, bv, X, N, out):
-        p = A(bank, 0, NBT)
-        mm(p, I, A("cq"), True, False)
-        mm(p, A("neg"), bv, False, False)
-        mm(p, A("half"), A(X, 15, 16 * NBT, 16), False, False)
-        mm(p, A("half"), A(N, 15, 16 * NBT, 16), False, False)
-        mm(p, I, A("cm"), False, True)
+        n = out[2]
+        p = A(bank, 0, n)
+        mms(p, [(I, A("cq", 0, n)), (NEG, bv), (A("half"), A(X, 15, 16 * n, 16)), (A("half"), A(N, 15, 16 * n, 16)),
+                (I, A("cm", 0, n))])
         act(out, p, AF.Abs, A("mgc"))
 
-    for b in range(2):
-        xcopy(b, 0)
     for t in range(5):
         last = t == 4
-        start[:] = [len(ops)]
-        for b in range(2):
+        now[0] = t
+        for b, n in enumerate(NS):
+            label("gather", b)
+            gather("ga%d" % b, A("xw%d" % b), "eu%d" % t, U0[b], n, JUDGE_GATHER[b])
+        for b, n in enumerate(NS):
+            label("score", b)
             s = str(b)
-            vcp(A("eu" + s), A("entt", *sl(b, t)))
-            gather("ga" + s, A("xw" + s), "eu" + s, (1,) if b == 0 else ())
-        if last:
-            act(A("yef"), A("entt"), AF.Identity, A("nzc"))
-            start[0] += 1
-        for b in range(2):
-            s = str(b)
-            b0, b1 = "p%d" % (2 * b), "p%d" % (2 * b + 1)
-            xb, fb = "p%d" % (4 + b), "p%d" % (6 + b)
-            K = A(b0, 0, NBT)
-            mm(K, A("i256"), A("ct", *sl(b, t)), True, False)
-            mm(K, I, A("kc"), False, False)
-            for k in range(4):
-                tt(A("mt" + s, 384 * k, 384 * k + 384), A(xb, 0, 384), A("ga" + s, k, 1536, 4), OP.subtract if b else OP.max)
-            if b:
-                for lo in range(0, 16 * NBT, 4 * NBT):
-                    act(A("ab1", lo, lo + 4 * NBT), A("mt1", lo, lo + 4 * NBT), AF.Abs)
-            else:
-                for k in range(16):
-                    mm(K, A("wn16", 15 - k, 143 - k), A("ga0", k, 1536, 16), False, False)
-            for k in sorted(range(16), key=lambda k: k % 4):
-                lo = 384 * (k % 4)
-                mm(K, A("w16" if b else "w32", 15 - k, 143 - k), A("ab1" if b else "mt0", lo + k // 4, lo + 384, 4), False, k == 15)
-            vtr(A("kt" + s), K)
-            scan(A("r1" + s), A("rg"), A("kt" + s), OP.add, OP.min)
-            ts(A("rm" + s, 15, NBT, 16), A("r1" + s, 15, NBT, 16), 262143.0, None, OP.min)
-            scan(A("mb" + s), RXL, A("rm" + s, 15, 15 + NBT), OP.mult, OP.add)
-            vtr(A("mbt" + s), A("mb" + s))
-            tt(A("hit" + s), K, A("mbt" + s), OP.is_equal)
-            E = A(b1, 0, NBT)
-            mm(E, A("idf"), A("entt", *sl(b, t)), True, False)
-            mm(E, A("i1152"), A("hit" + s), False, True)
-            vcp(A("ou" + s), E)
-            gather("gb" + s, A("xw" + s), "ou" + s)
-            scans("ga" + s, "m0" + s, "n0" + s, 1)
-            fin(fb, A("bt", *sl(b, t)), "m0" + s, "n0" + s, A("f0" + s))
-            scans("gb" + s, "mx" + s, "mn" + s, PARTS)
-            z = A("xw" + s, 0, NBT)
-            fin(b0, A("bt", *sl(b, t)), "mx" + s, "mn" + s, z)
-            dz = A(fb, NBT, 2 * NBT)
-            mm(dz, A("neg"), A("f0" + s), True, False)
-            mm(dz, I, z, False, True)
+            b0, b1, b2 = BANKS[b]
+            K = A(b0, 0, 128, 1, n)
+            mms(K, [(part("ct%d" % t, b), A("ict")), (A("one", 0, n), A("ik")), (A("one", 0, n), A("ig"))]
+                + [(A("xw" + s, *cls(t, b, XO)), A("wx%d" % m)) for m in ON_VECTOR[b]], True, False)
+            parts = len(JUDGE_GATHER[b])
+            w = 8 * n // parts
+            turn = 0
+            for p in range(parts):
+                xr = A("xr%d" % (t % 2), 8 * U0[b] + w * p, 8 * U0[b] + w * p + w)
+                if XBANKS[b]:
+                    xp = A(XBANKS[b][p], 0, w)
+                    mm(xp, I, xr, True, True)
+                for m in range(2):
+                    gm = A("ga" + s, 2 * w * p + m, 2 * w * p + 2 * w, 2)
+                    lo = 8 * n * m + w * p
+                    out = A("mt" + s, lo, lo + w)
+                    if FORM[b][m] == "x":
+                        tt(out, xp, gm, OP.max)
+                    elif FORM[b][m] == "d":
+                        tt(A("gb" + s, lo, lo + w), xp, gm, OP.subtract)
+                        act(out, A("gb" + s, lo, lo + w), AF.Abs)
+                    else:
+                        d = A(DBANKS[b][turn % len(DBANKS[b])], 0, w)
+                        turn += 1
+                        mms(d, [(NEG, xr), (I, gm)])
+                        act(out, d, AF.Abs)
+            for m in ON_VECTOR[b]:
+                for k in range(m, 16, 2):
+                    mm(A(b0, k, 128, 16, n), A("ga" + s, k, 16 * n, 16), A("wn16", 0, 128, 16), False, False)
+            for m in range(2):
+                for e in range(8):
+                    mm(A(b0, 2 * e + m, 128, 16, n), A("mt" + s, 8 * n * m + e, 8 * n * m + 8 * n, 8),
+                       A("w32" if m in ON_VECTOR[b] else "w16", 0, 128, 16), False, (m, e) == (1, 7))
+            label("least", b)
+            top = A("top", 0, 128, 1, n)
+            E = A(b1, 0, n)
+            mm(E, A("idh"), part("eh%d" % t, b), True, False)
+            scan(A("r1" + s, 0, 128, 1, n), top, K, OP.max, OP.min)
+            scan(A("mb" + s, 0, 128, 1, n), top, A("r1" + s, 15, 143, 1, n), OP.max, OP.min)
+            ht = A("ht" + s, 0, 128, 1, n)
+            tt(ht, K, A("mb" + s, 0, 128, 1, n), OP.is_equal)
+            mm(E, ht, A("ixo", 0, n, 1, n), False, True)
+            mm(part(KEEP, b), ht, A("idn", 0, n, 1, n), True, True)
+            ts(A("ou" + s, 0, n), E, 1024.0, None, OP.add)
+            gather("gb" + s, A("xw" + s), "ou" + s, 0, n, REGATHER[b])
+            scans("ga" + s, "m0" + s, "n0" + s, n, 3)
+            fin(b2, A("bt", *cls(t, b)), "m0" + s, "n0" + s, part("f0", b))
+            scans("gb" + s, "mx" + s, "mn" + s, n, len(REGATHER[b]))
+            z = A("xw" + s, ZO, ZO + n)
+            fin(b0, A("bt", *cls(t, b)), "mx" + s, "mn" + s, z)
+            mms(A(KEEP, NJ + U0[b], NJ + U0[b] + n), [(NEG, part("f0", b)), (I, z)])
         if not last:
-            for b in range(2):
-                xcopy(b, t + 1)
-        else:
-            start[0] -= 8
+            label("ahead")
+            repeat(t + 1)
+            act(A("f0g"), IND(A("f0"), A("sndl", 6 * t, 6 * t + 6)), AF.Copy)
         for h in range(1, 4):
-            for b in range(2):
+            for b, n in enumerate(NS):
+                label("hop", h, b)
                 s = str(b)
-                b0, b1 = "p%d" % (2 * b), "p%d" % (2 * b + 1)
-                z = A("xw" + s, NBT * (h - 1), NBT * h)
-                wl = A("wl" + s, 0, 6)
-                Y = A(b1, 0, NBT)
-                mm(Y, I, A("yc96"), True, False)
-                mm(Y, A("b16"), z, False, True)
-                R = A(b1, NBT, 2 * NBT)
-                mm(R, I, A("yc96"), True, False)
-                mm(R, A("b16"), z, False, False)
-                mm(R, I, A("cm"), False, True)
-                act(A("ri" + s), R, AF.Identity, A("mgc"))
-                tt(A("hot" + s), Y, A("ri" + s), OP.is_equal)
+                b0, b1, b2 = BANKS[b]
+                z = A("xw" + s, ZO + n * (h - 1), ZO + n * h)
+                wl = A("wl" + s, 0, n // 16)
+                F = A(b1, 0, n)
+                mms(F, [(I, A("yc96", 0, n)), (A("b16"), z), (I, A("cm", 0, n)), (NEG, A("cm", 0, n)), (A("nb16"), z)])
+                if HOT[b] == "s":
+                    act(A("hot" + s), F, AF.Relu, A("p1c"), 16.0)
+                else:
+                    ts(A("hot" + s), F, A("p1c"), None, OP.is_equal)
                 for tab, out in (("uw", "pw"), ("uq", "pq")):
-                    tt(A(out + s), A(tab, *sl(b, t)) if h == 1 else IND(A(tab), wl), A("hot" + s), OP.mult)
-                W = A(b0, 0, NBT)
-                mm(W, I, A("mask"), True, False)
-                mm(W, A("blkf"), A("pw" + s), False, True)
-                Q = A(b1, 0, NBT)
-                mm(Q, I, A("jc"), True, False)
-                mm(Q, A("b4096"), A("pq" + s), False, True)
-                act(A("aa" + s), Q, AF.Abs, A("bc", h - 1, h))
-                scan(A("ll" + s), RXL, W, OP.mult, OP.max)
-                vcp(wl, A("ll" + s, 15, NBT, 16))
+                    tt(A(out + s), A(tab, *cls(t, b)) if h == 1 else IND(A(tab), wl), A("hot" + s), OP.mult)
+                W = A(b0, 0, n)
+                mms(W, [(I, A("mask", 0, n)), (A("blkf"), A("pw" + s))])
+                Q = A(b1, 0, n)
+                mms(Q, [(I, A("jc", 0, n)), (A("b8k"), A("pq" + s))])
+                act(A("aa" + s), Q, AF.Abs, A("bc" + s, h - 1, h))
+                scan(A("ll" + s), A("rx", 0, n), W, OP.mult, OP.max)
+                vcp(wl, A("ll" + s, 15, n, 16))
                 tt(A("of" + s), IND(A("entt"), wl), A("aa" + s), OP.min)
-                vcp(A("ou" + s), A("of" + s))
-                tt(A("da%d%s" % (h, s)), IND(A("ct"), wl), A("aa" + s), OP.is_gt)
+                vcp(A("ou" + s, n * h, n * h + n), A("of" + s))
                 act(A("bw" + s), IND(A("bt"), wl), AF.Copy)
-                gather("gb" + s, A("xw" + s), "ou" + s)
+                gather("gb" + s, A("xw" + s), "ou" + s, n * h, n, HOP_GATHER[b])
                 if h == 3:
-                    act(A("xv" + s), IND(A("xw" + s, XO, XO + V), wl), AF.Copy)
-                scans("gb" + s, "mx" + s, "mn" + s, PARTS)
+                    act(A("xv" + s), IND(A("xw" + s, XO, XG), wl), AF.Copy)
+                    ts(A("cl" + s), A("ou" + s, n, 4 * n), ZO - 1.0, XO - 1.0, OP.max, OP.min)
+                    cl = [A("cl" + s, n * i, n * i + n) for i in range(3)]
+                    mms(A(b1, 0, n), [(A("i8k"), A("ca" + s))] + [(A("nf8k"), c) for c in cl]
+                        + [(I, A("cm2", 0, n)), (NEG, A("cm2", 0, n))] + [(A("f8k"), c) for c in cl]
+                        + [(A("i8k"), A("cb" + s)), (A("nb1"), A("xv" + s))], True, False)
+                scans("gb" + s, "mx" + s, "mn" + s, n, len(HOP_GATHER[b]))
                 fin(b0, A("bw" + s), "mx" + s, "mn" + s,
-                    A("xw" + s, NBT * h, NBT * (h + 1)) if h < 3 else A("z3" + s))
-        for b in range(2):
+                    A("xw" + s, ZO + n * h, ZO + n * (h + 1)) if h < 3 else A("z3" + s))
+        for b, n in enumerate(NS):
+            label("effect", b)
             s = str(b)
-            b0, b1, fb = "p%d" % (2 * b), "p%d" % (2 * b + 1), "p%d" % (6 + b)
-            d = A(b1, 0, NBT)
-            mm(d, A("neg"), A("xv" + s), True, False)
-            mm(d, I, A("z3" + s), False, True)
-            act(A("da" + s), d, AF.Abs)
-            D = A(b0, 0, NBT)
-            for h in range(1, 4):
-                mm(D, A("dead"), A("da%d%s" % (h, s)), h == 1, False)
-            mm(D, A("b1"), A("da" + s), False, True)
-            ts(A("st" + s), D, A("thc", t, t + 1), None, OP.is_le)
-            tt(A("sd" + s), A(fb, NBT, 2 * NBT), A("st" + s), OP.mult)
-            xn = A(b1, 0, NBT)
-            mm(xn, I, A("f0" + s), True, False)
-            mm(xn, I, A("sd" + s), False, True)
-        for b in range(2):
-            xn = A("p%d" % (2 * b + 1), 0, NBT)
-            if b == 0:
-                act(A("xw0", *sl(b, t, XO)), xn, AF.Copy)
-            else:
-                vcp(A("xw0", *sl(b, t, XO)), xn)
+            D = A(BANKS[b][1], 0, n)
+            tt(A("mz" + s), A("z3" + s), A("xv" + s), OP.max)
+            mms(D, [(A("nb1"), A("z3" + s)), (A("b2"), A("mz" + s))], False, True)
+            ts(part("st", b), D, A("thc", t, t + 1), None, OP.is_le)
+            tt(part("sd", b), A(KEEP, NJ + U0[b], NJ + U0[b] + n), part("st", b), OP.mult)
+        label("end")
         if not last:
-            vcp(A("gt%d" % t), IND(own0, A("sndu", 6 * t, 6 * t + 6)))
+            tt(A("gt%d" % t), IND(A("sd"), A("sndl", 6 * t, 6 * t + 6)), A("f0g"), OP.add)
             send(t, A("gt%d" % t), A("land%d" % t))
-        for b in range(2):
-            s = str(b)
-            b0, b1 = "p%d" % (2 * b), "p%d" % (2 * b + 1)
-            tt(A("hs" + s), A("st" + s), A("hit" + s), OP.mult)
-            E = A(b0, 0, NBT)
-            mm(E, A("idf"), A("entt", *sl(b, t)), True, False)
-            mm(E, A("i1152"), A("hs" + s), False, True)
-            if last:
-                act(A("yef", *sl(b, t)), E, AF.Identity, A("nzc"))
-                cols = slice(384 * b, 384 * b + 384)
-                xc = slice(XO + 384 * b, XO + 384 * b + 384)
-                add("y", lambda e, cols=cols: e.dma_start(out=T.ye[:, cols], in_=T.yef[:, cols]),
-                    [("yef", cols.start, cols.stop, 1)], [], (0.1, 0, False), 2.0, "o%d" % b, 16, True)
-                add("y", lambda e, cols=cols, xc=xc: e.dma_start(out=T.yx[:, cols], in_=T.xw0[:, xc]),
-                    [("xw0", xc.start, xc.stop, 1)], [], (0.1, 0, False), 2.0, "o%d" % (2 + b), 16, True)
-            else:
-                act(A("entt", *sl(b, t)), E, AF.Copy)
-                ts(A("ct", *sl(b, t)), A("entt", *sl(b, t)), 1440.0, 1024.0, OP.is_ge, OP.mult)
-                act(A("xw1", *sl(b, t, XO)), A("p%d" % (2 * b + 1), 0, NBT), AF.Copy)
-        if not last:
-            C = A("p0", 0, NBT)
-            mm(C, A("one"), A("hs0"), True, False)
-            mm(C, A("one"), A("hs1"), False, True)
-            rr, c0 = A("rr"), A("p0", 0, NBT)
-            add("v", lambda e, rr=rr, c0=c0: e.tensor_reduce(out=rr[0], in_=c0[0], axis=AX.X, op=OP.add),
-                regs(c0), regs(rr), vc(NBT))
+            tt(A("xw0", *cls(t, None, XO)), A("f0"), A("sd"), OP.add)
+            tt(A("hs"), A(KEEP, 0, NJ), A("st"), OP.mult)
+            for b in range(1, NB):
+                act(A("xw%d" % b, *cls(t, None, XO)), A("xw0", *cls(t, None, XO)), AF.Copy)
+            for bank, tab, by in (("p0", "entt", "ixo"), ("p1", "yef", "i1152")):
+                E = A(bank, 0, NJ)
+                mms(E, [(A("idf"), A(tab, *cls(t))), (A(by), A("hs"))])
+                act(A(tab, *cls(t)), E, AF.Copy)
+            C = A("p3", 0, NJ)
+            mm(C, A("one"), A("hs"), True, True)
+            rr = A("rr")
+            add("v", lambda e, rr=rr, C=C: e.tensor_reduce(out=rr[0], in_=C[0], axis=AX.X, op=OP.add), regs(C), regs(rr), vc(NJ))
             vcp(A("rri"), A("rr"))
             ts(A("rrj"), A("rri"), 31, None, OP.bitwise_and)
             tt(A("thc", t + 1, t + 2), A("rrj"), A("tha", t + 1, t + 2), OP.add)
-            for b in range(2):
-                vcp(A("xw%d" % b, XG + NBT * t, XG + NBT * (t + 1)), A("land%d" % t))
+            for b in range(NB):
+                copy("v" if b == 0 else "s", A("xw%d" % b, XG + 96 * t, XG + 96 * (t + 1)), A("land%d" % t))
+            if t == 0:
+                lists(4)
+        else:
+            label("out")
+            for b, n in enumerate(NS):
+                E = A(BANKS[b][0], 0, n)
+                mm(E, A("idf"), A("yef", *cls(t, b)), True, False)
+                tt(A("xw0", *cls(t, b, XO)), part("f0", b), part("sd", b), OP.add)
+                tt(part("hs", b), part(KEEP, b), part("st", b), OP.mult)
+                mm(E, A("i1152"), part("hs", b), False, True)
+                act(A("yef", *cls(t, b)), E, AF.Copy)
+                cols = slice(4 * U0[b], 4 * (U0[b] + n))
+                xc = slice(XO + cols.start, XO + cols.stop)
+                add("y", lambda e, cols=cols, xc=xc: e.dma_start(out=T.yx[:, cols], in_=T.xw0[:, xc]),
+                    [("xw0", xc.start, xc.stop, 1)], [], (0.1, 0, False), 2.0, "o%d" % (NB + b), 16, True)
+                add("y", lambda e, cols=cols: e.dma_start(out=T.ye[:, cols], in_=T.yef[:, cols]),
+                    [("yef", cols.start, cols.stop, 1)], [], (0.1, 0, False), 2.0, "o%d" % b, 16, True)
 
     _edges(ops)
     if "order" not in PLAN:

@@ -5,16 +5,14 @@ from concourse.mybir import AluOpType as OP, ActivationFunctionType as AF, AxisL
 V, NG, NJ = 768, 384, 192
 NS = [96, 96]
 U0 = [sum(NS[:b]) for b in range(len(NS))]
-NB = len(NS)
-JUDGE_GATHER = ["sv", "ss", "ss"]
-FORM = ["xp", "dd", "pp"]
-ON_VECTOR = [[m for m in range(2) if f[m] == "x"] for f in FORM]
-REGATHER = ["ss", "ss", "ss"]
-HOP_GATHER = ["sss", "sss", "ss"]
-HOT = "sss"
+NB, NM = len(NS), max(NS)
+JUDGE = ["sv", "vv"]
+PARTS = [("v", 12), ("s", 44), ("s", 40)]
+HOP = [[PARTS, PARTS]] * 3
+AGAIN = [[("s", 48), ("s", 48)], None]
+FPARTS = [48, 48]
 BANKS = [("p0", "p1", "p2"), ("p3", "p4", "p5")]
-XBANKS = [("p2", "p7"), ("p5", "p4"), ()]
-DBANKS = [("p1", "p6"), (), ()]
+DBANKS = [("p1", "p7"), ()]
 KEEP = "p6"
 ZO, XO = 1152, 1664
 XG = XO + V
@@ -27,7 +25,7 @@ WHERE = {}
 
 
 def _buf(name, cols, dtype=BF2, where="sbuf", rows=128, pool=True):
-    if not pool or where != "sbuf" or rows != 128 or cols > 288:
+    if not pool or where != "sbuf" or rows != 128 or cols > 384:
         SCRATCH[name] = (where, [rows, cols], dtype)
         WHERE[name] = (name, 0, cols, dtype)
         return
@@ -38,68 +36,62 @@ def _buf(name, cols, dtype=BF2, where="sbuf", rows=128, pool=True):
 
 
 for _b, _w in enumerate(NS):
-    _buf("xw%d" % _b, XE)
+    _buf("xw%d" % _b, XE if AGAIN[_b] else XE + ZO)
     for _n in ("ga", "gb", "mt", "mx", "mn", "m0", "n0"):
         _buf("%s%d" % (_n, _b), 16 * _w)
-    for _n in ("hot", "pq", "bw", "xv", "z3", "mz"):
+    for _n in ("hot", "qw", "bw", "xv", "z3", "mz", "t15", "gk"):
         _buf("%s%d" % (_n, _b), _w)
-    _buf("pw%d" % _b, _w, "float16")
-    _buf("cl%d" % _b, 3 * _w, "float16")
-    for _n in ("ca", "cb"):
-        _buf("%s%d" % (_n, _b), _w, "float16")
-    for _n in ("aa", "ll", "of"):
-        _buf("%s%d" % (_n, _b), _w, "float32")
-    _buf("r1%d" % _b, 144, "float32")
-    _buf("mb%d" % _b, 128, "float32")
+    for _n in ("rl", "mk", "ii"):
+        _buf("%s%d" % (_n, _b), 2 * _w)
+    for _n, _k in (("pw", 1), ("dn", 2), ("cl", 3)):
+        _buf("%s%d" % (_n, _b), _k * _w, "float16")
+    for _n, _k in (("aa", _w), ("of", _w), ("ll", 2 * _w), ("r1", 144), ("mb", 128)):
+        _buf("%s%d" % (_n, _b), _k, "float32")
     _buf("ht%d" % _b, 128)
-    _buf("bc%d" % _b, 4, "float32")
-    _buf("bi%d" % _b, 4, "int32")
-    _buf("ou%d" % _b, 4 * _w, "uint16")
-    _buf("wl%d" % _b, 8, "uint16")
-for _n in range(5):
+    for _n, _k in (("ou", 3 * _w), ("wl", 8), ("xl", 16)):
+        _buf("%s%d" % (_n, _b), _k, "uint16")
+for _n in range(2):
     _buf("eu%d" % _n, NJ, "uint16")
     _buf("ct%d" % _n, NJ)
-    _buf("eh%d" % _n, NJ, "float16")
-for _n in range(2):
-    _buf("xr%d" % _n, 8 * NJ)
+    _buf("xs%d" % _n, NJ)
+    _buf("ek%d" % _n, 2 * NJ, "float16")
+    _buf("xr%d" % _n, 16 * NJ)
 for _n in ("f0", "st", "sd", "hs"):
     _buf(_n, NJ)
-for _n in ("enti", "usri", "uw", "uq"):
+for _n in ("enti", "usri", "uw", "uqi"):
     _buf(_n, V, "int32")
-for _n in ("entt", "yef", "e1", "e2"):
+for _n in ("entt", "yef"):
     _buf(_n, V, "float32")
-_buf("bt", V)
+for _n, _w in (("bt", V), ("uq", V), ("lt", V), ("rx", 2 * NM), ("rm", 8 * NM), ("rn", 8 * NM), ("f0g", 96)):
+    _buf(_n, _w)
 _buf("sndi", 24, "int32", "sbuf", 128, False)
 _buf("sndu", 24, "uint16")
 _buf("sndl", 24, "uint16")
 _buf("thi", 5, "int32", "sbuf", 8)
 _buf("thf", 5, "float32", "sbuf", 8)
-for _n, _w in (("tha", 5), ("thc", 5), ("rr", 1), ("pf", 4), ("bk", 4), ("py", 1), ("p1c", 1), ("mgc", 1), ("nxo", 1), ("pg", 1),
+for _n, _w in (("tha", 5), ("thc", 5), ("rr", 1), ("pf", 4), ("bk", 4), ("py", 1), ("p1c", 1), ("mgc", 1), ("c256", 1), ("cz", 1), ("pg", 1),
                ("top", 128), ("idf", 128)):
     _buf(_n, _w, "float32")
-for _n, _w in (("rri", 1), ("rrj", 1), ("ji", 96), ("jj", 96), ("pi", 4), ("pj", 4), ("pk", 1)):
+for _n, _w in (("rri", 1), ("rrj", 1), ("ji", NM), ("jj", NM), ("pi", 4), ("pj", 4), ("pk", 1)):
     _buf(_n, _w, "int32")
-_buf("gs0", NG)
-_buf("f0g", 96)
+for _n, _w, _d in (("ca", NM, "float16"), ("cb", NM, "float16"), ("bc", 4, "float32"), ("bi", 4, "int32")):
+    _buf(_n, _w, _d)
+_buf("gs0", NG, BF2, "sbuf", 128, False)
 for _n in range(4):
     _buf("gt%d" % _n, 96, BF2, "sbuf", 128, False)
     _buf("land%d" % _n, 96, BF2, "sbuf", 128, False)
-for _n in ("one", "idn", "half", "neg", "ict", "ik", "ig", "ixo", "i1152", "blkh", "blk", "b16", "nb16", "nb1", "b2", "b8k",
-           "w16", "wn16", "w32", "wx0", "wx1"):
+for _n in ("one", "idn", "half", "nhalf", "neg", "ict", "ik", "ig", "ixo", "ixe", "i1152", "i15", "blkh", "blk", "b16", "nb16",
+           "nb1", "b2", "b8", "i256", "w16", "b1m", "i8k", "f8k", "nf8k"):
     _buf(_n, 128)
-for _n in ("idh", "blkf", "i8k", "f8k", "nf8k"):
-    _buf(_n, 128, "float16")
 for _n in ("oe", "ee0", "ee"):
     _buf(_n, 128, "float32", "sbuf", 8)
-for _n in ("yc96", "jc", "mask", "cm", "cq", "cm2"):
-    _buf(_n, 96)
-_buf("rx", 16 * max(NS))
-_buf("rn", 16 * max(NS))
+for _n in ("yc96", "jc", "j16", "mask", "cm", "cq", "cm2", "cm3"):
+    _buf(_n, NM)
 for _n in range(8):
     _buf("p%d" % _n, 512, "float32", "psum")
-LOADS = ["snd", "xa", "ent", "yc", "bn", "usr", "th"]
-SEMAPHORES = (["sv", "ss", "st", "sg", "loc"] + ["o%d" % n for n in range(2 * NB)] + ["ld_" + n for n in LOADS]
-              + ["ld_y%d" % b for b in range(NB)] + ["ld_x%d" % b for b in range(NB)] + ["arr%d" % t for t in range(5)])
+LOADS = ["snd", "xa", "ent", "yc", "bn", "usr", "th", "x1", "y1", "y2"]
+SEMAPHORES = (["sv", "ss", "st", "sg"] + ["o%d" % n for n in range(2 * NB)] + ["ld_" + n for n in LOADS]
+              + ["arr%d" % t for t in range(5)] + ["left%d" % t for t in range(5)])
 QS = {"v": "sv", "s": "ss", "t": "st", "g": "sg"}
 PLAN = {}
 
@@ -123,7 +115,7 @@ def _edges(ops):
             for (r2, j, w2) in hist.get(r[0], ()):
                 if j == i or not (_bank(r) or ((wr or w2) and _overlap(r, r2))):
                     continue
-                pre[j] = pre.get(j, False) or ops[j]["q"] != o["q"] or (w2 and (not wr or o["q"] != "t")) or ops[j]["dma"]
+                pre[j] = pre.get(j, False) or ops[j]["q"] != o["q"] or ((wr or w2) and o["q"] != "t") or ops[j]["dma"]
         for j in o["after"]:
             pre[j] = True
         for wr, r in both:
@@ -139,116 +131,35 @@ def _edges(ops):
 
 def _cost(o, m):
     f, n, gath = o["cost"]
-    return f * m[0] + max(64, n * (m[2] if gath else 1)) * 1.0e-3 * m[1] if n else f
+    return f * m[0] + max(64, n * m[2] * gath if gath else n) * 1.0e-3 * m[1] if n else f
 
 
-def _schedule(ops, succ, m, slack=0.12):
-    n = len(ops)
-    cost = [_cost(o, m) for o in ops]
-    pri = [0.0] * n
-    for i in range(n - 1, -1, -1):
-        x = 0.0
-        for j in succ[i]:
-            x = max(x, pri[j] + (m[3] if ops[j]["pre"][i] else 0.0))
-        pri[i] = x + cost[i] + ops[i]["lag"] * m[4]
-    left = [len(o["pre"]) for o in ops]
-    rdy = [0.0] * n
-    cand = {}
-    for i in range(n):
-        if left[i] == 0:
-            cand.setdefault(ops[i]["q"], []).append(i)
-    free = {}
-    order = []
-    while True:
-        q = None
-        for k in cand:
-            if cand[k]:
-                s = max(free.get(k, 0.0), min(rdy[i] for i in cand[k]))
-                if q is None or s < s0:
-                    q, s0 = k, s
-        if q is None:
-            return order
-        pick = None
-        for i in cand[q]:
-            if rdy[i] <= s0 + slack and (pick is None or pri[i] > pri[pick]):
-                pick = i
-        cand[q].remove(pick)
-        order.append(pick)
-        st = max(s0, rdy[pick])
-        free[q] = st + cost[pick]
-        for j in succ[pick]:
-            e = free[q] + ops[pick]["lag"] * m[4] + m[3] if ops[j]["pre"][pick] else st
-            rdy[j] = max(rdy[j], e)
-            left[j] -= 1
-            if left[j] == 0:
-                cand.setdefault(ops[j]["q"], []).append(j)
+MODELS = [(1.0, 0.87, 1.4, 0.13, 0.6), (1.2, 1.15, 1.8, 0.12, 1.1)]
+STEPS = 11000
+SEED, HEAT, LEAD = 8, 0.005, (0.5, 1.3, 2.1, 3.0)
 
 
-def _length(ops, order, m):
-    free, fin, top = {}, [0.0] * len(ops), 0.0
-    for i in order:
-        o = ops[i]
-        t = free.get(o["q"], 0.0)
-        for j in o["pre"]:
-            if o["pre"][j]:
-                t = max(t, fin[j] + m[3])
-        free[o["q"]] = t + _cost(o, m)
-        fin[i] = free[o["q"]] + o["lag"] * m[4]
-        top = max(top, fin[i])
-    return top
-
-
-MODELS = [(1.0, 0.9, 1.56, 0.1, 1.0), (1.0, 0.83, 1.2, 0.06, 1.0), (1.3, 1.2, 2.0, 0.1, 1.3), (1.0, 0.9, 1.3, 0.2, 1.3)]
-STEPS = 1200
-
-
-def _plan(ops):
-    succ = [[] for _ in ops]
-    for i, o in enumerate(ops):
-        for j in o["pre"]:
-            succ[j].append(i)
-    keys = 1 + max(o["key"] for o in ops)
-    rng = np.random.RandomState(5)
-    cur = np.full(keys + 1, 2.0)
-    cur[keys] = 0.0
-    best = None
-    for step in range(STEPS):
-        c = cur.copy()
-        if step:
-            if rng.rand() < 0.5:
-                for _i in range((1, 2, 4, 10, 25)[rng.randint(5)]):
-                    c[rng.randint(keys)] = 0.25 * rng.randint(26)
-            else:
-                a, w = rng.randint(keys), (3, 8, 20, 60)[rng.randint(4)]
-                hi = min(keys, a + w)
-                c[a:hi] = np.clip(c[a:hi] + 0.25 * rng.randint(-6, 7), 0.0, 6.25)
-        order = _schedule(ops, succ, MODELS[0], 0.12, [float(c[o["key"]]) for o in ops])
-        score = []
-        for m in range(len(MODELS)):
-            score.append(_length(ops, order, MODELS[m]))
-            if best and m == 0 and score[0] > 1.006 * best[1][0]:
-                break
-        if len(score) < len(MODELS):
-            continue
-        if not best:
-            base = score
-        x = sum(a / b for a, b in zip(score, base))
-        if not best or x <= best[0]:
-            best, cur = (x, score, order), c
-    return best[2]
-
-
-MODELS = [(1.0, 0.87, 1.56, 0.1, 1.0), (1.2, 1.15, 1.8, 0.15, 1.2)]
-STEPS = 6000
-
-
-def _plan(ops):
+def _planner(calls):
+    _edges(calls)
+    head, ops = [], []
+    for i, o in enumerate(calls):
+        if o["q"] == "t" and i - 1 in o["pre"] and calls[i - 1]["q"] == "t" and all(
+                not w or calls[j]["once"] or head[j] in ops[-1]["pre"] for j, w in o["pre"].items()):
+            p = ops[-1]
+        else:
+            p = {"q": o["q"], "key": o["key"], "lag": o["lag"], "calls": [], "pre": {}}
+            ops.append(p)
+        head.append(len(ops) - 1)
+        p["calls"].append(i)
+        for j, w in o["pre"].items():
+            if head[j] != len(ops) - 1:
+                p["pre"][head[j]] = p["pre"].get(head[j], False) or w
     n = len(ops)
     names = sorted(set(o["q"] for o in ops))
     queue = [names.index(o["q"]) for o in ops]
     key = [o["key"] for o in ops]
     wait = [[j for j in o["pre"] if o["pre"][j]] for o in ops]
-    costs = [[_cost(o, m) for o in ops] for m in MODELS]
+    costs = [[sum(_cost(calls[i], m) for i in o["calls"]) for o in ops] for m in MODELS]
     lags = [[o["lag"] * m[4] + m[3] for o in ops] for m in MODELS]
     succ = [[] for _ in ops]
     for i, o in enumerate(ops):
@@ -258,17 +169,21 @@ def _plan(ops):
     for i in range(n - 1, -1, -1):
         path[i] = costs[0][i] + max([path[j] + (lags[0][i] if w else 0.0) for j, w in succ[i]] + [lags[0][i]])
     count = [len(o["pre"]) for o in ops]
+    lands = [i for i in range(n) if ops[i]["q"] == "x"]
+    early = [i for i in range(n - 1, -1, -1) if calls[ops[i]["calls"][0]]["once"]]
 
     def schedule(bonus, patience):
         cost, lag = costs[0], lags[0]
         pri = [path[i] + bonus[key[i]] for i in range(n)]
+        for i in early:
+            pri[i] = cost[i] + lag[i] + bonus[key[i]] + max([pri[j] for j, _w in succ[i]] + [0.0])
         left, rdy = list(count), [0.0] * n
         cand = [[] for _ in names]
         for i in range(n):
             if not left[i]:
                 cand[queue[i]].append(i)
         free, soon = [0.0] * len(names), [0.0 if c else 1e9 for c in cand]
-        order, top = [], 0.0
+        order = []
         for _i in range(n):
             s0 = min(soon)
             q = soon.index(s0)
@@ -282,8 +197,6 @@ def _plan(ops):
             st = rdy[pick] if rdy[pick] > s0 else s0
             end = free[q] = st + cost[pick]
             done = end + lag[pick]
-            if done > top:
-                top = done
             soon[q] = max(end, min([rdy[i] for i in c])) if c else 1e9
             for j, w in succ[pick]:
                 e = done if w else st
@@ -296,52 +209,103 @@ def _plan(ops):
                     e = max(free[r], rdy[j])
                     if e < soon[r]:
                         soon[r] = e
-        return order, top
+        return order, pri, rdy
 
     def length(order, m):
         cost, lag = costs[m], lags[m]
-        free, fin = [0.0] * len(names), [0.0] * n
+        free, fin, why = [(0.0, -1)] * len(names), [0.0] * n, [-1] * n
         for i in order:
-            t = free[queue[i]]
+            t, w = free[queue[i]]
             for j in wait[i]:
                 if fin[j] > t:
-                    t = fin[j]
+                    t, w = fin[j], j
             t += cost[i]
-            free[queue[i]] = t
+            free[queue[i]] = (t, i)
             fin[i] = t + lag[i]
-        return max(fin)
+            why[i] = w
+        top = max(fin)
+        i, pairs = fin.index(top), []
+        while why[i] >= 0:
+            j = why[i]
+            if j not in ops[i]["pre"]:
+                pairs.append((i, j, fin[j] - lag[j] - cost[j]))
+            i = j
+        return top + (len(lands) == 3) * 2 * (fin[lands[-1]] - fin[lands[1]]), pairs
 
-    keys = 1 + max(key)
+    return ops, key, schedule, length
+
+
+def _plan(start, few, calls):
+    ops, key, schedule, length = _planner(few)
+    n, keys = len(ops), 1 + max(o["key"] for o in calls)
     batch = [0] * keys
-    for o in ops:
+    for o in calls:
         batch[o["key"]] = o["batch"]
-    rng = np.random.RandomState(5)
-    cur = best = None
-    for step in range(STEPS):
-        if step < 4:
-            c = ([-(0.5 + 0.25 * step) * b for b in batch], [0.1] * keys)
-        else:
+    kin = {}
+    for o in calls:
+        kin.setdefault(o["kin"], set()).add(o["key"])
+    kin = dict((k, sorted(l)) for l in kin.values() for k in l)
+    once = set(o["key"] for o in calls if o["once"])
+    rng = np.random.RandomState(SEED)
+    unit = []
+
+    def judge(c):
+        made = schedule(*c)
+        res = [length(made[0], m) for m in range(len(MODELS))]
+        if not unit:
+            unit.extend(r[0] for r in res)
+        return sum(r[0] / u for r, u in zip(res, unit)), c, made, res
+
+    def climb(cur, steps, heat, alike, fixed=()):
+        best = cur
+        for step in range(steps):
             c = (list(cur[1][0]), list(cur[1][1]))
-            for _i in range((1, 1, 2, 4)[rng.randint(4)]):
+            same = (lambda k: kin[k]) if rng.rand() < alike else (lambda k: (k,))
+            how = rng.rand()
+            if how < 0.6:
+                pairs = cur[3][0 if rng.rand() < 0.7 else -1][1]
+                i, j, at = pairs[rng.randint(len(pairs))]
+                gap = max(0.0, cur[2][1][j] - cur[2][1][i]) + 0.02 + (0.3, 0.3, 1.5, 5.0)[rng.randint(4)] * rng.rand()
+                up = rng.rand() < 0.5
+                for k in same(key[i] if up else key[j]):
+                    c[0][k] += gap if up else -gap
+                for k in same(key[i]):
+                    c[1][k] = min(0.9, max(c[1][k], cur[2][2][i] - at + 0.02))
+            elif how < 0.7:
+                x = 0.1 * rng.randint(7)
+                for k in same(key[rng.randint(n)]):
+                    c[1][k] = x
+            else:
                 a = key[rng.randint(n)]
-                if rng.rand() < 0.3:
-                    c[1][a] = 0.1 * rng.randint(7)
-                else:
-                    x = (0.3, 1.0, 3.0)[rng.randint(3)] * rng.randn()
-                    for k in range(a, min(keys, a + (1, 1, 3, 8, 20)[rng.randint(5)])):
+                x = (0.3, 1.0, 3.0)[rng.randint(3)] * rng.randn()
+                for b in range(a, min(keys, a + (1, 1, 3, 8, 20)[rng.randint(5)])):
+                    for k in same(b):
                         c[0][k] += x
-        order, top = schedule(*c)
-        bar = 1e9 if step < 4 else cur[0] - 0.001 * (1 - step / STEPS) * math.log(rng.rand())
-        if step == 0:
-            unit = [top] + [length(order, m) for m in range(1, len(MODELS))]
-        if cur and top / unit[0] > bar - cur[0] + cur[2] + 0.004:
-            continue
-        x = top / unit[0] + sum(length(order, m) / unit[m] for m in range(1, len(MODELS)))
-        if cur is None or x <= (cur[0] if step < 4 else bar):
-            cur = (x, c, top / unit[0])
-            if best is None or x < best[0]:
-                best = (x, order)
-    return best[1]
+            for k in fixed:
+                c[0][k], c[1][k] = cur[1][0][k], cur[1][1][k]
+            if c == cur[1]:
+                continue
+            new = judge(c)
+            if new[0] <= cur[0] - heat * (1 - step / steps) * math.log(rng.rand()):
+                cur = new
+                if cur[0] < best[0]:
+                    best = cur
+        return best
+
+    field = [judge(([-lead * b for b in batch], [0.1] * keys)) for lead in LEAD]
+    while len(field) > 1:
+        field = [climb(c, STEPS // (3 * len(field)), HEAT, 0.7, once) for c in field]
+        field = sorted(field, key=lambda c: c[0])[:len(field) // 2]
+    best = climb(field[0], STEPS // 6, HEAT / 2, 0.3, once)
+    ops, key, schedule, length = _planner(start)
+    n = len(ops)
+    del unit[:]
+    best = climb(judge(best[1]), STEPS // 2, HEAT / 2, 0.0, set(range(keys)) - once)
+    del unit[:]
+    ops, key, schedule, length = _planner(calls)
+    n = len(ops)
+    best = climb(judge(best[1]), STEPS // 10, HEAT / 4, 0.3)
+    return [i for p in best[2][0] for i in ops[p]["calls"]]
 
 
 def rank_program(g, core, T, topo):
@@ -351,17 +315,17 @@ def rank_program(g, core, T, topo):
     ops = []
     names = {}
     step = [None, 0]
-    now = [0]
     eng = {"v": g.vector, "s": g.scalar, "t": g.tensor, "g": g, "y": g.sync}
 
     def label(*x):
-        step[:] = [x or None, 0]
+        step[:] = [x, 0]
 
     def add(q, fn, rd, wr, cost, lag=0.0, sem=None, amount=1, dma=False, after=()):
         key = names.setdefault((step[0], step[1]), len(names))
         step[1] += 1
-        ops.append({"q": q, "fn": fn, "key": key, "batch": step[0][-1] if step[0] and len(step[0]) > 1 else 0, "rd": rd, "wr": wr, "cost": cost, "lag": lag, "sem": sem, "amount": amount,
-                    "dma": dma, "after": list(after), "remote": False})
+        ops.append({"q": q, "fn": fn, "key": key, "once": step[0] is None, "kin": (step[0] and step[0][::2], step[1]),
+                    "batch": step[0][-1] if step[0] and len(step[0]) > 1 else 0, "rd": rd, "wr": wr,
+                    "cost": cost, "lag": lag, "sem": sem, "amount": amount, "dma": dma, "after": list(after), "remote": False})
         return len(ops) - 1
 
     def A(name, lo=0, hi=None, step=1, rows=None):
@@ -406,8 +370,10 @@ def rank_program(g, core, T, topo):
         return add("v", fn, regs(a, s1, s2), regs(out), vc(out[2] * half(out, a)))
 
     def vcp(out, a):
-        return add("v", lambda e: e.tensor_copy(out=out[0], in_=a[0]), regs(a), regs(out),
-                   vc(out[2], True) if a[3] else vc(out[2] * half(out, a)))
+        fn = lambda e: e.tensor_copy(out=out[0], in_=a[0])
+        if out[3]:
+            return add("v", fn, regs(a) + out[1][1:], out[1][:1], vc(out[2], 2.4))
+        return add("v", fn, regs(a), regs(out), vc(out[2], True) if a[3] else vc(out[2] * half(out, a)))
 
     def scan(out, d0, d1, op0, op1):
         return add("v", lambda e: e.tensor_tensor_scan(out=out[0], data0=d0[0], data1=d1[0], initial=0.0, op0=op0, op1=op1),
@@ -418,13 +384,10 @@ def rank_program(g, core, T, topo):
 
     def act(out, a, func, bias=None, scale=1.0):
         if bias is None:
-            fn = lambda e: e.activation(out=out[0], in_=a[0], func=func)
+            fn = lambda e: e.activation(out=out[0], in_=a[0], func=func, scale=val(scale))
         else:
-            fn = lambda e: e.activation(out=out[0], in_=a[0], func=func, bias=val(bias), scale=scale)
-        return add("s", fn, regs(a, bias), regs(out), (0.065, out[2], a[3]))
-
-    def copy(q, out, a):
-        return vcp(out, a) if q == "v" else act(out, a, AF.Copy)
+            fn = lambda e: e.activation(out=out[0], in_=a[0], func=func, bias=val(bias), scale=val(scale))
+        return add("s", fn, regs(a, bias, scale), regs(out), (0.065, out[2], a[3]))
 
     def mm(out, l, r, start, stop):
         return add("t", lambda e: e.matmul(out[0], l[0], r[0], start, stop), regs(l, r), regs(out),
@@ -438,6 +401,11 @@ def rank_program(g, core, T, topo):
         return add("g", lambda e: e.affine_select(out=out[0], in_=a[0], pattern=pattern, compare_op=op, fill=0.0, base=base,
                                                  channel_multiplier=cm), regs(a), regs(out), (0.17, 2 * out[2], False))
 
+    def copy(q, out, a):
+        if q == "g":
+            return sel(out, a, [[0, out[2]]], OP.is_ge, 0, 0)
+        return vcp(out, a) if q == "v" else act(out, a, AF.Copy)
+
     def iota(out, pattern, base, cm):
         if kind(out) != "int32":
             fn = lambda e: e.iota(out[0], pattern=pattern, base=base, channel_multiplier=cm, allow_small_or_imprecise_dtypes=True)
@@ -445,9 +413,9 @@ def rank_program(g, core, T, topo):
             fn = lambda e: e.iota(out[0], pattern=pattern, base=base, channel_multiplier=cm)
         return add("g", fn, [], regs(out), (0.13, 2 * out[2], False))
 
-    def load(q, name, out, sem=None):
-        return add(q, lambda e: e.dma_start(out=out[0], in_=T[name][:, :]), [], regs(out), (0.1, 0, False), 2.2,
-                   sem or "ld_" + name, 16, True)
+    def load(q, name, out, lag, sem=None, after=()):
+        return add(q, lambda e: e.dma_start(out=out[0], in_=T[name][:, :]), [], regs(out), (0.1, 0, False), lag,
+                   sem or "ld_" + name, 16, True, after)
 
     dst = T.cores[(rank - 1) % len(T.cores)]
     src = T.cores[(rank + 1) % len(T.cores)]
@@ -457,10 +425,11 @@ def rank_program(g, core, T, topo):
     n_in = len(topo.engines(src, core)[:8])
 
     def send(slot, a, land):
-        j = add("g", lambda e: e.remote_dma(land[0], a[0], T.sem["arr%d" % slot], T.sem.loc, pid, rid, mask),
-                regs(a), [], (0.3, 0, False))
+        j = add("g", lambda e: e.remote_dma(land[0], a[0], T.sem["arr%d" % slot], T.sem["left%d" % slot], pid, rid, mask),
+                regs(a), [], (0.3, 0, False), 1.0, "left%d" % slot, len(es))
         ops[j]["remote"] = True
-        add("x", None, [], regs(land), (0.0, 0, False), 2.5, "arr%d" % slot, n_in, True, (j,))
+        add("x", None, [], regs(land), (0.0, 0, False), 1.5, "arr%d" % slot, n_in, True, (j,))
+        return j
 
     def cls(t, b=None, base=0):
         lo, n = (0, NJ) if b is None else (U0[b], NS[b])
@@ -470,21 +439,19 @@ def rank_program(g, core, T, topo):
         return A(name, times * U0[b], times * (U0[b] + NS[b]))
 
     own0 = A("xw0", XO, XG)
-    load("y", "snd", A("sndi"))
-    load("s", "xa", own0)
-    load("y", "ent", A("enti"))
-    load("s", "yc", A("xw0", 0, ZO))
-    load("y", "bn", A("bt"))
-    load("s", "usr", A("usri"))
-    load("y", "th", A("thi"))
-    for b in range(1, NB):
-        load("y", "xa", A("xw%d" % b, XO, XG), "ld_x%d" % b)
-        load("s", "yc", A("xw%d" % b, 0, ZO), "ld_y%d" % b)
+    load("y", "snd", A("sndi"), 1.5)
+    load("s", "xa", own0, 2.0)
+    load("y", "ent", A("enti"), 3.0)
+    load("s", "yc", A("xw0", 0, ZO), 3.5)
     for c in range(4):
         ts(A("sndu", 6 * c, 6 * c + 6), A("sndi", 6 * c, 6 * c + 6), 4, c, OP.mult, OP.add)
     act(A("gs0"), IND(own0, A("sndu")), AF.Copy)
-    send(4, A("gs0"), A("xw0", XG, XE))
+    first = send(4, A("gs0"), A("xw0", XG, XE))
     vcp(A("sndl"), A("sndi"))
+    for i, (name, out, sem) in enumerate((("xa", A("xw1", XO, XG), "ld_x1"), ("yc", A("xw1", 0, ZO), "ld_y1"), ("bn", A("bt"), None),
+                                          ("yc", A("xw1", XE, XE + ZO), "ld_y2"), ("usr", A("usri"), None), ("th", A("thi"), None))):
+        load("y", name, out, 2.0 + 0.8 * i, sem, (first,))
+    sel(A("xw1", ZO, XO), A("xw0", XO, XO + GAP), [[0, GAP]], OP.is_gt, 0, 0)
 
     fill(A("one"), 1.0)
     fill(A("oe"), 1.0)
@@ -493,248 +460,297 @@ def rank_program(g, core, T, topo):
     sel(A("blk"), A("blkh"), [[16, 8], [0, 16]], OP.is_ge, 15, -1)
     sel(A("ee0"), A("oe"), [[1, 128]], OP.is_ge, 0, -16)
     sel(A("ee"), A("ee0"), [[-1, 128]], OP.is_ge, 15, 16)
-    iota(A("ji"), [[1, 96]], 128, -1)
-    iota(A("jc"), [[1, 96]], 0, 0)
+    iota(A("ji"), [[1, NM]], 128, -1)
+    iota(A("jc"), [[1, NM]], 0, 0)
     iota(A("pi"), [[0, 4]], 0, 1)
     fill(A("top"), 0.0)
-    ts(A("top", 0, 128, 16), A("jc", 0, 8), 131072.0, 65535.0, OP.mult, OP.add)
+    ts(A("top", 0, 128, 16), A("jc", 0, 8), 131072.0, 131071.0, OP.mult, OP.add)
     ts(A("pj"), A("pi"), 15, None, OP.bitwise_and)
     vcp(A("pf"), A("pj"))
     ts(A("pk"), A("pi", 0, 1), 112, None, OP.bitwise_and)
     ts(A("pg"), A("pk"), 8192.0, None, OP.mult)
-    for name, of, x in (("half", "idn", 0.5), ("neg", "idn", -1.0), ("ict", "idn", 65536.0), ("i1152", "idn", 1152.0),
-                        ("ixo", "idn", -float(XO)), ("idf", "idn", 1.0), ("idh", "idn", 1.0), ("i8k", "idn", 8192.0), ("ik", "idn", A("pf", 0, 1)),
-                        ("ig", "idn", A("pg")), ("b16", "blk", 0.0625), ("nb16", "blk", -0.0625), ("nb1", "blk", -1.0),
-                        ("b2", "blk", 2.0), ("b8k", "blk", 8192.0), ("blkf", "blk", 1.0), ("f8k", "blk", 8192.0),
-                        ("nf8k", "blk", -8192.0), ("w16", "blk", 16.0), ("wn16", "blk", -16.0), ("w32", "blk", 32.0)):
-        ts(A(name), A(of), x, None, OP.mult)
-    for m in sorted(set(m for b in range(NB) for m in ON_VECTOR[b])):
-        vcp(A("wx%d" % m), A("wn16"))
-        fill(A("wx%d" % m, 1 - m, 128, 2), 0.0)
+    for name, of, x in (("half", "idn", 0.5), ("nhalf", "idn", -0.5), ("neg", "idn", -1.0), ("ict", "idn", 65536.0),
+                        ("i1152", "idn", 1152.0), ("ixo", "idn", -float(XO)), ("ixe", "idn", -XE / 2), ("idf", "idn", 1.0),
+                        ("ik", "idn", A("pf", 0, 1)), ("ig", "idn", A("pg")), ("i15", "idn", -15.0 * 2 ** 19),
+                        ("b16", "blk", 0.0625), ("nb16", "blk", -0.0625), ("nb1", "blk", -1.0), ("b2", "blk", 2.0),
+                        ("b8", "blk", 8.0), ("i256", "idn", 1.0 / 256), ("w16", "blk", 16.0), ("b1m", "blk", 2.0 ** 20),
+                        ("i8k", "idn", 8192.0), ("f8k", "blk", 8192.0), ("nf8k", "blk", -8192.0)):
+        act(A(name), A(of), AF.Identity, None, x)
     ts(A("py"), A("pf", 0, 1), -0.0625, -15.0 / 32, OP.mult, OP.add)
-    if HOT[0] == "s":
-        ts(A("p1c"), A("pf", 0, 1), 1.0, None, OP.add)
-    else:
-        ts(A("p1c"), A("pf", 0, 1), -0.0625, None, OP.mult)
-    ts(A("bk"), A("pf"), -8192.0, None, OP.mult)
-    for b, n in enumerate(NS):
-        iota(A("bi%d" % b), [[n, 4]], ZO, 0)
-        tt(A("bc%d" % b), A("bk"), A("bi%d" % b), OP.add)
-        c0 = (48 * (ZO - 1) + 3 * n + 3) % GAP
-        ts(A("ca%d" % b), A("jc", 0, n), 3.0, c0 - (GAP - 1) / 2, OP.mult, OP.add)
-        ts(A("cb%d" % b), A("jc", 0, n), -3.0, -float(c0), OP.mult, OP.add)
-        fill(A("r1%d" % b, 128, 144), 1048576.0)
+    ts(A("p1c"), A("pf", 0, 1), 16384.0, 1024.0, OP.mult, OP.add)
+    ts(A("bk"), A("pf"), -8192.0, -8192.0, OP.mult, OP.add)
     ts(A("jj"), A("ji"), 15, None, OP.bitwise_and)
     ts(A("mask"), A("jj"), 0, -4096.0, OP.not_equal, OP.mult)
-    ts(A("yc96"), A("one", 0, 96), A("py"), None, OP.mult)
-    for name, x, y in (("cm", MAGIC, None), ("cm2", MAGIC * 8192 * GAP, None), ("cq", -0.25, None), ("rx", 1.0, 0.0),
-                       ("rn", 0.0, 512.0), ("mgc", -MAGIC, None), ("nxo", -float(XO), None)):
+    act(A("j16"), A("jc"), AF.Identity, None, 16.0)
+    iota(A("bi"), [[NM, 4]], ZO, 0)
+    tt(A("bc"), A("bk"), A("bi"), OP.add)
+    c0 = (48 * (ZO - 1) + 3 * NM + 3) % GAP
+    ts(A("ca"), A("jc"), 3.0, c0 - (GAP - 1) / 2, OP.mult, OP.add)
+    ts(A("cb"), A("jc"), -3.0, -float(c0), OP.mult, OP.add)
+    for b, n in enumerate(NS):
+        s = str(b)
+        act(A("r1" + s, 128, 144), A("one", 0, 16), AF.Identity, None, 1048576.0)
+        if not AGAIN[b]:
+            ts(A("mk" + s, 0, n), A("mask", 0, n), 1024.0, None, OP.add)
+            tt(A("mk" + s, n, 2 * n), A("mask", 0, n), A("j16", 0, n), OP.add)
+            for i in range(2):
+                act(A("ii" + s, n * i, n * i + n), A("idn", 0, n), AF.Copy)
+                ts(A("ek%d" % i, 2 * U0[b] + n, 2 * U0[b] + 2 * n), A("one", 0, n), A("pf", 0, 1), None, OP.mult)
+    act(A("yc96"), A("one", 0, NM), AF.Identity, None, A("py"))
+    for name, x in (("cm", MAGIC), ("cm2", MAGIC * 8192 * GAP), ("cm3", MAGIC * 2 ** 24), ("cq", -0.25), ("mgc", -MAGIC)):
+        act(A(name), A("one", 0, WHERE[name][2]), AF.Identity, None, x)
+    for name, x in (("c256", 256.0), ("cz", 0.5 - ZO)):
         fill(A(name), x)
-        if y is not None:
-            fill(A(name, 0, WHERE[name][2], 16), y)
-    I, NEG = A("idn"), A("neg")
+    for name, x, y in (("rx", 1.0, 0.0), ("rm", 0.0, -512.0), ("rn", 0.0, 512.0)):
+        fill(A(name), x)
+        fill(A(name, 0, WHERE[name][2], 16), y)
+    I, NEG, HALF = A("idn"), A("neg"), A("half")
 
     def lists(t):
-        vcp(A("eu%d" % t), A("entt", *cls(t)))
-        ts(A("ct%d" % t), A("eu%d" % t), float(ZO), None, OP.is_lt)
-        ts(A("eh%d" % t), A("eu%d" % t), -1024.0, None, OP.add)
+        vcp(A("eu%d" % (t % 2)), A("entt", *cls(t)))
+        ts(A("ct%d" % (t % 2)), A("eu%d" % (t % 2)), float(ZO), None, OP.is_lt)
+        for b, n in enumerate(NS):
+            ts(A("ek%d" % (t % 2), 2 * U0[b], 2 * U0[b] + n), part("eu%d" % (t % 2), b), -1024.0, None, OP.add)
 
-    def repeat(t):
-        for r in range(8):
-            sel(A("xr%d" % (t % 2), r, 8 * NJ, 8), A("xw0", *cls(t, None, XO)), [[0, NJ]], OP.is_ge, 0, 0)
+    def repeat(t, queues):
+        for r in range(16):
+            copy(queues[r % len(queues)], A("xr%d" % (t % 2), r, 16 * NJ, 16), A("xw0", *cls(t, None, XO)))
+        for b, n in enumerate(NS):
+            w = n // len(JUDGE[b])
+            sel(part("xs%d" % (t % 2), b), A("xw0", *cls(t, b, XO)), [[1, n]], OP.is_ge, -w * JUDGE[b].count("s"), 0)
 
     for c in range(4):
-        ts(A("e1", *cls(c)), A("enti", *cls(c)), float(ZO), -float(XE), OP.is_ge, OP.mult)
-        ts(A("e2", *cls(c)), A("enti", *cls(c)), float(XO), None, OP.add)
-        tt(A("entt", *cls(c)), A("e1", *cls(c)), A("e2", *cls(c)), OP.add)
-        act(A("yef", *cls(c)), A("e2", *cls(c)), AF.Identity, A("nxo"))
-        lists(c)
+        vcp(A("yef", *cls(c)), A("enti", *cls(c)))
+        act(A("lt", NJ * c, NJ * c + NJ), A("yef", *cls(c)), AF.Sign, A("cz"))
+        E = A(("p2", "p4", "p5", "p2")[c], 0, NJ)
+        mms(E, [(A("idf"), A("yef", *cls(c))), (A("ixe"), A("lt", NJ * c, NJ * c + NJ))])
+        act(A("entt", *cls(c)), E, AF.Identity, A("c256"))
+    lists(0)
     ts(A("uw"), A("usri"), 4, None, OP.logical_shift_right)
-    ts(A("uq"), A("usri"), 15, None, OP.bitwise_and)
+    ts(A("uqi"), A("usri"), 15, None, OP.bitwise_and)
+    vcp(A("uq"), A("uqi"))
     vcp(A("thf"), A("thi"))
-    mm(A("p0", 0, 5), A("ee"), A("thf"), True, True)
-    vcp(A("tha"), A("p0", 0, 5))
-    vcp(A("thc", 0, 1), A("tha", 0, 1))
-    for b in range(1, NB):
-        act(A("xw%d" % b, XG, XE), A("xw0", XG, XE), AF.Copy)
-    repeat(0)
+    mm(A("p5", 0, 5), A("ee"), A("thf"), True, True)
+    act(A("tha"), A("p5", 0, 5), AF.Copy)
+    act(A("thc", 0, 1), A("tha", 0, 1), AF.Copy)
+    act(A("xw1", XG, XE), A("xw0", XG, XE), AF.Copy)
+    repeat(0, "vsvgvs")
+    setup = len(ops)
 
-    def scans(G, X, N, n, parts):
-        w = 16 * n // parts
-        for m in range(parts):
-            lo, hi = w * m, w * m + w
-            scan(A(X, lo, hi), A("rx", lo, hi), A(G, lo, hi), OP.mult, OP.max)
-            scan(A(N, lo, hi), A("rn", lo, hi), A(G, lo, hi), OP.add, OP.min)
+    def gather(out, b, off, first, parts):
+        lo = 0
+        for q, w in parts:
+            copy(q, A(out, 16 * lo, 16 * (lo + w)), IND(A("xw%d" % b, 0, XE), A(off, first + lo, first + lo + w)))
+            lo += w
 
-    def gather(out, win, off, lo, n, queues):
-        w = n // len(queues)
-        for m, q in enumerate(queues):
-            copy(q, A(out, 16 * w * m, 16 * w * m + 16 * w), IND(win, A(off, lo + w * m, lo + w * m + w)))
+    def scans(G, b, parts, mx="mx", mn="mn"):
+        lo = 0
+        for w in parts:
+            hi = lo + 16 * w
+            scan(A(mx + str(b), lo, hi), A("rm", 0, 16 * w), A(G, lo, hi), OP.add, OP.max)
+            scan(A(mn + str(b), lo, hi), A("rn", 0, 16 * w), A(G, lo, hi), OP.add, OP.min)
+            lo = hi
 
-    def fin(bank, bv, X, N, out):
-        n = out[2]
+    def fin(bank, b, early, at, late, out, mx="mx", mn="mn"):
+        n = NS[b]
         p = A(bank, 0, n)
-        mms(p, [(I, A("cq", 0, n)), (NEG, bv), (A("half"), A(X, 15, 16 * n, 16)), (A("half"), A(N, 15, 16 * n, 16)),
-                (I, A("cm", 0, n))])
+        mms(p, [(I, A("cq", 0, n))] + early + [(HALF, A(mx + str(b), at, 16 * n, 16)), (HALF, A(mn + str(b), at, 16 * n, 16))]
+            + late + [(I, A("cm", 0, n))])
         act(out, p, AF.Abs, A("mgc"))
 
-    for t in range(5):
-        last = t == 4
-        now[0] = t
-        for b, n in enumerate(NS):
-            label("gather", b)
-            gather("ga%d" % b, A("xw%d" % b), "eu%d" % t, U0[b], n, JUDGE_GATHER[b])
-        for b, n in enumerate(NS):
-            label("score", b)
-            s = str(b)
-            b0, b1, b2 = BANKS[b]
-            K = A(b0, 0, 128, 1, n)
-            mms(K, [(part("ct%d" % t, b), A("ict")), (A("one", 0, n), A("ik")), (A("one", 0, n), A("ig"))]
-                + [(A("xw" + s, *cls(t, b, XO)), A("wx%d" % m)) for m in ON_VECTOR[b]], True, False)
-            parts = len(JUDGE_GATHER[b])
-            w = 8 * n // parts
-            turn = 0
-            for p in range(parts):
-                xr = A("xr%d" % (t % 2), 8 * U0[b] + w * p, 8 * U0[b] + w * p + w)
-                if XBANKS[b]:
-                    xp = A(XBANKS[b][p], 0, w)
-                    mm(xp, I, xr, True, True)
-                for m in range(2):
-                    gm = A("ga" + s, 2 * w * p + m, 2 * w * p + 2 * w, 2)
-                    lo = 8 * n * m + w * p
-                    out = A("mt" + s, lo, lo + w)
-                    if FORM[b][m] == "x":
-                        tt(out, xp, gm, OP.max)
-                    elif FORM[b][m] == "d":
-                        tt(A("gb" + s, lo, lo + w), xp, gm, OP.subtract)
-                        act(out, A("gb" + s, lo, lo + w), AF.Abs)
-                    else:
-                        d = A(DBANKS[b][turn % len(DBANKS[b])], 0, w)
-                        turn += 1
-                        mms(d, [(NEG, xr), (I, gm)])
-                        act(out, d, AF.Abs)
-            for m in ON_VECTOR[b]:
-                for k in range(m, 16, 2):
-                    mm(A(b0, k, 128, 16, n), A("ga" + s, k, 16 * n, 16), A("wn16", 0, 128, 16), False, False)
-            for m in range(2):
-                for e in range(8):
-                    mm(A(b0, 2 * e + m, 128, 16, n), A("mt" + s, 8 * n * m + e, 8 * n * m + 8 * n, 8),
-                       A("w32" if m in ON_VECTOR[b] else "w16", 0, 128, 16), False, (m, e) == (1, 7))
-            label("least", b)
-            top = A("top", 0, 128, 1, n)
+    def score(t, b):
+        n, s, u = NS[b], str(b), str(t % 2)
+        b0 = BANKS[b][0]
+        mms(A(b0, 0, 128, 1, n), [(part("ct" + u, b), A("ict")), (A("one", 0, n), A("ik")), (A("one", 0, n), A("ig"))], True, False)
+        w = 8 * n // len(JUDGE[b])
+        turn = 0
+        for m in range(2):
+            for p, q in reversed(list(enumerate(JUDGE[b]))):
+                d = A("ga" + s, 2 * w * p + m, 2 * w * (p + 1), 2)
+                if q == "s":
+                    lo = 16 * U0[b] + 2 * w * p
+                    gm, d = d, A(DBANKS[b][turn], 0, w)
+                    turn += 1
+                    mms(d, [(NEG, A("xr" + u, lo + m, lo + 2 * w, 2)), (I, gm)])
+                act(A("mt" + s, 8 * n * m + w * p, 8 * n * m + w * (p + 1)), d, AF.Abs)
+            for e in range(8):
+                mm(A(b0, 2 * e + m, 128, 16, n), A("mt" + s, 8 * n * m + e, 8 * n * (m + 1), 8), A("w16", 0, 128, 16),
+                   False, (m, e) == (1, 7))
+
+    def trial(t, b):
+        n, s, u = NS[b], str(b), str(t % 2)
+        b0, b1, b2 = BANKS[b]
+        K, top = A(b0, 0, 128, 1, n), A("top", 0, 128, 1, n)
+        xs, bt = part("xs" + u, b), A("bt", *cls(t, b))
+        scan(A("r1" + s, 0, 128, 1, n), top, K, OP.max, OP.min)
+        scan(A("mb" + s, 0, 128, 1, n), top, A("r1" + s, 15, 143, 1, n), OP.max, OP.min)
+        ht = A("ht" + s, 0, 128, 1, n)
+        tt(ht, K, A("mb" + s, 0, 128, 1, n), OP.is_equal)
+        z = A("xw" + s, ZO, ZO + n)
+        if AGAIN[b]:
             E = A(b1, 0, n)
-            mm(E, A("idh"), part("eh%d" % t, b), True, False)
-            scan(A("r1" + s, 0, 128, 1, n), top, K, OP.max, OP.min)
-            scan(A("mb" + s, 0, 128, 1, n), top, A("r1" + s, 15, 143, 1, n), OP.max, OP.min)
-            ht = A("ht" + s, 0, 128, 1, n)
-            tt(ht, K, A("mb" + s, 0, 128, 1, n), OP.is_equal)
-            mm(E, ht, A("ixo", 0, n, 1, n), False, True)
+            mms(E, [(I, A("ek" + u, 2 * U0[b], 2 * U0[b] + n)), (ht, A("ixo", 0, n, 1, n))])
             mm(part(KEEP, b), ht, A("idn", 0, n, 1, n), True, True)
             ts(A("ou" + s, 0, n), E, 1024.0, None, OP.add)
-            gather("gb" + s, A("xw" + s), "ou" + s, 0, n, REGATHER[b])
-            scans("ga" + s, "m0" + s, "n0" + s, n, 3)
-            fin(b2, A("bt", *cls(t, b)), "m0" + s, "n0" + s, part("f0", b))
-            scans("gb" + s, "mx" + s, "mn" + s, n, len(REGATHER[b]))
-            z = A("xw" + s, ZO, ZO + n)
-            fin(b0, A("bt", *cls(t, b)), "mx" + s, "mn" + s, z)
-            mms(A(KEEP, NJ + U0[b], NJ + U0[b] + n), [(NEG, part("f0", b)), (I, z)])
-        if not last:
-            label("ahead")
-            repeat(t + 1)
-            act(A("f0g"), IND(A("f0"), A("sndl", 6 * t, 6 * t + 6)), AF.Copy)
-        for h in range(1, 4):
-            for b, n in enumerate(NS):
-                label("hop", h, b)
-                s = str(b)
-                b0, b1, b2 = BANKS[b]
-                z = A("xw" + s, ZO + n * (h - 1), ZO + n * h)
-                wl = A("wl" + s, 0, n // 16)
-                F = A(b1, 0, n)
-                mms(F, [(I, A("yc96", 0, n)), (A("b16"), z), (I, A("cm", 0, n)), (NEG, A("cm", 0, n)), (A("nb16"), z)])
-                if HOT[b] == "s":
-                    act(A("hot" + s), F, AF.Relu, A("p1c"), 16.0)
-                else:
-                    ts(A("hot" + s), F, A("p1c"), None, OP.is_equal)
-                for tab, out in (("uw", "pw"), ("uq", "pq")):
-                    tt(A(out + s), A(tab, *cls(t, b)) if h == 1 else IND(A(tab), wl), A("hot" + s), OP.mult)
-                W = A(b0, 0, n)
-                mms(W, [(I, A("mask", 0, n)), (A("blkf"), A("pw" + s))])
-                Q = A(b1, 0, n)
-                mms(Q, [(I, A("jc", 0, n)), (A("b8k"), A("pq" + s))])
-                act(A("aa" + s), Q, AF.Abs, A("bc" + s, h - 1, h))
-                scan(A("ll" + s), A("rx", 0, n), W, OP.mult, OP.max)
-                vcp(wl, A("ll" + s, 15, n, 16))
-                tt(A("of" + s), IND(A("entt"), wl), A("aa" + s), OP.min)
-                vcp(A("ou" + s, n * h, n * h + n), A("of" + s))
-                act(A("bw" + s), IND(A("bt"), wl), AF.Copy)
-                gather("gb" + s, A("xw" + s), "ou" + s, n * h, n, HOP_GATHER[b])
-                if h == 3:
-                    act(A("xv" + s), IND(A("xw" + s, XO, XG), wl), AF.Copy)
-                    ts(A("cl" + s), A("ou" + s, n, 4 * n), ZO - 1.0, XO - 1.0, OP.max, OP.min)
-                    cl = [A("cl" + s, n * i, n * i + n) for i in range(3)]
-                    mms(A(b1, 0, n), [(A("i8k"), A("ca" + s))] + [(A("nf8k"), c) for c in cl]
-                        + [(I, A("cm2", 0, n)), (NEG, A("cm2", 0, n))] + [(A("f8k"), c) for c in cl]
-                        + [(A("i8k"), A("cb" + s)), (A("nb1"), A("xv" + s))], True, False)
-                scans("gb" + s, "mx" + s, "mn" + s, n, len(HOP_GATHER[b]))
-                fin(b0, A("bw" + s), "mx" + s, "mn" + s,
-                    A("xw" + s, ZO + n * h, ZO + n * (h + 1)) if h < 3 else A("z3" + s))
-        for b, n in enumerate(NS):
-            label("effect", b)
-            s = str(b)
-            D = A(BANKS[b][1], 0, n)
-            tt(A("mz" + s), A("z3" + s), A("xv" + s), OP.max)
-            mms(D, [(A("nb1"), A("z3" + s)), (A("b2"), A("mz" + s))], False, True)
-            ts(part("st", b), D, A("thc", t, t + 1), None, OP.is_le)
-            tt(part("sd", b), A(KEEP, NJ + U0[b], NJ + U0[b] + n), part("st", b), OP.mult)
-        label("end")
-        if not last:
-            tt(A("gt%d" % t), IND(A("sd"), A("sndl", 6 * t, 6 * t + 6)), A("f0g"), OP.add)
-            send(t, A("gt%d" % t), A("land%d" % t))
-            tt(A("xw0", *cls(t, None, XO)), A("f0"), A("sd"), OP.add)
-            tt(A("hs"), A(KEEP, 0, NJ), A("st"), OP.mult)
-            for b in range(1, NB):
-                act(A("xw%d" % b, *cls(t, None, XO)), A("xw0", *cls(t, None, XO)), AF.Copy)
-            for bank, tab, by in (("p0", "entt", "ixo"), ("p1", "yef", "i1152")):
-                E = A(bank, 0, NJ)
-                mms(E, [(A("idf"), A(tab, *cls(t))), (A(by), A("hs"))])
-                act(A(tab, *cls(t)), E, AF.Copy)
-            C = A("p3", 0, NJ)
-            mm(C, A("one"), A("hs"), True, True)
-            rr = A("rr")
-            add("v", lambda e, rr=rr, C=C: e.tensor_reduce(out=rr[0], in_=C[0], axis=AX.X, op=OP.add), regs(C), regs(rr), vc(NJ))
-            vcp(A("rri"), A("rr"))
-            ts(A("rrj"), A("rri"), 31, None, OP.bitwise_and)
-            tt(A("thc", t + 1, t + 2), A("rrj"), A("tha", t + 1, t + 2), OP.add)
-            for b in range(NB):
-                copy("v" if b == 0 else "s", A("xw%d" % b, XG + 96 * t, XG + 96 * (t + 1)), A("land%d" % t))
-            if t == 0:
-                lists(4)
+            scans("ga" + s, b, FPARTS, "m0", "n0")
+            fin(b2, b, [(NEG, bt), (I, xs)], 15, [], part("f0", b), "m0", "n0")
+            gather("gb" + s, b, "ou" + s, 0, AGAIN[b])
+            scans("gb" + s, b, [w for _q, w in AGAIN[b]])
+            fin(b0, b, [(NEG, bt)], 15, [], z)
         else:
-            label("out")
-            for b, n in enumerate(NS):
-                E = A(BANKS[b][0], 0, n)
-                mm(E, A("idf"), A("yef", *cls(t, b)), True, False)
-                tt(A("xw0", *cls(t, b, XO)), part("f0", b), part("sd", b), OP.add)
-                tt(part("hs", b), part(KEEP, b), part("st", b), OP.mult)
-                mm(E, A("i1152"), part("hs", b), False, True)
-                act(A("yef", *cls(t, b)), E, AF.Copy)
-                cols = slice(4 * U0[b], 4 * (U0[b] + n))
-                xc = slice(XO + cols.start, XO + cols.stop)
-                add("y", lambda e, cols=cols, xc=xc: e.dma_start(out=T.yx[:, cols], in_=T.xw0[:, xc]),
-                    [("xw0", xc.start, xc.stop, 1)], [], (0.1, 0, False), 2.0, "o%d" % (NB + b), 16, True)
-                add("y", lambda e, cols=cols: e.dma_start(out=T.ye[:, cols], in_=T.yef[:, cols]),
-                    [("yef", cols.start, cols.stop, 1)], [], (0.1, 0, False), 2.0, "o%d" % b, 16, True)
+            act(A("t15" + s), A("ga" + s, 15, 16 * n, 16), AF.Copy)
+            H = A(b1, 0, 2 * n)
+            mm(H, ht, A("ii" + s, 0, 2 * n, 1, n), True, True)
+            mm(part(KEEP, b), ht, A("idn", 0, n, 1, n), True, True)
+            tt(A("dn" + s), H, part("ek" + u, b, 2), OP.mult)
+            W = A(b2, 0, 2 * n)
+            mms(W, [(I, A("mk" + s)), (A("blk"), A("dn" + s))])
+            scan(A("ll" + s), A("rx", 0, 2 * n), W, OP.mult, OP.max)
+            vcp(A("xl" + s, 0, n // 8), A("ll" + s, 15, 2 * n, 16))
+            xl, pl = A("xl" + s, 0, n // 16), A("xl" + s, n // 16, n // 8)
+            vcp(IND(A("ga" + s), pl), A("t15" + s))
+            tt(A("ga" + s, 15, 16 * n, 16), IND(A("xw" + s, ZO), xl), xs, OP.subtract)
+            act(A("gk" + s), IND(A("xw" + s, 0, XE), xl), AF.Copy)
+            scans("ga" + s, b, [n // 2] * 2)
+            fin(b0, b, [(NEG, bt), (I, xs)], 15, [], z)
+            mms(A(b2, 0, n), [(I, A("gk" + s)), (NEG, xs), (NEG, A("mx" + s, 14, 16 * n, 16))])
+            mms(A(b2, n, 2 * n), [(NEG, A("gk" + s)), (I, xs), (I, A("mn" + s, 14, 16 * n, 16))])
+            act(A("rl" + s), A(b2, 0, 2 * n), AF.Relu)
+            fin(b2, b, [(NEG, bt), (I, xs)], 14, [(HALF, A("rl" + s, 0, n)), (A("nhalf"), A("rl" + s, n, 2 * n))], part("f0", b))
+        mms(A(KEEP, NJ + U0[b], NJ + U0[b] + n), [(NEG, part("f0", b)), (I, z)])
 
-    _edges(ops)
+    def hop(t, h, b):
+        n, s = NS[b], str(b)
+        b0, b1, b2 = BANKS[b]
+        z = A("xw" + s, ZO + n * (h - 1), ZO + n * h)
+        wl = A("wl" + s, 0, n // 16)
+        cm = A("cm", 0, n)
+        F = A(b1, 0, n)
+        mms(F, [(I, A("yc96", 0, n)), (A("b16"), z), (I, cm), (NEG, cm), (A("nb16"), z),
+                (A("i256"), A("uq", *cls(t, b)) if h == 1 else A("qw" + s))])
+        act(A("hot" + s), F, AF.Relu, A("p1c"), 2.0 ** 18)
+        tt(A("pw" + s), A("uw", *cls(t, b)) if h == 1 else IND(A("uw"), wl), A("hot" + s), OP.min)
+        W = A(b0, 0, n)
+        mms(W, [(I, A("mask", 0, n)), (A("blk"), A("pw" + s))])
+        Q = A(b1, 0, n)
+        mms(Q, [(I, A("jc", 0, n)), (A("b8"), A("hot" + s))])
+        act(A("aa" + s), Q, AF.Abs, A("bc", h - 1, h))
+        scan(A("ll" + s, 0, n), A("rx", 0, n), W, OP.mult, OP.max)
+        vcp(wl, A("ll" + s, 15, n, 16))
+        tt(A("of" + s), IND(A("entt"), wl), A("aa" + s), OP.min)
+        vcp(A("ou" + s, n * (h - 1), n * h), A("of" + s))
+        act(A("bw" + s), IND(A("bt"), wl), AF.Copy)
+        gather("gb" + s, b, "ou" + s, n * (h - 1), HOP[h - 1][b])
+        scans("gb" + s, b, [w for _q, w in HOP[h - 1][b]])
+        fin(b0, b, [(NEG, A("bw" + s))], 15, [], A("xw" + s, ZO + n * h, ZO + n * (h + 1)) if h < 3 else A("z3" + s))
+        if h < 3:
+            act(A("qw" + s), IND(A("uq"), wl), AF.Copy)
+        else:
+            act(A("xv" + s), IND(A("xw" + s, XO, XG), wl), AF.Copy)
+            ts(A("cl" + s), A("ou" + s), ZO - 1.0, XO - 1.0, OP.max, OP.min)
+            cl = [A("cl" + s, n * i, n * i + n) for i in range(3)]
+            mms(A(b2, 0, n), [(A("i15"), A("one", 0, n)), (A("b1m"), part("ct%d" % (t % 2), b)), (I, A("cm3", 0, n)),
+                              (NEG, A("cm3", 0, n)), (A("i8k"), A("ca"))] + [(A("nf8k"), c) for c in cl]
+                + [(I, A("cm2", 0, n)), (NEG, A("cm2", 0, n))] + [(A("f8k"), c) for c in cl]
+                + [(A("i8k"), A("cb")), (A("nb1"), A("xv" + s))], True, False)
+
+    def effect(t, b):
+        n, s = NS[b], str(b)
+        D = A(BANKS[b][2], 0, n)
+        tt(A("mz" + s), A("z3" + s), A("xv" + s), OP.max)
+        mms(D, [(A("nb1"), A("z3" + s)), (A("b2"), A("mz" + s))], False, True)
+        ts(part("st", b), D, A("thc", t, t + 1), None, OP.is_le)
+        tt(part("sd", b), A(KEEP, NJ + U0[b], NJ + U0[b] + n), part("st", b), OP.mult)
+
+    def close(t):
+        tt(A("gt%d" % t), IND(A("sd"), A("sndl", 6 * t, 6 * t + 6)), A("f0g"), OP.add)
+        send(t, A("gt%d" % t), A("land%d" % t))
+        tt(A("xw0", *cls(t, None, XO)), A("f0"), A("sd"), OP.add)
+        tt(A("hs"), A(KEEP, 0, NJ), A("st"), OP.mult)
+        act(A("xw1", *cls(t, None, XO)), A("xw0", *cls(t, None, XO)), AF.Copy)
+        for bank, tab, by in (("p4", "entt", "ixo"), ("p5", "yef", "i1152")):
+            E = A(bank, 0, NJ)
+            mms(E, [(A("idf"), A(tab, *cls(t))), (A(by), A("hs"))])
+            act(A(tab, *cls(t)), E, AF.Copy)
+        C, rr = A("p2", 0, NJ), A("rr")
+        mm(C, A("one"), A("hs"), True, True)
+        add("v", lambda e: e.tensor_reduce(out=rr[0], in_=C[0], axis=AX.X, op=OP.add), regs(C), regs(rr), vc(NJ))
+        vcp(A("rri"), rr)
+        ts(A("rrj"), A("rri"), 31, None, OP.bitwise_and)
+        tt(A("thc", t + 1, t + 2), A("rrj"), A("tha", t + 1, t + 2), OP.add)
+        for b in range(NB):
+            copy("v" if b == 0 else "s", A("xw%d" % b, XG + 96 * t, XG + 96 * (t + 1)), A("land%d" % t))
+
+    def store(t, b):
+        n = NS[b]
+        E = A(BANKS[b][0], 0, n)
+        mm(E, A("idf"), A("yef", *cls(t, b)), True, False)
+        tt(A("xw0", *cls(t, b, XO)), part("f0", b), part("sd", b), OP.add)
+        tt(part("hs", b), part(KEEP, b), part("st", b), OP.mult)
+        mm(E, A("i1152"), part("hs", b), False, True)
+        act(A("yef", *cls(t, b)), E, AF.Copy)
+        cols = slice(4 * U0[b], 4 * (U0[b] + n))
+        xc = slice(XO + cols.start, XO + cols.stop)
+        add("y", lambda e: e.dma_start(out=T.yx[:, cols], in_=T.xw0[:, xc]),
+            [("xw0", xc.start, xc.stop, 1)], [], (0.1, 0, False), 2.0, "o%d" % (NB + b), 16, True)
+        add("y", lambda e: e.dma_start(out=T.ye[:, cols], in_=T.yef[:, cols]),
+            [("yef", cols.start, cols.stop, 1)], [], (0.1, 0, False), 2.0, "o%d" % b, 16, True)
+
+    def rounds(which):
+        for t in which:
+            u = str(t % 2)
+            for b, n in enumerate(NS):
+                label("gather", b)
+                w = n // len(JUDGE[b])
+                for p, q in enumerate(JUDGE[b]):
+                    lo = U0[b] + w * p
+                    out, src = A("ga%d" % b, 16 * w * p, 16 * w * (p + 1)), IND(A("xw%d" % b, 0, XE), A("eu" + u, lo, lo + w))
+                    if q == "s":
+                        act(out, src, AF.Copy)
+                    else:
+                        tt(out, src, A("xr" + u, 16 * lo, 16 * (lo + w)), OP.subtract)
+            for b in range(NB):
+                label("score", b)
+                score(t, b)
+                label("least", b)
+                trial(t, b)
+            if t < 4:
+                label("ahead")
+                repeat(t + 1, "g")
+                lists(t + 1)
+                act(A("f0g"), IND(A("f0"), A("sndl", 6 * t, 6 * t + 6)), AF.Copy)
+            for h in range(1, 4):
+                for b in range(NB):
+                    label("hop", h, b)
+                    hop(t, h, b)
+            for b in range(NB):
+                label("effect", b)
+                effect(t, b)
+            if t < 4:
+                label("end")
+                close(t)
+            else:
+                label("out")
+                for b in range(NB):
+                    store(t, b)
+
     if "order" not in PLAN:
-        PLAN["order"] = _plan(ops)
+        some = []
+        for which in ((0,), (0, 1, 4)):
+            rounds(which)
+            some.append([dict(o) for o in ops])
+            del ops[setup:]
+        rounds(range(5))
+        PLAN["order"] = _plan(some[0], some[1], ops)
+    else:
+        rounds(range(5))
+        _edges(ops)
     needed = [False] * len(ops)
     for o in ops:
         for j in o["pre"]:
             needed[j] = needed[j] or o["pre"][j]
     know = {}
     count = {}
-    remotes = 0
     for i in PLAN["order"]:
         o = ops[i]
         q = o["q"]
@@ -757,16 +773,13 @@ def rank_program(g, core, T, topo):
                         kq[a] = max(kq.get(a, 0), ops[j2]["snap"][a])
         ins = o["fn"](eng[q])
         o["snap"] = dict(kq)
-        if o["remote"]:
-            remotes += 1
-            continue
         if o["sem"] or needed[i]:
             sm = o["sem"] or QS[q]
             count[sm] = count.get(sm, 0) + o["amount"]
-            ins.then_inc(T.sem[sm], o["amount"])
+            if not o["remote"]:
+                ins.then_inc(T.sem[sm], o["amount"])
             o["done"] = (sm, count[sm])
             if not o["sem"]:
                 o["snap"][sm] = count[sm]
     for sm in sorted(count):
         g.wait_ge(T.sem[sm], count[sm])
-    g.wait_ge(T.sem.loc, remotes * len(es))

@@ -8,9 +8,11 @@ U0 = [sum(NS[:b]) for b in range(len(NS))]
 NB, NM = len(NS), max(NS)
 JUDGE = ["sv", "vv"]
 PARTS = [("v", 12), ("s", 44), ("s", 40)]
+SCANS = [56, 40]
 HOP = [[PARTS, PARTS]] * 3
-AGAIN = [[("s", 48), ("s", 48)], None]
+AGAIN = [None, [("s", 48), ("s", 48)]]
 FPARTS = [48, 48]
+START = "vsvgvs"
 BANKS = [("p0", "p1", "p2"), ("p3", "p4", "p5")]
 DBANKS = [("p1", "p7"), ()]
 KEEP = "p6"
@@ -39,11 +41,10 @@ for _b, _w in enumerate(NS):
     _buf("xw%d" % _b, XE if AGAIN[_b] else XE + ZO)
     for _n in ("ga", "gb", "mt", "mx", "mn", "m0", "n0"):
         _buf("%s%d" % (_n, _b), 16 * _w)
-    for _n in ("hot", "qw", "bw", "xv", "z3", "mz", "t15", "gk"):
+    for _n in ("pq", "bw", "xv", "z3", "mz", "t15", "gk"):
         _buf("%s%d" % (_n, _b), _w)
-    for _n in ("rl", "mk", "ii"):
-        _buf("%s%d" % (_n, _b), 2 * _w)
-    for _n, _k in (("pw", 1), ("dn", 2), ("cl", 3)):
+    _buf("rl%d" % _b, 2 * _w)
+    for _n, _k in (("hot", 1), ("ww", 1), ("dn", 2), ("cl", 3)):
         _buf("%s%d" % (_n, _b), _k * _w, "float16")
     for _n, _k in (("aa", _w), ("of", _w), ("ll", 2 * _w), ("r1", 144), ("mb", 128)):
         _buf("%s%d" % (_n, _b), _k, "float32")
@@ -55,33 +56,33 @@ for _n in range(2):
     _buf("ct%d" % _n, NJ)
     _buf("xs%d" % _n, NJ)
     _buf("ek%d" % _n, 2 * NJ, "float16")
+    _buf("w1%d" % _n, NJ, "float16")
     _buf("xr%d" % _n, 16 * NJ)
 for _n in ("f0", "st", "sd", "hs"):
     _buf(_n, NJ)
-for _n in ("enti", "usri", "uw", "uqi"):
+for _n in ("enti", "usri", "uq"):
     _buf(_n, V, "int32")
-for _n in ("entt", "yef"):
+for _n in ("entt", "yef", "uw"):
     _buf(_n, V, "float32")
-for _n, _w in (("bt", V), ("uq", V), ("lt", V), ("rx", 2 * NM), ("rm", 8 * NM), ("rn", 8 * NM), ("f0g", 96)):
+for _n, _w in (("bt", V), ("lt", V), ("rx", 2 * NM), ("rm", 16 * max(SCANS)), ("rn", 16 * max(SCANS)), ("f0g", 96)):
     _buf(_n, _w)
 _buf("sndi", 24, "int32", "sbuf", 128, False)
 _buf("sndu", 24, "uint16")
 _buf("sndl", 24, "uint16")
 _buf("thi", 5, "int32", "sbuf", 8)
 _buf("thf", 5, "float32", "sbuf", 8)
-for _n, _w in (("tha", 5), ("thc", 5), ("rr", 1), ("pf", 4), ("bk", 4), ("py", 1), ("p1c", 1), ("mgc", 1), ("c256", 1), ("cz", 1), ("pg", 1),
+for _n, _w in (("tha", 5), ("thc", 5), ("rr", 1), ("pf", 4), ("bk", 4), ("py", 1), ("p1c", 1), ("mgc", 1), ("c256", 1), ("cw", 1), ("n1k", 1), ("cz", 1), ("pg", 1),
                ("top", 128), ("idf", 128)):
     _buf(_n, _w, "float32")
 for _n, _w in (("rri", 1), ("rrj", 1), ("ji", NM), ("jj", NM), ("pi", 4), ("pj", 4), ("pk", 1)):
     _buf(_n, _w, "int32")
-for _n, _w, _d in (("ca", NM, "float16"), ("cb", NM, "float16"), ("bc", 4, "float32"), ("bi", 4, "int32")):
+for _n, _w, _d in (("ca", NM, "float16"), ("cb", NM, "float16"), ("bc", 4, "float32"), ("bi", 4, "float32"), ("mk", 2 * NM, BF2)):
     _buf(_n, _w, _d)
 _buf("gs0", NG, BF2, "sbuf", 128, False)
 for _n in range(4):
     _buf("gt%d" % _n, 96, BF2, "sbuf", 128, False)
-    _buf("land%d" % _n, 96, BF2, "sbuf", 128, False)
-for _n in ("one", "idn", "half", "nhalf", "neg", "ict", "ik", "ig", "ixo", "ixe", "i1152", "i15", "blkh", "blk", "b16", "nb16",
-           "nb1", "b2", "b8", "i256", "w16", "b1m", "i8k", "f8k", "nf8k"):
+for _n in ("one", "zero", "i1k", "idn", "half", "nhalf", "neg", "ict", "ik", "ig", "ixo", "ixe", "i1152", "i15", "blkh", "blk", "b16", "nb16",
+           "nb1", "b2", "i32k", "w16", "b1m", "i8k", "f8k", "nf8k"):
     _buf(_n, 128)
 for _n in ("oe", "ee0", "ee"):
     _buf(_n, 128, "float32", "sbuf", 8)
@@ -91,8 +92,11 @@ for _n in range(8):
     _buf("p%d" % _n, 512, "float32", "psum")
 LOADS = ["snd", "xa", "ent", "yc", "bn", "usr", "th", "x1", "y1", "y2"]
 SEMAPHORES = (["sv", "ss", "st", "sg"] + ["o%d" % n for n in range(2 * NB)] + ["ld_" + n for n in LOADS]
-              + ["arr%d" % t for t in range(5)] + ["left%d" % t for t in range(5)])
+              + ["arr%d" % t for t in range(5)] + ["left%d" % t for t in range(5)]
+              + ["free%d" % t for t in range(4)] + ["told%d" % t for t in range(4)])
 QS = {"v": "sv", "s": "ss", "t": "st", "g": "sg"}
+HURRY = dict([(_n, 2.0) for _n in ("pi", "idn", "blk", "neg", "ict", "ik", "ig", "w16", "top", "r10", "r11")]
+             + [(_n, 1.0) for _n in ("rm", "rn", "rx", "mk", "mgc", "cq", "cm", "half", "ixo")])
 PLAN = {}
 
 
@@ -135,8 +139,8 @@ def _cost(o, m):
 
 
 MODELS = [(1.0, 0.87, 1.4, 0.13, 0.6), (1.2, 1.15, 1.8, 0.12, 1.1)]
-STEPS = 11000
-SEED, HEAT, LEAD = 8, 0.005, (0.5, 1.3, 2.1, 3.0)
+STEPS = 10000
+SEED, HEAT, LEAD = 10, 0.005, (0.5, 1.3, 2.1, 3.0)
 
 
 def _planner(calls):
@@ -235,7 +239,7 @@ def _planner(calls):
     return ops, key, schedule, length
 
 
-def _plan(start, few, calls):
+def _plan(few, calls):
     ops, key, schedule, length = _planner(few)
     n, keys = len(ops), 1 + max(o["key"] for o in calls)
     batch = [0] * keys
@@ -249,9 +253,12 @@ def _plan(start, few, calls):
     rng = np.random.RandomState(SEED)
     unit = []
 
-    def judge(c):
+    def judge(c, most=None):
         made = schedule(*c)
-        res = [length(made[0], m) for m in range(len(MODELS))]
+        res = [length(made[0], 0)]
+        if most and res[0][0] / unit[0] > most:
+            return None
+        res += [length(made[0], m) for m in range(1, len(MODELS))]
         if not unit:
             unit.extend(r[0] for r in res)
         return sum(r[0] / u for r, u in zip(res, unit)), c, made, res
@@ -285,22 +292,23 @@ def _plan(start, few, calls):
                 c[0][k], c[1][k] = cur[1][0][k], cur[1][1][k]
             if c == cur[1]:
                 continue
-            new = judge(c)
-            if new[0] <= cur[0] - heat * (1 - step / steps) * math.log(rng.rand()):
+            bar = cur[0] - heat * (1 - step / steps) * math.log(rng.rand())
+            new = judge(c, bar - cur[0] + cur[3][0][0] / unit[0] + 0.004)
+            if new and new[0] <= bar:
                 cur = new
                 if cur[0] < best[0]:
                     best = cur
         return best
 
-    field = [judge(([-lead * b for b in batch], [0.1] * keys)) for lead in LEAD]
+    hurry = [0.0] * keys
+    for o in calls:
+        hurry[o["key"]] = o["hurry"]
+    field = [judge(([h - lead * b for b, h in zip(batch, hurry)], [0.4 if h > 7 else 0.1 for h in hurry])) for lead in LEAD]
     while len(field) > 1:
         field = [climb(c, STEPS // (3 * len(field)), HEAT, 0.7, once) for c in field]
         field = sorted(field, key=lambda c: c[0])[:len(field) // 2]
     best = climb(field[0], STEPS // 6, HEAT / 2, 0.3, once)
-    ops, key, schedule, length = _planner(start)
-    n = len(ops)
-    del unit[:]
-    best = climb(judge(best[1]), STEPS // 2, HEAT / 2, 0.0, set(range(keys)) - once)
+    best = climb(best, STEPS // 6, HEAT / 5, 0.0)
     del unit[:]
     ops, key, schedule, length = _planner(calls)
     n = len(ops)
@@ -315,6 +323,7 @@ def rank_program(g, core, T, topo):
     ops = []
     names = {}
     step = [None, 0]
+    hurry = [0.0]
     eng = {"v": g.vector, "s": g.scalar, "t": g.tensor, "g": g, "y": g.sync}
 
     def label(*x):
@@ -323,7 +332,7 @@ def rank_program(g, core, T, topo):
     def add(q, fn, rd, wr, cost, lag=0.0, sem=None, amount=1, dma=False, after=()):
         key = names.setdefault((step[0], step[1]), len(names))
         step[1] += 1
-        ops.append({"q": q, "fn": fn, "key": key, "once": step[0] is None, "kin": (step[0] and step[0][::2], step[1]),
+        ops.append({"q": q, "fn": fn, "key": key, "once": step[0] is None, "hurry": HURRY.get(wr[0][0] if wr else None, hurry[0]) if step[0] is None else 0.0, "kin": (step[0] and step[0][::2], step[1]),
                     "batch": step[0][-1] if step[0] and len(step[0]) > 1 else 0, "rd": rd, "wr": wr,
                     "cost": cost, "lag": lag, "sem": sem, "amount": amount, "dma": dma, "after": list(after), "remote": False})
         return len(ops) - 1
@@ -397,8 +406,8 @@ def rank_program(g, core, T, topo):
         for i, (l, r) in enumerate(pairs):
             mm(out, l, r, start and i == 0, stop and i == len(pairs) - 1)
 
-    def sel(out, a, pattern, op, base, cm):
-        return add("g", lambda e: e.affine_select(out=out[0], in_=a[0], pattern=pattern, compare_op=op, fill=0.0, base=base,
+    def sel(out, a, pattern, op, base, cm, other=0.0):
+        return add("g", lambda e: e.affine_select(out=out[0], in_=a[0], pattern=pattern, compare_op=op, fill=other, base=base,
                                                  channel_multiplier=cm), regs(a), regs(out), (0.17, 2 * out[2], False))
 
     def copy(q, out, a):
@@ -420,13 +429,22 @@ def rank_program(g, core, T, topo):
     dst = T.cores[(rank - 1) % len(T.cores)]
     src = T.cores[(rank + 1) % len(T.cores)]
     rid, pid = topo.addr(dst, core)
-    es = topo.engines(core, dst)[:8]
-    mask = sum(1 << e for e in es)
-    n_in = len(topo.engines(src, core)[:8])
+    es = topo.engines(core, dst)
+    mask = topo.mask(core, dst)
+    n_in = len(topo.engines(src, core))
 
-    def send(slot, a, land):
+    back, bid = topo.addr(src, core)
+    one_engine = 1 << topo.engines(core, src)[0]
+
+    def free(slot, land):
+        j = add("g", lambda e: e.remote_sem_update(T.sem["free%d" % slot], T.sem["told%d" % slot], bid, back, one_engine),
+                [], regs(land), (0.3, 0, False), 1.0, "told%d" % slot, 1)
+        ops[j]["remote"] = True
+        return add("z", None, [], [], (0.0, 0, False), 1.0, "free%d" % slot, 1, True, (j,))
+
+    def send(slot, a, land, after=()):
         j = add("g", lambda e: e.remote_dma(land[0], a[0], T.sem["arr%d" % slot], T.sem["left%d" % slot], pid, rid, mask),
-                regs(a), [], (0.3, 0, False), 1.0, "left%d" % slot, len(es))
+                regs(a), [], (0.3, 0, False), 1.0, "left%d" % slot, len(es), False, after)
         ops[j]["remote"] = True
         add("x", None, [], regs(land), (0.0, 0, False), 1.5, "arr%d" % slot, n_in, True, (j,))
         return j
@@ -440,21 +458,24 @@ def rank_program(g, core, T, topo):
 
     own0 = A("xw0", XO, XG)
     load("y", "snd", A("sndi"), 1.5)
-    load("s", "xa", own0, 2.0)
+    xa = load("s", "xa", own0, 2.0)
     load("y", "ent", A("enti"), 3.0)
-    load("s", "yc", A("xw0", 0, ZO), 3.5)
+    load("y", "yc", A("xw0", 0, ZO), 2.0, None, (xa,))
+    hurry[0] = 8.0
     for c in range(4):
         ts(A("sndu", 6 * c, 6 * c + 6), A("sndi", 6 * c, 6 * c + 6), 4, c, OP.mult, OP.add)
     act(A("gs0"), IND(own0, A("sndu")), AF.Copy)
     first = send(4, A("gs0"), A("xw0", XG, XE))
+    hurry[0] = 0.0
     vcp(A("sndl"), A("sndi"))
-    for i, (name, out, sem) in enumerate((("xa", A("xw1", XO, XG), "ld_x1"), ("yc", A("xw1", 0, ZO), "ld_y1"), ("bn", A("bt"), None),
-                                          ("yc", A("xw1", XE, XE + ZO), "ld_y2"), ("usr", A("usri"), None), ("th", A("thi"), None))):
-        load("y", name, out, 2.0 + 0.8 * i, sem, (first,))
-    sel(A("xw1", ZO, XO), A("xw0", XO, XO + GAP), [[0, GAP]], OP.is_gt, 0, 0)
-
     fill(A("one"), 1.0)
-    fill(A("oe"), 1.0)
+    twice = "xw%d" % AGAIN.index(None)
+    for i, (name, out, sem) in enumerate((("xa", A("xw1", XO, XG), "ld_x1"), ("yc", A("xw1", 0, ZO), "ld_y1"), ("bn", A("bt"), None),
+                                          ("yc", A(twice, XE, XE + ZO), "ld_y2"), ("usr", A("usri"), None), ("th", A("thi"), None))):
+        load("y", name, out, 2.0 + 0.8 * i, sem, (first,))
+    fill(A(twice, ZO, XO), 0.0)
+
+    iota(A("oe"), [[0, 128]], 1, 0)
     sel(A("idn"), A("one"), [[-1, 128]], OP.is_equal, 0, 1)
     sel(A("blkh"), A("one"), [[-16, 8], [0, 16]], OP.is_ge, 0, 1)
     sel(A("blk"), A("blkh"), [[16, 8], [0, 16]], OP.is_ge, 15, -1)
@@ -463,54 +484,60 @@ def rank_program(g, core, T, topo):
     iota(A("ji"), [[1, NM]], 128, -1)
     iota(A("jc"), [[1, NM]], 0, 0)
     iota(A("pi"), [[0, 4]], 0, 1)
-    fill(A("top"), 0.0)
+    act(A("top"), A("one"), AF.Identity, None, 0.0)
     ts(A("top", 0, 128, 16), A("jc", 0, 8), 131072.0, 131071.0, OP.mult, OP.add)
     ts(A("pj"), A("pi"), 15, None, OP.bitwise_and)
     vcp(A("pf"), A("pj"))
     ts(A("pk"), A("pi", 0, 1), 112, None, OP.bitwise_and)
-    ts(A("pg"), A("pk"), 8192.0, None, OP.mult)
-    for name, of, x in (("half", "idn", 0.5), ("nhalf", "idn", -0.5), ("neg", "idn", -1.0), ("ict", "idn", 65536.0),
-                        ("i1152", "idn", 1152.0), ("ixo", "idn", -float(XO)), ("ixe", "idn", -XE / 2), ("idf", "idn", 1.0),
-                        ("ik", "idn", A("pf", 0, 1)), ("ig", "idn", A("pg")), ("i15", "idn", -15.0 * 2 ** 19),
-                        ("b16", "blk", 0.0625), ("nb16", "blk", -0.0625), ("nb1", "blk", -1.0), ("b2", "blk", 2.0),
-                        ("b8", "blk", 8.0), ("i256", "idn", 1.0 / 256), ("w16", "blk", 16.0), ("b1m", "blk", 2.0 ** 20),
-                        ("i8k", "idn", 8192.0), ("f8k", "blk", 8192.0), ("nf8k", "blk", -8192.0)):
+    ts(A("pg"), A("pk"), 8192.0, 32768.0, OP.mult, OP.add)
+    for name, of, x in (("neg", "idn", -1.0), ("ict", "idn", -32768.0), ("ixe", "idn", -XE / 2), ("idf", "idn", 1.0),
+                        ("ik", "idn", A("pf", 0, 1)), ("ig", "idn", A("pg")), ("w16", "blk", 16.0)):
         act(A(name), A(of), AF.Identity, None, x)
+    iota(A("zero"), [[0, 128]], 0, 0)
+    for name, x in (("i1k", 1024.0), ("half", 0.5), ("nhalf", -0.5), ("i1152", 1152.0), ("ixo", -float(XO)), ("i15", 2.0 ** 19),
+                    ("i32k", 2.0 ** -15), ("i8k", 8192.0)):
+        sel(A(name), A("zero"), [[-1, 128]], OP.not_equal, 0, 1, x)
+    for name, x in (("b16", 0.0625), ("nb16", -0.0625), ("nb1", -1.0), ("b2", 2.0), ("b1m", -2.0 ** 19), ("f8k", 8192.0),
+                    ("nf8k", -8192.0)):
+        sel(A(name), A("zero"), [[16, 8], [0, 16]], OP.is_gt, 0, -1, x)
+        sel(A(name), A(name), [[16, 8], [0, 16]], OP.is_ge, 15, -1)
     ts(A("py"), A("pf", 0, 1), -0.0625, -15.0 / 32, OP.mult, OP.add)
-    ts(A("p1c"), A("pf", 0, 1), 16384.0, 1024.0, OP.mult, OP.add)
-    ts(A("bk"), A("pf"), -8192.0, -8192.0, OP.mult, OP.add)
+    act(A("p1c"), A("pf", 0, 1), AF.Identity, None, 2048.0)
+    act(A("bk", 0, 1), A("pf", 0, 1), AF.Identity, None, -8192.0)
     ts(A("jj"), A("ji"), 15, None, OP.bitwise_and)
     ts(A("mask"), A("jj"), 0, -4096.0, OP.not_equal, OP.mult)
-    act(A("j16"), A("jc"), AF.Identity, None, 16.0)
+    iota(A("j16"), [[16, NM]], 0, 0)
     iota(A("bi"), [[NM, 4]], ZO, 0)
-    tt(A("bc"), A("bk"), A("bi"), OP.add)
+    act(A("bc"), A("bi"), AF.Identity, A("bk", 0, 1))
     c0 = (48 * (ZO - 1) + 3 * NM + 3) % GAP
     ts(A("ca"), A("jc"), 3.0, c0 - (GAP - 1) / 2, OP.mult, OP.add)
     ts(A("cb"), A("jc"), -3.0, -float(c0), OP.mult, OP.add)
     for b, n in enumerate(NS):
         s = str(b)
-        act(A("r1" + s, 128, 144), A("one", 0, 16), AF.Identity, None, 1048576.0)
+        iota(A("r1" + s, 128, 144), [[0, 16]], 1048576, 0)
         if not AGAIN[b]:
-            ts(A("mk" + s, 0, n), A("mask", 0, n), 1024.0, None, OP.add)
-            tt(A("mk" + s, n, 2 * n), A("mask", 0, n), A("j16", 0, n), OP.add)
             for i in range(2):
-                act(A("ii" + s, n * i, n * i + n), A("idn", 0, n), AF.Copy)
-                ts(A("ek%d" % i, 2 * U0[b] + n, 2 * U0[b] + 2 * n), A("one", 0, n), A("pf", 0, 1), None, OP.mult)
+                act(A("ek%d" % i, 2 * U0[b] + n, 2 * U0[b] + 2 * n), A("one", 0, n), AF.Identity, None, A("pf", 0, 1))
+    mms(A("p6", 0, NM), [(A("idn"), A("mask")), (A("i1k"), A("one", 0, NM))])
+    mms(A("p6", NM, 2 * NM), [(A("idn"), A("mask")), (A("idn"), A("j16"))])
+    act(A("mk"), A("p6", 0, 2 * NM), AF.Copy)
     act(A("yc96"), A("one", 0, NM), AF.Identity, None, A("py"))
-    for name, x in (("cm", MAGIC), ("cm2", MAGIC * 8192 * GAP), ("cm3", MAGIC * 2 ** 24), ("cq", -0.25), ("mgc", -MAGIC)):
-        act(A(name), A("one", 0, WHERE[name][2]), AF.Identity, None, x)
-    for name, x in (("c256", 256.0), ("cz", 0.5 - ZO)):
-        fill(A(name), x)
-    for name, x, y in (("rx", 1.0, 0.0), ("rm", 0.0, -512.0), ("rn", 0.0, 512.0)):
-        fill(A(name), x)
-        fill(A(name, 0, WHERE[name][2], 16), y)
+    for name, x in (("cm", MAGIC), ("cm2", MAGIC * 8192 * GAP), ("cm3", MAGIC * 2 ** 24), ("cq", -0.25)):
+        sel(A(name), A("one", 0, NM), [[0, NM]], OP.is_gt, 0, 0, x)
+    for name, x in (("c256", 256.0), ("cz", 0.5 - ZO), ("mgc", -MAGIC), ("n1k", -1024.0), ("cw", 1024 - 15.0 / 32)):
+        act(A(name), A("one", 0, 1), AF.Identity, None, x)
+    for lo in (0, NM):
+        sel(A("rx", lo, lo + NM), A("one", 0, NM), [[0, NM // 16], [1, 16]], OP.is_gt, 0, 0)
+    for name, x in (("rm", -512.0), ("rn", 512.0)):
+        fill(A(name), 0.0)
+        act(A(name, 0, WHERE[name][2], 16), A("one", 0, WHERE[name][2] // 16), AF.Identity, None, x)
     I, NEG, HALF = A("idn"), A("neg"), A("half")
 
     def lists(t):
         vcp(A("eu%d" % (t % 2)), A("entt", *cls(t)))
-        ts(A("ct%d" % (t % 2)), A("eu%d" % (t % 2)), float(ZO), None, OP.is_lt)
+        act(A("ct%d" % (t % 2)), A("entt", *cls(t)), AF.Sign, A("cz"))
         for b, n in enumerate(NS):
-            ts(A("ek%d" % (t % 2), 2 * U0[b], 2 * U0[b] + n), part("eu%d" % (t % 2), b), -1024.0, None, OP.add)
+            act(A("ek%d" % (t % 2), 2 * U0[b], 2 * U0[b] + n), A("entt", *cls(t, b)), AF.Identity, A("n1k"))
 
     def repeat(t, queues):
         for r in range(16):
@@ -520,21 +547,24 @@ def rank_program(g, core, T, topo):
             sel(part("xs%d" % (t % 2), b), A("xw0", *cls(t, b, XO)), [[1, n]], OP.is_ge, -w * JUDGE[b].count("s"), 0)
 
     for c in range(4):
+        hurry[0] = 3.0 * (c == 0)
         vcp(A("yef", *cls(c)), A("enti", *cls(c)))
         act(A("lt", NJ * c, NJ * c + NJ), A("yef", *cls(c)), AF.Sign, A("cz"))
         E = A(("p2", "p4", "p5", "p2")[c], 0, NJ)
         mms(E, [(A("idf"), A("yef", *cls(c))), (A("ixe"), A("lt", NJ * c, NJ * c + NJ))])
         act(A("entt", *cls(c)), E, AF.Identity, A("c256"))
+    hurry[0] = 3.0
     lists(0)
-    ts(A("uw"), A("usri"), 4, None, OP.logical_shift_right)
-    ts(A("uqi"), A("usri"), 15, None, OP.bitwise_and)
-    vcp(A("uq"), A("uqi"))
+    repeat(0, START)
+    hurry[0] = 0.0
+    ts(A("uw"), A("usri"), 0.0625, None, OP.mult)
+    ts(A("uq"), A("usri"), 15, None, OP.bitwise_and)
+    act(A("w10"), A("uw", *cls(0)), AF.Identity, A("cw"))
     vcp(A("thf"), A("thi"))
     mm(A("p5", 0, 5), A("ee"), A("thf"), True, True)
     act(A("tha"), A("p5", 0, 5), AF.Copy)
     act(A("thc", 0, 1), A("tha", 0, 1), AF.Copy)
-    act(A("xw1", XG, XE), A("xw0", XG, XE), AF.Copy)
-    repeat(0, "vsvgvs")
+    copy("g", A("xw1", XG, XE), A("xw0", XG, XE))
     setup = len(ops)
 
     def gather(out, b, off, first, parts):
@@ -590,7 +620,7 @@ def rank_program(g, core, T, topo):
         if AGAIN[b]:
             E = A(b1, 0, n)
             mms(E, [(I, A("ek" + u, 2 * U0[b], 2 * U0[b] + n)), (ht, A("ixo", 0, n, 1, n))])
-            mm(part(KEEP, b), ht, A("idn", 0, n, 1, n), True, True)
+            mm(part(KEEP, b), ht, A("idn" if t < 4 else "i1152", 0, n, 1, n), True, True)
             ts(A("ou" + s, 0, n), E, 1024.0, None, OP.add)
             scans("ga" + s, b, FPARTS, "m0", "n0")
             fin(b2, b, [(NEG, bt), (I, xs)], 15, [], part("f0", b), "m0", "n0")
@@ -600,11 +630,12 @@ def rank_program(g, core, T, topo):
         else:
             act(A("t15" + s), A("ga" + s, 15, 16 * n, 16), AF.Copy)
             H = A(b1, 0, 2 * n)
-            mm(H, ht, A("ii" + s, 0, 2 * n, 1, n), True, True)
-            mm(part(KEEP, b), ht, A("idn", 0, n, 1, n), True, True)
+            for lo in (0, n):
+                mm(A(b1, lo, lo + n), ht, A("idn", 0, n, 1, n), True, True)
+            mm(part(KEEP, b), ht, A("idn" if t < 4 else "i1152", 0, n, 1, n), True, True)
             tt(A("dn" + s), H, part("ek" + u, b, 2), OP.mult)
             W = A(b2, 0, 2 * n)
-            mms(W, [(I, A("mk" + s)), (A("blk"), A("dn" + s))])
+            mms(W, [(I, A("mk")), (A("blk"), A("dn" + s))])
             scan(A("ll" + s), A("rx", 0, 2 * n), W, OP.mult, OP.max)
             vcp(A("xl" + s, 0, n // 8), A("ll" + s, 15, 2 * n, 16))
             xl, pl = A("xl" + s, 0, n // 16), A("xl" + s, n // 16, n // 8)
@@ -627,24 +658,24 @@ def rank_program(g, core, T, topo):
         cm = A("cm", 0, n)
         F = A(b1, 0, n)
         mms(F, [(I, A("yc96", 0, n)), (A("b16"), z), (I, cm), (NEG, cm), (A("nb16"), z),
-                (A("i256"), A("uq", *cls(t, b)) if h == 1 else A("qw" + s))])
-        act(A("hot" + s), F, AF.Relu, A("p1c"), 2.0 ** 18)
-        tt(A("pw" + s), A("uw", *cls(t, b)) if h == 1 else IND(A("uw"), wl), A("hot" + s), OP.min)
+                (A("i32k"), part("w1%d" % (t % 2), b) if h == 1 else A("ww" + s))])
+        act(A("hot" + s), F, AF.Relu, A("p1c"), 2.0 ** 15)
         W = A(b0, 0, n)
-        mms(W, [(I, A("mask", 0, n)), (A("blk"), A("pw" + s))])
+        mms(W, [(I, A("mask", 0, n)), (A("blk"), A("hot" + s))])
+        tt(A("pq" + s), A("uq", *cls(t, b)) if h == 1 else IND(A("uq"), wl), A("hot" + s), OP.min)
         Q = A(b1, 0, n)
-        mms(Q, [(I, A("jc", 0, n)), (A("b8"), A("hot" + s))])
+        mms(Q, [(I, A("jc", 0, n)), (A("f8k"), A("pq" + s))])
         act(A("aa" + s), Q, AF.Abs, A("bc", h - 1, h))
         scan(A("ll" + s, 0, n), A("rx", 0, n), W, OP.mult, OP.max)
-        vcp(wl, A("ll" + s, 15, n, 16))
+        ts(wl, A("ll" + s, 15, n, 16), -1024.0, None, OP.add)
         tt(A("of" + s), IND(A("entt"), wl), A("aa" + s), OP.min)
         vcp(A("ou" + s, n * (h - 1), n * h), A("of" + s))
         act(A("bw" + s), IND(A("bt"), wl), AF.Copy)
         gather("gb" + s, b, "ou" + s, n * (h - 1), HOP[h - 1][b])
-        scans("gb" + s, b, [w for _q, w in HOP[h - 1][b]])
+        scans("gb" + s, b, SCANS)
         fin(b0, b, [(NEG, A("bw" + s))], 15, [], A("xw" + s, ZO + n * h, ZO + n * (h + 1)) if h < 3 else A("z3" + s))
         if h < 3:
-            act(A("qw" + s), IND(A("uq"), wl), AF.Copy)
+            act(A("ww" + s), IND(A("uw"), wl), AF.Identity, A("cw"))
         else:
             act(A("xv" + s), IND(A("xw" + s, XO, XG), wl), AF.Copy)
             ts(A("cl" + s), A("ou" + s), ZO - 1.0, XO - 1.0, OP.max, OP.min)
@@ -664,7 +695,8 @@ def rank_program(g, core, T, topo):
 
     def close(t):
         tt(A("gt%d" % t), IND(A("sd"), A("sndl", 6 * t, 6 * t + 6)), A("f0g"), OP.add)
-        send(t, A("gt%d" % t), A("land%d" % t))
+        ghosts = [A("xw%d" % b, XG + 96 * t, XG + 96 * (t + 1)) for b in range(NB)]
+        send(t, A("gt%d" % t), ghosts[0], (free(t, ghosts[0]),))
         tt(A("xw0", *cls(t, None, XO)), A("f0"), A("sd"), OP.add)
         tt(A("hs"), A(KEEP, 0, NJ), A("st"), OP.mult)
         act(A("xw1", *cls(t, None, XO)), A("xw0", *cls(t, None, XO)), AF.Copy)
@@ -678,20 +710,16 @@ def rank_program(g, core, T, topo):
         vcp(A("rri"), rr)
         ts(A("rrj"), A("rri"), 31, None, OP.bitwise_and)
         tt(A("thc", t + 1, t + 2), A("rrj"), A("tha", t + 1, t + 2), OP.add)
-        for b in range(NB):
-            copy("v" if b == 0 else "s", A("xw%d" % b, XG + 96 * t, XG + 96 * (t + 1)), A("land%d" % t))
+        copy("g", ghosts[1], ghosts[0])
 
     def store(t, b):
         n = NS[b]
-        E = A(BANKS[b][0], 0, n)
-        mm(E, A("idf"), A("yef", *cls(t, b)), True, False)
-        tt(A("xw0", *cls(t, b, XO)), part("f0", b), part("sd", b), OP.add)
         tt(part("hs", b), part(KEEP, b), part("st", b), OP.mult)
-        mm(E, A("i1152"), part("hs", b), False, True)
-        act(A("yef", *cls(t, b)), E, AF.Copy)
+        tt(A("yef", *cls(t, b)), A("yef", *cls(t, b)), part("hs", b), OP.add)
+        tt(A("xw0", *cls(t, b, XO)), part("f0", b), part("sd", b), OP.add)
         cols = slice(4 * U0[b], 4 * (U0[b] + n))
         xc = slice(XO + cols.start, XO + cols.stop)
-        add("y", lambda e: e.dma_start(out=T.yx[:, cols], in_=T.xw0[:, xc]),
+        add("s", lambda e: e.dma_start(out=T.yx[:, cols], in_=T.xw0[:, xc]),
             [("xw0", xc.start, xc.stop, 1)], [], (0.1, 0, False), 2.0, "o%d" % (NB + b), 16, True)
         add("y", lambda e: e.dma_start(out=T.ye[:, cols], in_=T.yef[:, cols]),
             [("yef", cols.start, cols.stop, 1)], [], (0.1, 0, False), 2.0, "o%d" % b, 16, True)
@@ -718,6 +746,7 @@ def rank_program(g, core, T, topo):
                 label("ahead")
                 repeat(t + 1, "g")
                 lists(t + 1)
+                act(A("w1%d" % ((t + 1) % 2)), A("uw", *cls(t + 1)), AF.Identity, A("cw"))
                 act(A("f0g"), IND(A("f0"), A("sndl", 6 * t, 6 * t + 6)), AF.Copy)
             for h in range(1, 4):
                 for b in range(NB):
@@ -735,13 +764,11 @@ def rank_program(g, core, T, topo):
                     store(t, b)
 
     if "order" not in PLAN:
-        some = []
-        for which in ((0,), (0, 1, 4)):
-            rounds(which)
-            some.append([dict(o) for o in ops])
-            del ops[setup:]
+        rounds((0, 1, 4))
+        few = [dict(o) for o in ops]
+        del ops[setup:]
         rounds(range(5))
-        PLAN["order"] = _plan(some[0], some[1], ops)
+        PLAN["order"] = _plan(few, ops)
     else:
         rounds(range(5))
         _edges(ops)
@@ -754,7 +781,7 @@ def rank_program(g, core, T, topo):
     for i in PLAN["order"]:
         o = ops[i]
         q = o["q"]
-        if q == "x":
+        if q in "xz":
             count[o["sem"]] = o["amount"]
             o["done"] = (o["sem"], o["amount"])
             o["snap"] = {}

@@ -1,5 +1,6 @@
 import math
 import numpy as np
+from concourse.bass import DstId, RemoteDMATransfer
 from concourse.mybir import AluOpType as OP, ActivationFunctionType as AF, AxisListType as AX
 
 V, NG, NJ = 768, 384, 192
@@ -7,20 +8,23 @@ NS = [96, 96]
 U0 = [sum(NS[:b]) for b in range(len(NS))]
 NB, NM = len(NS), max(NS)
 JUDGE = ["sv", "vv"]
-PARTS = [("v", 12), ("s", 44), ("s", 40)]
-SCANS = [56, 40]
+PARTS = [("v", 20), ("s", 40), ("s", 36)]
+SCANS = [60, 36]
 HOP = [[PARTS, PARTS]] * 3
 AGAIN = [None, [("s", 48), ("s", 48)]]
 FPARTS = [48, 48]
+FIRST = 2.0
+LATE = ("i1152", "i15", "i8k", "nb1", "b2", "b1m", "nf8k", "nhalf")
 START = "vsvgvs"
 BANKS = [("p0", "p1", "p2"), ("p3", "p4", "p5")]
-DBANKS = [("p1", "p7"), ()]
-KEEP = "p6"
+DBANKS = [("p1", "p2"), ()]
+KEEP, LIST = "p6", "p7"
 ZO, XO = 1152, 1664
 XG = XO + V
 XE = XG + NG
 GAP = XO - ZO
 MAGIC = 12582912.0
+WO = 1040.0
 BF2 = "bfloat16"
 SCRATCH = {}
 WHERE = {}
@@ -41,15 +45,15 @@ for _b, _w in enumerate(NS):
     _buf("xw%d" % _b, XE if AGAIN[_b] else XE + ZO)
     for _n in ("ga", "gb", "mt", "mx", "mn", "m0", "n0"):
         _buf("%s%d" % (_n, _b), 16 * _w)
-    for _n in ("pq", "bw", "xv", "z3", "mz", "t15", "gk"):
+    for _n in ("pq", "xv", "z3", "mz", "t15", "gk"):
         _buf("%s%d" % (_n, _b), _w)
     _buf("rl%d" % _b, 2 * _w)
-    for _n, _k in (("hot", 1), ("ww", 1), ("dn", 2), ("cl", 3)):
+    for _n, _k in (("hot", 1), ("ww", 1), ("bw", 1), ("dn", 2), ("cl", 3)):
         _buf("%s%d" % (_n, _b), _k * _w, "float16")
     for _n, _k in (("aa", _w), ("of", _w), ("ll", 2 * _w), ("r1", 144), ("mb", 128)):
         _buf("%s%d" % (_n, _b), _k, "float32")
     _buf("ht%d" % _b, 128)
-    for _n, _k in (("ou", 3 * _w), ("wl", 8), ("xl", 16)):
+    for _n, _k in (("ou", 3 * _w), ("wl", 24), ("xl", 16)):
         _buf("%s%d" % (_n, _b), _k, "uint16")
 for _n in range(2):
     _buf("eu%d" % _n, NJ, "uint16")
@@ -58,20 +62,20 @@ for _n in range(2):
     _buf("ek%d" % _n, 2 * NJ, "float16")
     _buf("w1%d" % _n, NJ, "float16")
     _buf("xr%d" % _n, 16 * NJ)
-for _n in ("f0", "st", "sd", "hs"):
+for _n in ("f0", "st", "sd", "hs", "df"):
     _buf(_n, NJ)
 for _n in ("enti", "usri", "uq"):
     _buf(_n, V, "int32")
 for _n in ("entt", "yef", "uw"):
     _buf(_n, V, "float32")
-for _n, _w in (("bt", V), ("lt", V), ("rx", 2 * NM), ("rm", 16 * max(SCANS)), ("rn", 16 * max(SCANS)), ("f0g", 96)):
+for _n, _w in (("bt", V), ("lt", V), ("rx", 2 * NM), ("rm", 16 * max(SCANS + FPARTS)), ("rn", 16 * max(SCANS + FPARTS)), ("dg", 96)):
     _buf(_n, _w)
 _buf("sndi", 24, "int32", "sbuf", 128, False)
 _buf("sndu", 24, "uint16")
 _buf("sndl", 24, "uint16")
 _buf("thi", 5, "int32", "sbuf", 8)
 _buf("thf", 5, "float32", "sbuf", 8)
-for _n, _w in (("tha", 5), ("thc", 5), ("rr", 1), ("pf", 4), ("bk", 4), ("py", 1), ("p1c", 1), ("mgc", 1), ("c256", 1), ("cw", 1), ("n1k", 1), ("cz", 1), ("pg", 1),
+for _n, _w in (("tha", 5), ("thc", 5), ("rr", 1), ("pf", 4), ("bk", 4), ("py", 1), ("p1c", 1), ("c1k", 1), ("c25", 1), ("mgc", 1), ("c256", 1), ("cw", 1), ("n1k", 1), ("cz", 1), ("pg", 1),
                ("top", 128), ("idf", 128)):
     _buf(_n, _w, "float32")
 for _n, _w in (("rri", 1), ("rrj", 1), ("ji", NM), ("jj", NM), ("pi", 4), ("pj", 4), ("pk", 1)):
@@ -79,6 +83,7 @@ for _n, _w in (("rri", 1), ("rrj", 1), ("ji", NM), ("jj", NM), ("pi", 4), ("pj",
 for _n, _w, _d in (("ca", NM, "float16"), ("cb", NM, "float16"), ("bc", 4, "float32"), ("bi", 4, "float32"), ("mk", 2 * NM, BF2)):
     _buf(_n, _w, _d)
 _buf("gs0", NG, BF2, "sbuf", 128, False)
+_buf("f0g", 96, BF2, "sbuf", 128, False)
 for _n in range(4):
     _buf("gt%d" % _n, 96, BF2, "sbuf", 128, False)
 for _n in ("one", "zero", "i1k", "idn", "half", "nhalf", "neg", "ict", "ik", "ig", "ixo", "ixe", "i1152", "i15", "blkh", "blk", "b16", "nb16",
@@ -86,17 +91,19 @@ for _n in ("one", "zero", "i1k", "idn", "half", "nhalf", "neg", "ict", "ik", "ig
     _buf(_n, 128)
 for _n in ("oe", "ee0", "ee"):
     _buf(_n, 128, "float32", "sbuf", 8)
-for _n in ("yc96", "jc", "j16", "mask", "cm", "cq", "cm2", "cm3"):
+for _n in ("yc96", "jc", "j16", "mask", "mq", "cm", "cq", "cm2", "cm3"):
     _buf(_n, NM)
 for _n in range(8):
     _buf("p%d" % _n, 512, "float32", "psum")
-LOADS = ["snd", "xa", "ent", "yc", "bn", "usr", "th", "x1", "y1", "y2"]
+SCRATCH[LIST] = ("psum", [128, 32, 16], "float32")
+LOADS = ["snd", "xa", "ent", "yc", "bn", "usr", "th"]
 SEMAPHORES = (["sv", "ss", "st", "sg"] + ["o%d" % n for n in range(2 * NB)] + ["ld_" + n for n in LOADS]
               + ["arr%d" % t for t in range(5)] + ["left%d" % t for t in range(5)]
               + ["free%d" % t for t in range(4)] + ["told%d" % t for t in range(4)])
 QS = {"v": "sv", "s": "ss", "t": "st", "g": "sg"}
 HURRY = dict([(_n, 2.0) for _n in ("pi", "idn", "blk", "neg", "ict", "ik", "ig", "w16", "top", "r10", "r11")]
-             + [(_n, 1.0) for _n in ("rm", "rn", "rx", "mk", "mgc", "cq", "cm", "half", "ixo")])
+             + [(_n, 1.0) for _n in ("rm", "rn", "rx", "mk", "mgc", "cq", "half", "ixo")]
+             + [(_n, 4.0) for _n in ("uw", "cm", "bt", "usri")])
 PLAN = {}
 
 
@@ -135,12 +142,14 @@ def _edges(ops):
 
 def _cost(o, m):
     f, n, gath = o["cost"]
+    if o["q"] == "t":
+        return m[5] * (0.02 * m[0] + n * 1e-3 * m[1])
     return f * m[0] + max(64, n * m[2] * gath if gath else n) * 1.0e-3 * m[1] if n else f
 
 
-MODELS = [(1.0, 0.87, 1.4, 0.13, 0.6), (1.2, 1.15, 1.8, 0.12, 1.1)]
-STEPS = 10000
-SEED, HEAT, LEAD = 10, 0.005, (0.5, 1.3, 2.1, 3.0)
+MODELS = [(1.0, 0.87, 1.4, 0.13, 0.6, 1.05), (1.45, 1.2, 2.0, 0.18, 1.3, 0.6)]
+STEPS = 3000
+SEED, HEAT, LEAD = 3, 0.005, (0.5, 1.3, 2.1, 3.0)
 
 
 def _planner(calls):
@@ -388,6 +397,12 @@ def rank_program(g, core, T, topo):
         return add("v", lambda e: e.tensor_tensor_scan(out=out[0], data0=d0[0], data1=d1[0], initial=0.0, op0=op0, op1=op1),
                    regs(d0, d1), regs(out), vc(out[2] * half(out, d0, d1)))
 
+    def sixteens(lo, n):
+        return (T[LIST][:, lo // 16:(lo + n) // 16, :], [(LIST, lo, lo + n, 1)], n, False)
+
+    def greatest(out, a):
+        return add("v", lambda e: e.tensor_reduce(out=out[0], in_=a[0], axis=AX.X, op=OP.max), regs(a), regs(out), vc(a[2]))
+
     def fill(out, x):
         return add("v", lambda e: e.memset(out[0], x), [], regs(out), vc(out[2] * half(out)))
 
@@ -442,11 +457,16 @@ def rank_program(g, core, T, topo):
         ops[j]["remote"] = True
         return add("z", None, [], [], (0.0, 0, False), 1.0, "free%d" % slot, 1, True, (j,))
 
-    def send(slot, a, land, after=()):
-        j = add("g", lambda e: e.remote_dma(land[0], a[0], T.sem["arr%d" % slot], T.sem["left%d" % slot], pid, rid, mask),
-                regs(a), [], (0.3, 0, False), 1.0, "left%d" % slot, len(es), False, after)
+    def send(slot, parts, land, after=()):
+        def call(e):
+            if len(parts) == 1:
+                return e.remote_dma(land[0], parts[0][0], T.sem["arr%d" % slot], T.sem["left%d" % slot], pid, rid, mask)
+            move = RemoteDMATransfer(dst_ids=[DstId(rid=rid, pnc=pid)], dma_engine_mask=mask, remote_sem=T.sem["arr%d" % slot],
+                                     srcs=[a[0] for a in parts], dsts=[land[0]], alu_op=1)
+            return e.remote_dma_fused([move], local_sem=T.sem["left%d" % slot])
+        j = add("g", call, regs(*parts), [], (0.3, 0, False), 1.0, "left%d" % slot, len(es), False, after)
         ops[j]["remote"] = True
-        add("x", None, [], regs(land), (0.0, 0, False), 1.5, "arr%d" % slot, n_in, True, (j,))
+        add("x", None, [], regs(land), (0.0, 0, False), 1.5 + FIRST * (slot == 4), "arr%d" % slot, n_in, True, (j,))
         return j
 
     def cls(t, b=None, base=0):
@@ -465,14 +485,18 @@ def rank_program(g, core, T, topo):
     for c in range(4):
         ts(A("sndu", 6 * c, 6 * c + 6), A("sndi", 6 * c, 6 * c + 6), 4, c, OP.mult, OP.add)
     act(A("gs0"), IND(own0, A("sndu")), AF.Copy)
-    first = send(4, A("gs0"), A("xw0", XG, XE))
+    first = send(4, [A("gs0")], A("xw0", XG, XE))
     hurry[0] = 0.0
     vcp(A("sndl"), A("sndi"))
     fill(A("one"), 1.0)
     twice = "xw%d" % AGAIN.index(None)
-    for i, (name, out, sem) in enumerate((("xa", A("xw1", XO, XG), "ld_x1"), ("yc", A("xw1", 0, ZO), "ld_y1"), ("bn", A("bt"), None),
-                                          ("yc", A(twice, XE, XE + ZO), "ld_y2"), ("usr", A("usri"), None), ("th", A("thi"), None))):
-        load("y", name, out, 2.0 + 0.8 * i, sem, (first,))
+    for name, out, lag in (("usr", A("usri"), 2.5), ("bn", A("bt"), 3.2), ("th", A("thi"), 3.3)):
+        load("y", name, out, lag, None, (first,))
+    hurry[0] = 2.0
+    vcp(A("xw1", XO, XG), own0)
+    vcp(A("xw1", 0, ZO), A("xw0", 0, ZO))
+    hurry[0] = 0.0
+    vcp(A(twice, XE, XE + ZO), A("xw0", 0, ZO))
     fill(A(twice, ZO, XO), 0.0)
 
     iota(A("oe"), [[0, 128]], 1, 0)
@@ -496,14 +520,20 @@ def rank_program(g, core, T, topo):
     iota(A("zero"), [[0, 128]], 0, 0)
     for name, x in (("i1k", 1024.0), ("half", 0.5), ("nhalf", -0.5), ("i1152", 1152.0), ("ixo", -float(XO)), ("i15", 2.0 ** 19),
                     ("i32k", 2.0 ** -15), ("i8k", 8192.0)):
-        sel(A(name), A("zero"), [[-1, 128]], OP.not_equal, 0, 1, x)
+        if name in LATE:
+            sel(A(name), A("zero"), [[-1, 128]], OP.not_equal, 0, 1, x)
+        else:
+            ts(A(name), A("idn"), x, None, OP.mult)
     for name, x in (("b16", 0.0625), ("nb16", -0.0625), ("nb1", -1.0), ("b2", 2.0), ("b1m", -2.0 ** 19), ("f8k", 8192.0),
                     ("nf8k", -8192.0)):
-        sel(A(name), A("zero"), [[16, 8], [0, 16]], OP.is_gt, 0, -1, x)
-        sel(A(name), A(name), [[16, 8], [0, 16]], OP.is_ge, 15, -1)
+        if name in LATE:
+            sel(A(name), A("zero"), [[16, 8], [0, 16]], OP.is_gt, 0, -1, x)
+            sel(A(name), A(name), [[16, 8], [0, 16]], OP.is_ge, 15, -1)
+        else:
+            ts(A(name), A("blk"), x, None, OP.mult)
     ts(A("py"), A("pf", 0, 1), -0.0625, -15.0 / 32, OP.mult, OP.add)
     act(A("p1c"), A("pf", 0, 1), AF.Identity, None, 2048.0)
-    act(A("bk", 0, 1), A("pf", 0, 1), AF.Identity, None, -8192.0)
+    ts(A("bk", 0, 1), A("pf", 0, 1), -8192.0, None, OP.mult)
     ts(A("jj"), A("ji"), 15, None, OP.bitwise_and)
     ts(A("mask"), A("jj"), 0, -4096.0, OP.not_equal, OP.mult)
     iota(A("j16"), [[16, NM]], 0, 0)
@@ -521,10 +551,12 @@ def rank_program(g, core, T, topo):
     mms(A("p6", 0, NM), [(A("idn"), A("mask")), (A("i1k"), A("one", 0, NM))])
     mms(A("p6", NM, 2 * NM), [(A("idn"), A("mask")), (A("idn"), A("j16"))])
     act(A("mk"), A("p6", 0, 2 * NM), AF.Copy)
+    ts(A("mq"), A("mask"), -WO, None, OP.add)
     act(A("yc96"), A("one", 0, NM), AF.Identity, None, A("py"))
     for name, x in (("cm", MAGIC), ("cm2", MAGIC * 8192 * GAP), ("cm3", MAGIC * 2 ** 24), ("cq", -0.25)):
         sel(A(name), A("one", 0, NM), [[0, NM]], OP.is_gt, 0, 0, x)
-    for name, x in (("c256", 256.0), ("cz", 0.5 - ZO), ("mgc", -MAGIC), ("n1k", -1024.0), ("cw", 1024 - 15.0 / 32)):
+    for name, x in (("c256", 256.0), ("cz", 0.5 - ZO), ("mgc", -MAGIC), ("n1k", -1024.0), ("cw", WO - 15.0 / 32),
+                    ("c1k", 1024.0), ("c25", 0.25)):
         act(A(name), A("one", 0, 1), AF.Identity, None, x)
     for lo in (0, NM):
         sel(A("rx", lo, lo + NM), A("one", 0, NM), [[0, NM // 16], [1, 16]], OP.is_gt, 0, 0)
@@ -534,7 +566,7 @@ def rank_program(g, core, T, topo):
     I, NEG, HALF = A("idn"), A("neg"), A("half")
 
     def lists(t):
-        vcp(A("eu%d" % (t % 2)), A("entt", *cls(t)))
+        copy("g" if t else "v", A("eu%d" % (t % 2)), A("entt", *cls(t)))
         act(A("ct%d" % (t % 2)), A("entt", *cls(t)), AF.Sign, A("cz"))
         for b, n in enumerate(NS):
             act(A("ek%d" % (t % 2), 2 * U0[b], 2 * U0[b] + n), A("entt", *cls(t, b)), AF.Identity, A("n1k"))
@@ -550,16 +582,16 @@ def rank_program(g, core, T, topo):
         hurry[0] = 3.0 * (c == 0)
         vcp(A("yef", *cls(c)), A("enti", *cls(c)))
         act(A("lt", NJ * c, NJ * c + NJ), A("yef", *cls(c)), AF.Sign, A("cz"))
-        E = A(("p2", "p4", "p5", "p2")[c], 0, NJ)
+        E = A(("p2", "p4", "p6", "p2")[c], 0, NJ)
         mms(E, [(A("idf"), A("yef", *cls(c))), (A("ixe"), A("lt", NJ * c, NJ * c + NJ))])
         act(A("entt", *cls(c)), E, AF.Identity, A("c256"))
     hurry[0] = 3.0
     lists(0)
     repeat(0, START)
     hurry[0] = 0.0
-    ts(A("uw"), A("usri"), 0.0625, None, OP.mult)
+    copy("g", A("uw"), A("usri"))
     ts(A("uq"), A("usri"), 15, None, OP.bitwise_and)
-    act(A("w10"), A("uw", *cls(0)), AF.Identity, A("cw"))
+    act(A("w10"), A("uw", *cls(0)), AF.Identity, A("cw"), 0.0625)
     vcp(A("thf"), A("thi"))
     mm(A("p5", 0, 5), A("ee"), A("thf"), True, True)
     act(A("tha"), A("p5", 0, 5), AF.Copy)
@@ -584,7 +616,7 @@ def rank_program(g, core, T, topo):
     def fin(bank, b, early, at, late, out, mx="mx", mn="mn"):
         n = NS[b]
         p = A(bank, 0, n)
-        mms(p, [(I, A("cq", 0, n))] + early + [(HALF, A(mx + str(b), at, 16 * n, 16)), (HALF, A(mn + str(b), at, 16 * n, 16))]
+        mms(p, early + [(HALF, A(mx + str(b), at, 16 * n, 16)), (HALF, A(mn + str(b), at, 16 * n, 16))]
             + late + [(I, A("cm", 0, n))])
         act(out, p, AF.Abs, A("mgc"))
 
@@ -592,6 +624,13 @@ def rank_program(g, core, T, topo):
         n, s, u = NS[b], str(b), str(t % 2)
         b0 = BANKS[b][0]
         mms(A(b0, 0, 128, 1, n), [(part("ct" + u, b), A("ict")), (A("one", 0, n), A("ik")), (A("one", 0, n), A("ig"))], True, False)
+        if "s" not in JUDGE[b]:
+            for m in range(4):
+                act(A("mt" + s, 4 * n * m, 4 * n * (m + 1)), A("ga" + s, m, 16 * n, 4), AF.Abs)
+                for e in range(4):
+                    mm(A(b0, 4 * e + m, 128, 16, n), A("mt" + s, 4 * n * m + e, 4 * n * (m + 1), 4), A("w16", 0, 128, 16),
+                       False, (m, e) == (3, 3))
+            return
         w = 8 * n // len(JUDGE[b])
         turn = 0
         for m in range(2):
@@ -611,7 +650,8 @@ def rank_program(g, core, T, topo):
         n, s, u = NS[b], str(b), str(t % 2)
         b0, b1, b2 = BANKS[b]
         K, top = A(b0, 0, 128, 1, n), A("top", 0, 128, 1, n)
-        xs, bt = part("xs" + u, b), A("bt", *cls(t, b))
+        xs = part("xs" + u, b)
+        less = [(NEG, A("bt", *cls(t, b))), (I, A("cq", 0, n))]
         scan(A("r1" + s, 0, 128, 1, n), top, K, OP.max, OP.min)
         scan(A("mb" + s, 0, 128, 1, n), top, A("r1" + s, 15, 143, 1, n), OP.max, OP.min)
         ht = A("ht" + s, 0, 128, 1, n)
@@ -621,61 +661,58 @@ def rank_program(g, core, T, topo):
             E = A(b1, 0, n)
             mms(E, [(I, A("ek" + u, 2 * U0[b], 2 * U0[b] + n)), (ht, A("ixo", 0, n, 1, n))])
             mm(part(KEEP, b), ht, A("idn" if t < 4 else "i1152", 0, n, 1, n), True, True)
-            ts(A("ou" + s, 0, n), E, 1024.0, None, OP.add)
+            act(A("ou" + s, 0, n), E, AF.Relu, A("c1k"))
             scans("ga" + s, b, FPARTS, "m0", "n0")
-            fin(b2, b, [(NEG, bt), (I, xs)], 15, [], part("f0", b), "m0", "n0")
+            fin(b2, b, less + [(I, xs)], 15, [], part("f0", b), "m0", "n0")
             gather("gb" + s, b, "ou" + s, 0, AGAIN[b])
             scans("gb" + s, b, [w for _q, w in AGAIN[b]])
-            fin(b0, b, [(NEG, bt)], 15, [], z)
+            fin(b0, b, less, 15, [], z)
         else:
-            act(A("t15" + s), A("ga" + s, 15, 16 * n, 16), AF.Copy)
+            copy("g", A("t15" + s), A("ga" + s, 15, 16 * n, 16))
             H = A(b1, 0, 2 * n)
             for lo in (0, n):
                 mm(A(b1, lo, lo + n), ht, A("idn", 0, n, 1, n), True, True)
             mm(part(KEEP, b), ht, A("idn" if t < 4 else "i1152", 0, n, 1, n), True, True)
             tt(A("dn" + s), H, part("ek" + u, b, 2), OP.mult)
-            W = A(b2, 0, 2 * n)
+            W = sixteens(256, 2 * n)
             mms(W, [(I, A("mk")), (A("blk"), A("dn" + s))])
-            scan(A("ll" + s), A("rx", 0, 2 * n), W, OP.mult, OP.max)
-            vcp(A("xl" + s, 0, n // 8), A("ll" + s, 15, 2 * n, 16))
+            greatest(A("xl" + s, 0, n // 8), W)
             xl, pl = A("xl" + s, 0, n // 16), A("xl" + s, n // 16, n // 8)
             vcp(IND(A("ga" + s), pl), A("t15" + s))
             tt(A("ga" + s, 15, 16 * n, 16), IND(A("xw" + s, ZO), xl), xs, OP.subtract)
             act(A("gk" + s), IND(A("xw" + s, 0, XE), xl), AF.Copy)
             scans("ga" + s, b, [n // 2] * 2)
-            fin(b0, b, [(NEG, bt), (I, xs)], 15, [], z)
+            fin(b0, b, less + [(I, xs)], 15, [], z)
             mms(A(b2, 0, n), [(I, A("gk" + s)), (NEG, xs), (NEG, A("mx" + s, 14, 16 * n, 16))])
             mms(A(b2, n, 2 * n), [(NEG, A("gk" + s)), (I, xs), (I, A("mn" + s, 14, 16 * n, 16))])
             act(A("rl" + s), A(b2, 0, 2 * n), AF.Relu)
-            fin(b2, b, [(NEG, bt), (I, xs)], 14, [(HALF, A("rl" + s, 0, n)), (A("nhalf"), A("rl" + s, n, 2 * n))], part("f0", b))
+            fin(b2, b, less + [(I, xs)], 14, [(HALF, A("rl" + s, 0, n)), (A("nhalf"), A("rl" + s, n, 2 * n))], part("f0", b))
         mms(A(KEEP, NJ + U0[b], NJ + U0[b] + n), [(NEG, part("f0", b)), (I, z)])
 
     def hop(t, h, b):
         n, s = NS[b], str(b)
         b0, b1, b2 = BANKS[b]
         z = A("xw" + s, ZO + n * (h - 1), ZO + n * h)
-        wl = A("wl" + s, 0, n // 16)
+        was, wl = [A("wl" + s, 8 * i, 8 * i + n // 16) for i in ((h - 2) % 3, h - 1)]
         cm = A("cm", 0, n)
         F = A(b1, 0, n)
         mms(F, [(I, A("yc96", 0, n)), (A("b16"), z), (I, cm), (NEG, cm), (A("nb16"), z),
                 (A("i32k"), part("w1%d" % (t % 2), b) if h == 1 else A("ww" + s))])
         act(A("hot" + s), F, AF.Relu, A("p1c"), 2.0 ** 15)
-        W = A(b0, 0, n)
-        mms(W, [(I, A("mask", 0, n)), (A("blk"), A("hot" + s))])
-        tt(A("pq" + s), A("uq", *cls(t, b)) if h == 1 else IND(A("uq"), wl), A("hot" + s), OP.min)
+        W = sixteens(128 * b, n)
+        mms(W, [(I, A("mq", 0, n)), (A("blk"), A("hot" + s))])
+        tt(A("pq" + s), A("uq", *cls(t, b)) if h == 1 else IND(A("uq"), was), A("hot" + s), OP.min)
         Q = A(b1, 0, n)
         mms(Q, [(I, A("jc", 0, n)), (A("f8k"), A("pq" + s))])
         act(A("aa" + s), Q, AF.Abs, A("bc", h - 1, h))
-        scan(A("ll" + s, 0, n), A("rx", 0, n), W, OP.mult, OP.max)
-        ts(wl, A("ll" + s, 15, n, 16), -1024.0, None, OP.add)
-        tt(A("of" + s), IND(A("entt"), wl), A("aa" + s), OP.min)
-        vcp(A("ou" + s, n * (h - 1), n * h), A("of" + s))
-        act(A("bw" + s), IND(A("bt"), wl), AF.Copy)
+        greatest(wl, W)
+        tt(A("ou" + s, n * (h - 1), n * h), IND(A("entt"), wl), A("aa" + s), OP.min)
+        act(A("bw" + s), IND(A("bt"), wl), AF.Identity, A("c25"))
         gather("gb" + s, b, "ou" + s, n * (h - 1), HOP[h - 1][b])
         scans("gb" + s, b, SCANS)
         fin(b0, b, [(NEG, A("bw" + s))], 15, [], A("xw" + s, ZO + n * h, ZO + n * (h + 1)) if h < 3 else A("z3" + s))
         if h < 3:
-            act(A("ww" + s), IND(A("uw"), wl), AF.Identity, A("cw"))
+            act(A("ww" + s), IND(A("uw"), wl), AF.Identity, A("cw"), 0.0625)
         else:
             act(A("xv" + s), IND(A("xw" + s, XO, XG), wl), AF.Copy)
             ts(A("cl" + s), A("ou" + s), ZO - 1.0, XO - 1.0, OP.max, OP.min)
@@ -688,7 +725,9 @@ def rank_program(g, core, T, topo):
     def effect(t, b):
         n, s = NS[b], str(b)
         D = A(BANKS[b][2], 0, n)
-        tt(A("mz" + s), A("z3" + s), A("xv" + s), OP.max)
+        X = A(BANKS[b][1], 0, n)
+        mm(X, I, A("xv" + s), True, True)
+        tt(A("mz" + s), X, A("z3" + s), OP.max)
         mms(D, [(A("nb1"), A("z3" + s)), (A("b2"), A("mz" + s))], False, True)
         ts(part("st", b), D, A("thc", t, t + 1), None, OP.is_le)
         tt(part("sd", b), A(KEEP, NJ + U0[b], NJ + U0[b] + n), part("st", b), OP.mult)
@@ -696,7 +735,7 @@ def rank_program(g, core, T, topo):
     def close(t):
         tt(A("gt%d" % t), IND(A("sd"), A("sndl", 6 * t, 6 * t + 6)), A("f0g"), OP.add)
         ghosts = [A("xw%d" % b, XG + 96 * t, XG + 96 * (t + 1)) for b in range(NB)]
-        send(t, A("gt%d" % t), ghosts[0], (free(t, ghosts[0]),))
+        send(t, [A("gt%d" % t)], ghosts[0], (free(t, ghosts[0]),))
         tt(A("xw0", *cls(t, None, XO)), A("f0"), A("sd"), OP.add)
         tt(A("hs"), A(KEEP, 0, NJ), A("st"), OP.mult)
         act(A("xw1", *cls(t, None, XO)), A("xw0", *cls(t, None, XO)), AF.Copy)
@@ -746,7 +785,7 @@ def rank_program(g, core, T, topo):
                 label("ahead")
                 repeat(t + 1, "g")
                 lists(t + 1)
-                act(A("w1%d" % ((t + 1) % 2)), A("uw", *cls(t + 1)), AF.Identity, A("cw"))
+                act(A("w1%d" % ((t + 1) % 2)), A("uw", *cls(t + 1)), AF.Identity, A("cw"), 0.0625)
                 act(A("f0g"), IND(A("f0"), A("sndl", 6 * t, 6 * t + 6)), AF.Copy)
             for h in range(1, 4):
                 for b in range(NB):

@@ -4,20 +4,27 @@ from concourse.bass import DstId, RemoteDMATransfer
 from concourse.mybir import AluOpType as OP, ActivationFunctionType as AF, AxisListType as AX
 
 V, NG, NJ = 768, 384, 192
-NS = [96, 96]
-U0 = [sum(NS[:b]) for b in range(len(NS))]
-NB, NM = len(NS), max(NS)
-JUDGE = ["sv", "vv"]
-PARTS = [("v", 20), ("s", 40), ("s", 36)]
-SCANS = [60, 36]
-HOP = [[PARTS, PARTS]] * 3
-AGAIN = [None, [("s", 48), ("s", 48)]]
-FPARTS = [48, 48]
+NB, N = 3, 64
+TEAMS = [(0,), (1,), (2,)]
+TN = [N * len(_t) for _t in TEAMS]
+T0 = [N * _t[0] for _t in TEAMS]
+NM = max(TN)
+JUDGE = [[("s", 32), ("v", 32)], [("v", 64)], [("v", 64)]]
+AGAIN = [None, None, [("s", 32), ("s", 32)]]
+CUTS = [2, 2, 2]
+EK = []
+for _j, _w in enumerate(TN):
+    _lo = sum(_x * (1 if _a else 2) for _x, _a in zip(TN[:_j], AGAIN))
+    EK.append((_lo, None) if AGAIN[_j] else (_lo + _w, _lo) if _j == 0 else (_lo, _lo + _w))
+PARTS = [("s", 32), ("s", 22), ("v", 10)]
+HOP = [[PARTS] * NB] * 3
+SCANS = [32, 32]
+TSCANS = [64]
 FIRST = 2.0
 LATE = ("i1152", "i15", "i8k", "nb1", "b2", "b1m", "nf8k", "nhalf")
 START = "vsvgvs"
-BANKS = [("p0", "p1", "p2"), ("p3", "p4", "p5")]
-DBANKS = [("p1", "p2"), ()]
+BANKS = [("p0", "p1"), ("p2", "p3"), ("p4", "p5")]
+DBANKS = [("p1", "p5"), ("p3", "p5"), ("p5", "p5")]
 KEEP, LIST = "p6", "p7"
 ZO, XO = 1152, 1664
 XG = XO + V
@@ -41,20 +48,27 @@ def _buf(name, cols, dtype=BF2, where="sbuf", rows=128, pool=True):
     WHERE[name] = (p, lo, cols, dtype)
 
 
-for _b, _w in enumerate(NS):
-    _buf("xw%d" % _b, XE if AGAIN[_b] else XE + ZO)
-    for _n in ("ga", "gb", "mt", "mx", "mn", "m0", "n0"):
-        _buf("%s%d" % (_n, _b), 16 * _w)
-    for _n in ("pq", "xv", "z3", "mz", "t15", "gk"):
-        _buf("%s%d" % (_n, _b), _w)
-    _buf("rl%d" % _b, 2 * _w)
-    for _n, _k in (("hot", 1), ("ww", 1), ("bw", 1), ("dn", 2), ("cl", 3)):
-        _buf("%s%d" % (_n, _b), _k * _w, "float16")
-    for _n, _k in (("aa", _w), ("of", _w), ("ll", 2 * _w), ("r1", 144), ("mb", 128)):
-        _buf("%s%d" % (_n, _b), _k, "float32")
-    _buf("ht%d" % _b, 128)
-    for _n, _k in (("ou", 3 * _w), ("wl", 24), ("xl", 16)):
+TWICE = [_t[0] for _t, _a in zip(TEAMS, AGAIN) if not _a]
+for _b in range(NB):
+    _buf("xw%d" % _b, XE + ZO if _b in TWICE else XE)
+    for _n in ("gb", "mx", "mn"):
+        _buf("%s%d" % (_n, _b), 16 * N)
+    for _n in ("pq", "xv", "z3", "mz"):
+        _buf("%s%d" % (_n, _b), N)
+    for _n, _k in (("hot", 1), ("ww", 1), ("bw", 1), ("cl", 3)):
+        _buf("%s%d" % (_n, _b), _k * N, "float16")
+    _buf("aa%d" % _b, N, "float32")
+    for _n, _k in (("ou", 3 * N), ("wl", 24)):
         _buf("%s%d" % (_n, _b), _k, "uint16")
+for _b, _w in enumerate(TN):
+    for _n in ("ga", "mt", "m0", "n0"):
+        _buf("%s%d" % (_n, _b), 16 * _w)
+    for _n, _k in (("t15", _w), ("gk", _w), ("rl", 2 * _w), ("ht", 128)):
+        _buf("%s%d" % (_n, _b), _k)
+    _buf("dn%d" % _b, 2 * _w, "float16")
+    _buf("r1%d" % _b, 144, "float32")
+    _buf("mb%d" % _b, 128, "float32")
+    _buf("xl%d" % _b, 16, "uint16")
 for _n in range(2):
     _buf("eu%d" % _n, NJ, "uint16")
     _buf("ct%d" % _n, NJ)
@@ -62,25 +76,25 @@ for _n in range(2):
     _buf("ek%d" % _n, 2 * NJ, "float16")
     _buf("w1%d" % _n, NJ, "float16")
     _buf("xr%d" % _n, 16 * NJ)
-for _n in ("f0", "st", "sd", "hs", "df"):
+for _n in ("f0", "st", "sd", "hs"):
     _buf(_n, NJ)
 for _n in ("enti", "usri", "uq"):
     _buf(_n, V, "int32")
 for _n in ("entt", "yef", "uw"):
     _buf(_n, V, "float32")
-for _n, _w in (("bt", V), ("lt", V), ("rx", 2 * NM), ("rm", 16 * max(SCANS + FPARTS)), ("rn", 16 * max(SCANS + FPARTS)), ("dg", 96)):
+for _n, _w in (("bt", V), ("lt", V), ("rm", 16 * max(SCANS + TSCANS)), ("rn", 16 * max(SCANS + TSCANS))):
     _buf(_n, _w)
 _buf("sndi", 24, "int32", "sbuf", 128, False)
 _buf("sndu", 24, "uint16")
 _buf("sndl", 24, "uint16")
 _buf("thi", 5, "int32", "sbuf", 8)
 _buf("thf", 5, "float32", "sbuf", 8)
-for _n, _w in (("tha", 5), ("thc", 5), ("rr", 1), ("pf", 4), ("bk", 4), ("py", 1), ("p1c", 1), ("c1k", 1), ("c25", 1), ("mgc", 1), ("c256", 1), ("cw", 1), ("n1k", 1), ("cz", 1), ("pg", 1),
-               ("top", 128), ("idf", 128)):
+for _n, _w in (("tha", 5), ("thc", 5), ("rr", 1), ("pf", 4), ("bk", 4), ("py", 1), ("p1c", 1), ("c25", 1), ("mgc", 1), ("c256", 1), ("cw", 1),
+               ("n1k", 1), ("cz", 1), ("pg", 1), ("c1k", 1), ("top", 128), ("cap", 128), ("idf", 128)):
     _buf(_n, _w, "float32")
 for _n, _w in (("rri", 1), ("rrj", 1), ("ji", NM), ("jj", NM), ("pi", 4), ("pj", 4), ("pk", 1)):
     _buf(_n, _w, "int32")
-for _n, _w, _d in (("ca", NM, "float16"), ("cb", NM, "float16"), ("bc", 4, "float32"), ("bi", 4, "float32"), ("mk", 2 * NM, BF2)):
+for _n, _w, _d in (("ca", N, "float16"), ("cb", N, "float16"), ("bc", 4, "float32"), ("bi", 4, "float32"), ("mk", 2 * NJ, BF2)):
     _buf(_n, _w, _d)
 _buf("gs0", NG, BF2, "sbuf", 128, False)
 _buf("f0g", 96, BF2, "sbuf", 128, False)
@@ -91,19 +105,19 @@ for _n in ("one", "zero", "i1k", "idn", "half", "nhalf", "neg", "ict", "ik", "ig
     _buf(_n, 128)
 for _n in ("oe", "ee0", "ee"):
     _buf(_n, 128, "float32", "sbuf", 8)
-for _n in ("yc96", "jc", "j16", "mask", "mq", "cm", "cq", "cm2", "cm3"):
+for _n in ("j16", "mask", "cm", "cq"):
     _buf(_n, NM)
+for _n in ("yc96", "jc", "mq", "cm2", "cm3"):
+    _buf(_n, N)
 for _n in range(8):
     _buf("p%d" % _n, 512, "float32", "psum")
 SCRATCH[LIST] = ("psum", [128, 32, 16], "float32")
 LOADS = ["snd", "xa", "ent", "yc", "bn", "usr", "th"]
-SEMAPHORES = (["sv", "ss", "st", "sg"] + ["o%d" % n for n in range(2 * NB)] + ["ld_" + n for n in LOADS]
+COPIES = [("yc", _b, XE) for _b in TWICE] + [(_n, _b, _c) for _b in range(1, NB) for _n, _c in (("xa", XO), ("yc", 0))]
+SEMAPHORES = (["sv", "ss", "st", "sg"] + ["o%d" % n for n in range(2 * NB)] + ["ld_" + n for n in LOADS] + ["cp%d" % n for n in range(len(COPIES))]
               + ["arr%d" % t for t in range(5)] + ["left%d" % t for t in range(5)]
               + ["free%d" % t for t in range(4)] + ["told%d" % t for t in range(4)])
 QS = {"v": "sv", "s": "ss", "t": "st", "g": "sg"}
-HURRY = dict([(_n, 2.0) for _n in ("pi", "idn", "blk", "neg", "ict", "ik", "ig", "w16", "top", "r10", "r11")]
-             + [(_n, 1.0) for _n in ("rm", "rn", "rx", "mk", "mgc", "cq", "half", "ixo")]
-             + [(_n, 4.0) for _n in ("uw", "cm", "bt", "usri")])
 PLAN = {}
 
 
@@ -147,182 +161,188 @@ def _cost(o, m):
     return f * m[0] + max(64, n * m[2] * gath if gath else n) * 1.0e-3 * m[1] if n else f
 
 
-MODELS = [(1.0, 0.87, 1.4, 0.13, 0.6, 1.05), (1.45, 1.2, 2.0, 0.18, 1.3, 0.6)]
-STEPS = 3000
-SEED, HEAT, LEAD = 3, 0.005, (0.5, 1.3, 2.1, 3.0)
+MODELS = [(1.05, 0.9, 1.4, 0.135, 0.95, 0.72), (1.0, 1.15, 1.1, 0.1, 0.9, 0.9), (1.05, 0.85, 1.9, 0.19, 0.9, 0.8)]
+STEPS = {2: 260000, 0: 25000, 4: 15000}
+HEAT = {2: 0.003, 0: 0.0007, 4: 0.0007}
+SEED, LEAD = 3, 1.0
 
 
-def _planner(calls):
-    _edges(calls)
+def _pieces(calls):
     head, ops = [], []
     for i, o in enumerate(calls):
         if o["q"] == "t" and i - 1 in o["pre"] and calls[i - 1]["q"] == "t" and all(
-                not w or calls[j]["once"] or head[j] in ops[-1]["pre"] for j, w in o["pre"].items()):
+                not w or calls[j]["once"] or calls[j]["round"] < o["round"] or head[j] in ops[-1]["pre"] for j, w in o["pre"].items()):
             p = ops[-1]
         else:
-            p = {"q": o["q"], "key": o["key"], "lag": o["lag"], "calls": [], "pre": {}}
+            p = {"q": o["q"], "key": o["key"], "lag": o["lag"], "round": o["round"], "batch": o["batch"], "calls": [], "pre": {}}
             ops.append(p)
         head.append(len(ops) - 1)
         p["calls"].append(i)
         for j, w in o["pre"].items():
             if head[j] != len(ops) - 1:
                 p["pre"][head[j]] = p["pre"].get(head[j], False) or w
+    return ops
+
+
+def _shop(calls, pieces, t, models):
+    own = [i for i, o in enumerate(pieces) if o["round"] == t]
+    at = dict((i, k) for k, i in enumerate(own))
+    ops = [pieces[i] for i in own]
+    s = {"ops": ops, "queue": ["vstgyxz".index(o["q"]) for o in ops], "succ": [[] for _ in ops],
+         "pre": [[at[j] for j in o["pre"] if j in at] for o in ops],
+         "wait": [[at[j] for j, w in o["pre"].items() if w and j in at] for o in ops],
+         "cost": [[sum(_cost(calls[i], m) for i in o["calls"]) for o in ops] for m in models],
+         "lag": [[o["lag"] * m[4] + m[3] for o in ops] for m in models]}
+    for i, l in enumerate(s["pre"]):
+        for j in l:
+            s["succ"][j].append(i)
+    return s
+
+
+def _listed(s, known):
+    ops, queue, cost, lag = s["ops"], s["queue"], s["cost"][0], s["lag"][0]
     n = len(ops)
-    names = sorted(set(o["q"] for o in ops))
-    queue = [names.index(o["q"]) for o in ops]
-    key = [o["key"] for o in ops]
-    wait = [[j for j in o["pre"] if o["pre"][j]] for o in ops]
-    costs = [[sum(_cost(calls[i], m) for i in o["calls"]) for o in ops] for m in MODELS]
-    lags = [[o["lag"] * m[4] + m[3] for o in ops] for m in MODELS]
-    succ = [[] for _ in ops]
-    for i, o in enumerate(ops):
-        for j in o["pre"]:
-            succ[j].append((i, o["pre"][j]))
-    path = [0.0] * n
+    succ = [list(l) for l in s["succ"]]
+    last = {}
+    for i in sorted((i for i in range(n) if ops[i]["key"] in known), key=lambda i: known[ops[i]["key"]]):
+        if queue[i] in last:
+            succ[last[queue[i]]].append(i)
+        last[queue[i]] = i
+    pri = [0.0] * n
     for i in range(n - 1, -1, -1):
-        path[i] = costs[0][i] + max([path[j] + (lags[0][i] if w else 0.0) for j, w in succ[i]] + [lags[0][i]])
-    count = [len(o["pre"]) for o in ops]
-    lands = [i for i in range(n) if ops[i]["q"] == "x"]
-    early = [i for i in range(n - 1, -1, -1) if calls[ops[i]["calls"][0]]["once"]]
+        pri[i] = -known[ops[i]["key"]] if ops[i]["key"] in known else cost[i] + lag[i] + max([pri[j] for j in s["succ"][i]] + [-99.0])
+    if not known:
+        pri = [p - LEAD * o["batch"] for p, o in zip(pri, ops)]
+    left, rdy, free, order = [0] * n, [0.0] * n, [0.0] * 7, []
+    for l in succ:
+        for j in l:
+            left[j] += 1
+    cand = [i for i in range(n) if not left[i]]
+    while cand:
+        now, i = min((max(rdy[i], free[queue[i]]), i) for i in cand)
+        q = queue[i]
+        i = max((j for j in cand if queue[j] == q and rdy[j] <= now + 0.1), key=lambda j: pri[j])
+        cand.remove(i)
+        order.append(i)
+        now = max(now, rdy[i])
+        free[q] = now + cost[i]
+        for j in succ[i]:
+            rdy[j] = max(rdy[j], free[q] + lag[i] if i in s["wait"][j] else now)
+            left[j] -= 1
+            if not left[j]:
+                cand.append(j)
+    assert len(order) == n
+    return order
 
-    def schedule(bonus, patience):
-        cost, lag = costs[0], lags[0]
-        pri = [path[i] + bonus[key[i]] for i in range(n)]
-        for i in early:
-            pri[i] = cost[i] + lag[i] + bonus[key[i]] + max([pri[j] for j, _w in succ[i]] + [0.0])
-        left, rdy = list(count), [0.0] * n
-        cand = [[] for _ in names]
-        for i in range(n):
-            if not left[i]:
-                cand[queue[i]].append(i)
-        free, soon = [0.0] * len(names), [0.0 if c else 1e9 for c in cand]
-        order = []
-        for _i in range(n):
-            s0 = min(soon)
-            q = soon.index(s0)
-            c = cand[q]
-            pick, p = -1, -1e9
-            for i in c:
-                if pri[i] > p and rdy[i] <= s0 + patience[key[i]]:
-                    pick, p = i, pri[i]
-            c.remove(pick)
-            order.append(pick)
-            st = rdy[pick] if rdy[pick] > s0 else s0
-            end = free[q] = st + cost[pick]
-            done = end + lag[pick]
-            soon[q] = max(end, min([rdy[i] for i in c])) if c else 1e9
-            for j, w in succ[pick]:
-                e = done if w else st
-                if e > rdy[j]:
-                    rdy[j] = e
-                left[j] -= 1
-                if not left[j]:
-                    r = queue[j]
-                    cand[r].append(j)
-                    e = max(free[r], rdy[j])
-                    if e < soon[r]:
-                        soon[r] = e
-        return order, pri, rdy
 
-    def length(order, m):
-        cost, lag = costs[m], lags[m]
-        free, fin, why = [(0.0, -1)] * len(names), [0.0] * n, [-1] * n
-        for i in order:
-            t, w = free[queue[i]]
-            for j in wait[i]:
+def _improve(s, order, steps, heat, rng):
+    queue, pre, succ, wait, cost, lag = [s[k] for k in ("queue", "pre", "succ", "wait", "cost", "lag")]
+    n, nm = len(order), len(cost)
+    work = [list(zip(range(n), wait, cost[m], lag[m])) for m in range(nm)]
+    prev, nxt = [n] * (n + 1), [n] * (n + 1)
+
+    def link(seg, last, tail):
+        last = dict(last)
+        for x in seg:
+            p = last[queue[x]]
+            prev[x], nxt[p], last[queue[x]] = p, x, x
+        for q, x in tail.items():
+            nxt[last[q]], prev[x] = x, last[q]
+
+    def run(a, m, end, fin):
+        w = work[m]
+        for x in order[a:]:
+            i, js, c, l = w[x]
+            t = end[prev[i]]
+            for j in js:
                 if fin[j] > t:
-                    t, w = fin[j], j
-            t += cost[i]
-            free[queue[i]] = (t, i)
-            fin[i] = t + lag[i]
-            why[i] = w
-        top = max(fin)
-        i, pairs = fin.index(top), []
-        while why[i] >= 0:
-            j = why[i]
-            if j not in ops[i]["pre"]:
-                pairs.append((i, j, fin[j] - lag[j] - cost[j]))
-            i = j
-        return top + (len(lands) == 3) * 2 * (fin[lands[-1]] - fin[lands[1]]), pairs
+                    t = fin[j]
+            end[i] = t = t + c
+            fin[i] = t + l
+        return end, fin
 
-    return ops, key, schedule, length
-
-
-def _plan(few, calls):
-    ops, key, schedule, length = _planner(few)
-    n, keys = len(ops), 1 + max(o["key"] for o in calls)
-    batch = [0] * keys
-    for o in calls:
-        batch[o["key"]] = o["batch"]
-    kin = {}
-    for o in calls:
-        kin.setdefault(o["kin"], set()).add(o["key"])
-    kin = dict((k, sorted(l)) for l in kin.values() for k in l)
-    once = set(o["key"] for o in calls if o["once"])
-    rng = np.random.RandomState(SEED)
-    unit = []
-
-    def judge(c, most=None):
-        made = schedule(*c)
-        res = [length(made[0], 0)]
-        if most and res[0][0] / unit[0] > most:
-            return None
-        res += [length(made[0], m) for m in range(1, len(MODELS))]
-        if not unit:
-            unit.extend(r[0] for r in res)
-        return sum(r[0] / u for r, u in zip(res, unit)), c, made, res
-
-    def climb(cur, steps, heat, alike, fixed=()):
-        best = cur
-        for step in range(steps):
-            c = (list(cur[1][0]), list(cur[1][1]))
-            same = (lambda k: kin[k]) if rng.rand() < alike else (lambda k: (k,))
-            how = rng.rand()
-            if how < 0.6:
-                pairs = cur[3][0 if rng.rand() < 0.7 else -1][1]
-                i, j, at = pairs[rng.randint(len(pairs))]
-                gap = max(0.0, cur[2][1][j] - cur[2][1][i]) + 0.02 + (0.3, 0.3, 1.5, 5.0)[rng.randint(4)] * rng.rand()
-                up = rng.rand() < 0.5
-                for k in same(key[i] if up else key[j]):
-                    c[0][k] += gap if up else -gap
-                for k in same(key[i]):
-                    c[1][k] = min(0.9, max(c[1][k], cur[2][2][i] - at + 0.02))
-            elif how < 0.7:
-                x = 0.1 * rng.randint(7)
-                for k in same(key[rng.randint(n)]):
-                    c[1][k] = x
+    def held(m):
+        end, fin = times[m]
+        i, out = fin.index(max(fin)), []
+        while i < n:
+            at, j = end[i] - cost[m][i] - 1e-9, prev[i]
+            if j < n and end[j] >= at:
+                if j not in pre[i]:
+                    out.append((j, i))
+                i = j
             else:
-                a = key[rng.randint(n)]
-                x = (0.3, 1.0, 3.0)[rng.randint(3)] * rng.randn()
-                for b in range(a, min(keys, a + (1, 1, 3, 8, 20)[rng.randint(5)])):
-                    for k in same(b):
-                        c[0][k] += x
-            for k in fixed:
-                c[0][k], c[1][k] = cur[1][0][k], cur[1][1][k]
-            if c == cur[1]:
-                continue
-            bar = cur[0] - heat * (1 - step / steps) * math.log(rng.rand())
-            new = judge(c, bar - cur[0] + cur[3][0][0] / unit[0] + 0.004)
-            if new and new[0] <= bar:
-                cur = new
-                if cur[0] < best[0]:
-                    best = cur
-        return best
+                i = ([j for j in wait[i] if fin[j] >= at] + [n])[0]
+        return out
 
-    hurry = [0.0] * keys
-    for o in calls:
-        hurry[o["key"]] = o["hurry"]
-    field = [judge(([h - lead * b for b, h in zip(batch, hurry)], [0.4 if h > 7 else 0.1 for h in hurry])) for lead in LEAD]
-    while len(field) > 1:
-        field = [climb(c, STEPS // (3 * len(field)), HEAT, 0.7, once) for c in field]
-        field = sorted(field, key=lambda c: c[0])[:len(field) // 2]
-    best = climb(field[0], STEPS // 6, HEAT / 2, 0.3, once)
-    best = climb(best, STEPS // 6, HEAT / 5, 0.0)
-    del unit[:]
-    ops, key, schedule, length = _planner(calls)
-    n = len(ops)
-    best = climb(judge(best[1]), STEPS // 10, HEAT / 4, 0.3)
-    return [i for p in best[2][0] for i in ops[p]["calls"]]
+    link(order, dict((q, n) for q in queue), dict((q, n) for q in queue))
+    times = [run(0, m, [0.0] * (n + 1), [0.0] * n) for m in range(nm)]
+    unit = [max(x[1]) for x in times]
+    vals, best, kept, arcs = [1.0] * nm, float(nm), list(order), None
+    for step in range(steps):
+        if step % 1000 == 0:
+            dice = rng.rand(1000, 6).tolist()
+        d = dice[step % 1000]
+        arcs = arcs or [held(m) for m in range(nm)]
+        up, pairs = d[0] < 0.5, arcs[int(d[1] * nm)]
+        if pairs and d[2] < 0.8:
+            u, v = pairs[int(d[3] * len(pairs))]
+            far = int(d[4] * 10) + 1 if d[4] < 0.3 else 0
+        else:
+            u = v = int(d[3] * n)
+            far = 1 + int(d[4] * 2)
+        for _k in range(far):
+            u, v = (prev[u] if u < n else n, v) if up else (u, nxt[v] if v < n else n)
+        if u == n or v == n:
+            continue
+        a, b = order.index(u), order.index(v)
+        seg = order[a:b + 1]
+        edges = pre if up else succ
+        x = v if up else u
+        take, need = set([x]), set(edges[x])
+        for x in (seg[-2::-1] if up else seg[1:]):
+            if x in need:
+                take.add(x)
+                need.update(edges[x])
+        if u in take and v in take:
+            continue
+        new = [x for x in seg if (x in take) == up] + [x for x in seg if (x in take) != up]
+        tail = dict((queue[x], nxt[x]) for x in seg)
+        head = dict((queue[x], prev[x]) for x in seg[::-1])
+        order[a:b + 1] = new
+        link(new, head, tail)
+        bar = -heat * nm * (1 - step / steps) ** 2 * math.log(d[5] + 1e-300) + 1e-12
+        tot, got, got_vals = 0.0, [], []
+        for m in range(nm):
+            x = run(a, m, times[m][0][:], times[m][1][:])
+            got.append(x)
+            got_vals.append(max(x[1]) / unit[m])
+            tot += got_vals[m] - vals[m]
+            if tot > bar + (0.004 if m < nm - 1 else 0.0):
+                order[a:b + 1] = seg
+                link(seg, head, tail)
+                break
+        else:
+            times, vals, arcs = got, got_vals, None
+            if sum(vals) < best:
+                best, kept = sum(vals), list(order)
+    order[:] = kept
+    link(order, dict((q, n) for q in queue), dict((q, n) for q in queue))
+    end = run(0, 0, [0.0] * (n + 1), [0.0] * n)[0]
+    return kept, dict((s["ops"][i]["key"], end[i] - cost[0][i] + 1e-7 * k) for k, i in enumerate(kept))
+
+
+def _plan(calls):
+    pieces = _pieces(calls)
+    rng = np.random.RandomState(SEED)
+    known, orders = {}, {}
+    for t in (2, 0, 4, 1, 3):
+        s = _shop(calls, pieces, t, MODELS)
+        order = _listed(s, known)
+        if t in STEPS:
+            order, starts = _improve(s, order, STEPS[t], HEAT[t], rng)
+            known = known or starts
+        orders[t] = [i for p in order for i in s["ops"][p]["calls"]]
+    return [i for t in range(5) for i in orders[t]]
 
 
 def rank_program(g, core, T, topo):
@@ -331,17 +351,16 @@ def rank_program(g, core, T, topo):
         return
     ops = []
     names = {}
-    step = [None, 0]
-    hurry = [0.0]
+    step = [None, 0, 0]
     eng = {"v": g.vector, "s": g.scalar, "t": g.tensor, "g": g, "y": g.sync}
 
     def label(*x):
-        step[:] = [x, 0]
+        step[:2] = [x, 0]
 
     def add(q, fn, rd, wr, cost, lag=0.0, sem=None, amount=1, dma=False, after=()):
         key = names.setdefault((step[0], step[1]), len(names))
         step[1] += 1
-        ops.append({"q": q, "fn": fn, "key": key, "once": step[0] is None, "hurry": HURRY.get(wr[0][0] if wr else None, hurry[0]) if step[0] is None else 0.0, "kin": (step[0] and step[0][::2], step[1]),
+        ops.append({"q": q, "fn": fn, "key": key, "once": step[0] is None, "round": step[2],
                     "batch": step[0][-1] if step[0] and len(step[0]) > 1 else 0, "rd": rd, "wr": wr,
                     "cost": cost, "lag": lag, "sem": sem, "amount": amount, "dma": dma, "after": list(after), "remote": False})
         return len(ops) - 1
@@ -457,47 +476,39 @@ def rank_program(g, core, T, topo):
         ops[j]["remote"] = True
         return add("z", None, [], [], (0.0, 0, False), 1.0, "free%d" % slot, 1, True, (j,))
 
-    def send(slot, parts, land, after=()):
-        def call(e):
-            if len(parts) == 1:
-                return e.remote_dma(land[0], parts[0][0], T.sem["arr%d" % slot], T.sem["left%d" % slot], pid, rid, mask)
-            move = RemoteDMATransfer(dst_ids=[DstId(rid=rid, pnc=pid)], dma_engine_mask=mask, remote_sem=T.sem["arr%d" % slot],
-                                     srcs=[a[0] for a in parts], dsts=[land[0]], alu_op=1)
-            return e.remote_dma_fused([move], local_sem=T.sem["left%d" % slot])
-        j = add("g", call, regs(*parts), [], (0.3, 0, False), 1.0, "left%d" % slot, len(es), False, after)
+    def send(slot, what, land, after=()):
+        j = add("g", lambda e: e.remote_dma(land[0], what[0], T.sem["arr%d" % slot], T.sem["left%d" % slot], pid, rid, mask),
+                regs(what), [], (0.3, 0, False), 1.0, "left%d" % slot, len(es), False, after)
         ops[j]["remote"] = True
         add("x", None, [], regs(land), (0.0, 0, False), 1.5 + FIRST * (slot == 4), "arr%d" % slot, n_in, True, (j,))
         return j
 
-    def cls(t, b=None, base=0):
-        lo, n = (0, NJ) if b is None else (U0[b], NS[b])
+    def cls(t, lo=0, n=NJ, base=0):
         return base + 4 * lo + t % 4, base + 4 * (lo + n), 4
 
-    def part(name, b, times=1):
-        return A(name, times * U0[b], times * (U0[b] + NS[b]))
+    def part(name, b):
+        return A(name, N * b, N * b + N)
+
+    def team(name, j):
+        return A(name, T0[j], T0[j] + TN[j])
 
     own0 = A("xw0", XO, XG)
     load("y", "snd", A("sndi"), 1.5)
     xa = load("s", "xa", own0, 2.0)
     load("y", "ent", A("enti"), 3.0)
     load("y", "yc", A("xw0", 0, ZO), 2.0, None, (xa,))
-    hurry[0] = 8.0
     for c in range(4):
         ts(A("sndu", 6 * c, 6 * c + 6), A("sndi", 6 * c, 6 * c + 6), 4, c, OP.mult, OP.add)
     act(A("gs0"), IND(own0, A("sndu")), AF.Copy)
-    first = send(4, [A("gs0")], A("xw0", XG, XE))
-    hurry[0] = 0.0
+    first = send(4, A("gs0"), A("xw0", XG, XE))
     vcp(A("sndl"), A("sndi"))
     fill(A("one"), 1.0)
-    twice = "xw%d" % AGAIN.index(None)
     for name, out, lag in (("usr", A("usri"), 2.5), ("bn", A("bt"), 3.2), ("th", A("thi"), 3.3)):
         load("y", name, out, lag, None, (first,))
-    hurry[0] = 2.0
-    vcp(A("xw1", XO, XG), own0)
-    vcp(A("xw1", 0, ZO), A("xw0", 0, ZO))
-    hurry[0] = 0.0
-    vcp(A(twice, XE, XE + ZO), A("xw0", 0, ZO))
-    fill(A(twice, ZO, XO), 0.0)
+    for i, (name, b, lo) in enumerate(COPIES):
+        load("y", name, A("xw%d" % b, lo, lo + (V if name == "xa" else ZO)), 4.0 + 0.6 * i, "cp%d" % i, (first,))
+    for b in TWICE:
+        fill(A("xw%d" % b, ZO, XO), 0.0)
 
     iota(A("oe"), [[0, 128]], 1, 0)
     sel(A("idn"), A("one"), [[-1, 128]], OP.is_equal, 0, 1)
@@ -506,10 +517,11 @@ def rank_program(g, core, T, topo):
     sel(A("ee0"), A("oe"), [[1, 128]], OP.is_ge, 0, -16)
     sel(A("ee"), A("ee0"), [[-1, 128]], OP.is_ge, 15, 16)
     iota(A("ji"), [[1, NM]], 128, -1)
-    iota(A("jc"), [[1, NM]], 0, 0)
+    iota(A("jc"), [[1, N]], 0, 0)
     iota(A("pi"), [[0, 4]], 0, 1)
-    act(A("top"), A("one"), AF.Identity, None, 0.0)
-    ts(A("top", 0, 128, 16), A("jc", 0, 8), 131072.0, 131071.0, OP.mult, OP.add)
+    for name, x in (("top", 131071.0), ("cap", 65535.0)):
+        act(A(name), A("one"), AF.Identity, None, 0.0)
+        ts(A(name, 0, 128, 16), A("jc", 0, 8), 131072.0, x, OP.mult, OP.add)
     ts(A("pj"), A("pi"), 15, None, OP.bitwise_and)
     vcp(A("pf"), A("pj"))
     ts(A("pk"), A("pi", 0, 1), 112, None, OP.bitwise_and)
@@ -537,29 +549,29 @@ def rank_program(g, core, T, topo):
     ts(A("jj"), A("ji"), 15, None, OP.bitwise_and)
     ts(A("mask"), A("jj"), 0, -4096.0, OP.not_equal, OP.mult)
     iota(A("j16"), [[16, NM]], 0, 0)
-    iota(A("bi"), [[NM, 4]], ZO, 0)
+    iota(A("bi"), [[N, 4]], ZO, 0)
     act(A("bc"), A("bi"), AF.Identity, A("bk", 0, 1))
-    c0 = (48 * (ZO - 1) + 3 * NM + 3) % GAP
+    c0 = (48 * (ZO - 1) + 3 * N + 3) % GAP
     ts(A("ca"), A("jc"), 3.0, c0 - (GAP - 1) / 2, OP.mult, OP.add)
     ts(A("cb"), A("jc"), -3.0, -float(c0), OP.mult, OP.add)
-    for b, n in enumerate(NS):
-        s = str(b)
-        iota(A("r1" + s, 128, 144), [[0, 16]], 1048576, 0)
-        if not AGAIN[b]:
+    for j, n in enumerate(TN):
+        iota(A("r1%d" % j, 128, 144), [[0, 16]], 1048576, 0)
+        mid, lo = EK[j]
+        if not AGAIN[j]:
             for i in range(2):
-                act(A("ek%d" % i, 2 * U0[b] + n, 2 * U0[b] + 2 * n), A("one", 0, n), AF.Identity, None, A("pf", 0, 1))
-    mms(A("p6", 0, NM), [(A("idn"), A("mask")), (A("i1k"), A("one", 0, NM))])
-    mms(A("p6", NM, 2 * NM), [(A("idn"), A("mask")), (A("idn"), A("j16"))])
-    act(A("mk"), A("p6", 0, 2 * NM), AF.Copy)
-    ts(A("mq"), A("mask"), -WO, None, OP.add)
-    act(A("yc96"), A("one", 0, NM), AF.Identity, None, A("py"))
+                act(A("ek%d" % i, lo, lo + n), A("one", 0, n), AF.Identity, None, A("pf", 0, 1))
+            mms(A("p6", lo, lo + n), [(A("idn"), A("mask", 0, n)), (A("idn"), A("j16", 0, n))])
+            mms(A("p6", mid, mid + n), [(A("idn"), A("mask", 0, n)), (A("i1k"), A("one", 0, n))])
+    wide = 2 * sum(n for n, a in zip(TN, AGAIN) if not a)
+    act(A("mk", 0, wide), A("p6", 0, wide), AF.Copy)
+    ts(A("mq"), A("mask", 0, N), -WO, None, OP.add)
+    act(A("yc96"), A("one", 0, N), AF.Identity, None, A("py"))
     for name, x in (("cm", MAGIC), ("cm2", MAGIC * 8192 * GAP), ("cm3", MAGIC * 2 ** 24), ("cq", -0.25)):
-        sel(A(name), A("one", 0, NM), [[0, NM]], OP.is_gt, 0, 0, x)
-    for name, x in (("c256", 256.0), ("cz", 0.5 - ZO), ("mgc", -MAGIC), ("n1k", -1024.0), ("cw", WO - 15.0 / 32),
-                    ("c1k", 1024.0), ("c25", 0.25)):
+        n = WHERE[name][2]
+        sel(A(name), A("one", 0, n), [[0, n]], OP.is_gt, 0, 0, x)
+    for name, x in (("c256", 256.0), ("cz", 0.5 - ZO), ("mgc", -MAGIC), ("n1k", -1024.0), ("cw", WO - 15.0 / 32), ("c25", 0.25),
+                    ("c1k", 1024.0)):
         act(A(name), A("one", 0, 1), AF.Identity, None, x)
-    for lo in (0, NM):
-        sel(A("rx", lo, lo + NM), A("one", 0, NM), [[0, NM // 16], [1, 16]], OP.is_gt, 0, 0)
     for name, x in (("rm", -512.0), ("rn", 512.0)):
         fill(A(name), 0.0)
         act(A(name, 0, WHERE[name][2], 16), A("one", 0, WHERE[name][2] // 16), AF.Identity, None, x)
@@ -568,178 +580,188 @@ def rank_program(g, core, T, topo):
     def lists(t):
         copy("g" if t else "v", A("eu%d" % (t % 2)), A("entt", *cls(t)))
         act(A("ct%d" % (t % 2)), A("entt", *cls(t)), AF.Sign, A("cz"))
-        for b, n in enumerate(NS):
-            act(A("ek%d" % (t % 2), 2 * U0[b], 2 * U0[b] + n), A("entt", *cls(t, b)), AF.Identity, A("n1k"))
+        runs = []
+        for j, n in enumerate(TN):
+            if runs and runs[-1][0] + runs[-1][2] == EK[j][0]:
+                runs[-1][2] += n
+            else:
+                runs.append([EK[j][0], T0[j], n])
+        for lo, at, n in runs:
+            act(A("ek%d" % (t % 2), lo, lo + n), A("entt", *cls(t, at, n)), AF.Identity, A("n1k"))
 
     def repeat(t, queues):
         for r in range(16):
-            copy(queues[r % len(queues)], A("xr%d" % (t % 2), r, 16 * NJ, 16), A("xw0", *cls(t, None, XO)))
-        for b, n in enumerate(NS):
-            w = n // len(JUDGE[b])
-            sel(part("xs%d" % (t % 2), b), A("xw0", *cls(t, b, XO)), [[1, n]], OP.is_ge, -w * JUDGE[b].count("s"), 0)
+            copy(queues[r % len(queues)], A("xr%d" % (t % 2), r, 16 * NJ, 16), A("xw0", *cls(t, base=XO)))
+        for j, n in enumerate(TN):
+            sel(team("xs%d" % (t % 2), j), A("xw0", *cls(t, T0[j], n, XO)), [[1, n]], OP.is_ge,
+                -sum(w for q, w in JUDGE[j] if q == "s"), 0)
 
     for c in range(4):
-        hurry[0] = 3.0 * (c == 0)
         vcp(A("yef", *cls(c)), A("enti", *cls(c)))
         act(A("lt", NJ * c, NJ * c + NJ), A("yef", *cls(c)), AF.Sign, A("cz"))
-        E = A(("p2", "p4", "p6", "p2")[c], 0, NJ)
+        E = A(("p0", "p2", "p4", "p3")[c], 0, NJ)
         mms(E, [(A("idf"), A("yef", *cls(c))), (A("ixe"), A("lt", NJ * c, NJ * c + NJ))])
         act(A("entt", *cls(c)), E, AF.Identity, A("c256"))
-    hurry[0] = 3.0
     lists(0)
     repeat(0, START)
-    hurry[0] = 0.0
     copy("g", A("uw"), A("usri"))
     ts(A("uq"), A("usri"), 15, None, OP.bitwise_and)
     act(A("w10"), A("uw", *cls(0)), AF.Identity, A("cw"), 0.0625)
     vcp(A("thf"), A("thi"))
-    mm(A("p5", 0, 5), A("ee"), A("thf"), True, True)
-    act(A("tha"), A("p5", 0, 5), AF.Copy)
+    mm(A(KEEP, 0, 5), A("ee"), A("thf"), True, True)
+    act(A("tha"), A(KEEP, 0, 5), AF.Copy)
     act(A("thc", 0, 1), A("tha", 0, 1), AF.Copy)
-    copy("g", A("xw1", XG, XE), A("xw0", XG, XE))
-    setup = len(ops)
 
-    def gather(out, b, off, first, parts):
-        lo = 0
+    def gather(b, off, lo, parts):
+        at = 0
         for q, w in parts:
-            copy(q, A(out, 16 * lo, 16 * (lo + w)), IND(A("xw%d" % b, 0, XE), A(off, first + lo, first + lo + w)))
-            lo += w
+            copy(q, A("gb%d" % b, 16 * at, 16 * (at + w)), IND(A("xw%d" % b, 0, XE), A(off, lo + at, lo + at + w)))
+            at += w
 
-    def scans(G, b, parts, mx="mx", mn="mn"):
-        lo = 0
+    def scans(G, mx, mn, lo, parts):
         for w in parts:
             hi = lo + 16 * w
-            scan(A(mx + str(b), lo, hi), A("rm", 0, 16 * w), A(G, lo, hi), OP.add, OP.max)
-            scan(A(mn + str(b), lo, hi), A("rn", 0, 16 * w), A(G, lo, hi), OP.add, OP.min)
+            scan(A(mx, lo, hi), A("rm", 0, 16 * w), A(G, lo, hi), OP.add, OP.max)
+            scan(A(mn, lo, hi), A("rn", 0, 16 * w), A(G, lo, hi), OP.add, OP.min)
             lo = hi
 
-    def fin(bank, b, early, at, late, out, mx="mx", mn="mn"):
-        n = NS[b]
-        p = A(bank, 0, n)
-        mms(p, early + [(HALF, A(mx + str(b), at, 16 * n, 16)), (HALF, A(mn + str(b), at, 16 * n, 16))]
-            + late + [(I, A("cm", 0, n))])
+    def fin(p, early, mx, mn, late, out):
+        mms(p, early + [(HALF, mx), (HALF, mn)] + late + [(I, A("cm", 0, p[2]))])
         act(out, p, AF.Abs, A("mgc"))
 
-    def score(t, b):
-        n, s, u = NS[b], str(b), str(t % 2)
-        b0 = BANKS[b][0]
-        mms(A(b0, 0, 128, 1, n), [(part("ct" + u, b), A("ict")), (A("one", 0, n), A("ik")), (A("one", 0, n), A("ig"))], True, False)
-        if "s" not in JUDGE[b]:
-            for m in range(4):
-                act(A("mt" + s, 4 * n * m, 4 * n * (m + 1)), A("ga" + s, m, 16 * n, 4), AF.Abs)
-                for e in range(4):
-                    mm(A(b0, 4 * e + m, 128, 16, n), A("mt" + s, 4 * n * m + e, 4 * n * (m + 1), 4), A("w16", 0, 128, 16),
-                       False, (m, e) == (3, 3))
-            return
-        w = 8 * n // len(JUDGE[b])
-        turn = 0
-        for m in range(2):
-            for p, q in reversed(list(enumerate(JUDGE[b]))):
-                d = A("ga" + s, 2 * w * p + m, 2 * w * (p + 1), 2)
-                if q == "s":
-                    lo = 16 * U0[b] + 2 * w * p
-                    gm, d = d, A(DBANKS[b][turn], 0, w)
-                    turn += 1
-                    mms(d, [(NEG, A("xr" + u, lo + m, lo + 2 * w, 2)), (I, gm)])
-                act(A("mt" + s, 8 * n * m + w * p, 8 * n * m + w * (p + 1)), d, AF.Abs)
-            for e in range(8):
-                mm(A(b0, 2 * e + m, 128, 16, n), A("mt" + s, 8 * n * m + e, 8 * n * (m + 1), 8), A("w16", 0, 128, 16),
-                   False, (m, e) == (1, 7))
+    def less(t, lo, n):
+        return [(NEG, A("bt", *cls(t, lo, n))), (I, A("cq", 0, n)), (I, A("xs%d" % (t % 2), lo, lo + n))]
 
-    def trial(t, b):
-        n, s, u = NS[b], str(b), str(t % 2)
-        b0, b1, b2 = BANKS[b]
-        K, top = A(b0, 0, 128, 1, n), A("top", 0, 128, 1, n)
-        xs = part("xs" + u, b)
-        less = [(NEG, A("bt", *cls(t, b))), (I, A("cq", 0, n))]
+    def score(t, j):
+        n, s, u, cut = TN[j], str(j), str(t % 2), CUTS[j]
+        keys = BANKS[TEAMS[j][0]][0]
+        mms(A(keys, 0, 128, 1, n), [(team("ct" + u, j), A("ict")), (A("one", 0, n), A("ik")), (A("one", 0, n), A("ig"))], True, False)
+        per = 16 // cut
+        turn = 0
+        for m in range(cut):
+            hi = n
+            for q, w in reversed(JUDGE[j]):
+                lo = hi - w
+                d = A("ga" + s, 16 * lo + m, 16 * hi, cut)
+                if q == "s":
+                    gm, d = d, A(DBANKS[j][turn % 2], 0, per * w)
+                    turn += 1
+                    mms(d, [(NEG, A("xr" + u, 16 * (T0[j] + lo) + m, 16 * (T0[j] + hi), cut)), (I, gm)])
+                act(A("mt" + s, per * (n * m + lo), per * (n * m + hi)), d, AF.Abs)
+                hi = lo
+            for e in range(per):
+                mm(A(keys, cut * e + m, 128, 16, n), A("mt" + s, per * n * m + e, per * n * (m + 1), per), A("w16", 0, 128, 16),
+                   False, (m, e) == (cut - 1, per - 1))
+
+    def trial(t, j):
+        n, s, u = TN[j], str(j), str(t % 2)
+        b0, b1 = BANKS[TEAMS[j][0]]
+        win = "xw%d" % TEAMS[j][0]
+        K, top = A(b0, 0, 128, 1, n), A("cap" if AGAIN[j] else "top", 0, 128, 1, n)
         scan(A("r1" + s, 0, 128, 1, n), top, K, OP.max, OP.min)
         scan(A("mb" + s, 0, 128, 1, n), top, A("r1" + s, 15, 143, 1, n), OP.max, OP.min)
         ht = A("ht" + s, 0, 128, 1, n)
         tt(ht, K, A("mb" + s, 0, 128, 1, n), OP.is_equal)
-        z = A("xw" + s, ZO, ZO + n)
-        if AGAIN[b]:
+        if AGAIN[j]:
             E = A(b1, 0, n)
-            mms(E, [(I, A("ek" + u, 2 * U0[b], 2 * U0[b] + n)), (ht, A("ixo", 0, n, 1, n))])
-            mm(part(KEEP, b), ht, A("idn" if t < 4 else "i1152", 0, n, 1, n), True, True)
-            act(A("ou" + s, 0, n), E, AF.Relu, A("c1k"))
-            scans("ga" + s, b, FPARTS, "m0", "n0")
-            fin(b2, b, less + [(I, xs)], 15, [], part("f0", b), "m0", "n0")
-            gather("gb" + s, b, "ou" + s, 0, AGAIN[b])
-            scans("gb" + s, b, [w for _q, w in AGAIN[b]])
-            fin(b0, b, less, 15, [], z)
+            mms(E, [(I, A("ek" + u, EK[j][0], EK[j][0] + n)), (ht, A("ixo", 0, n, 1, n))])
+            act(A("ou%d" % TEAMS[j][0], 0, n), E, AF.Relu, A("c1k"))
+            for b in TEAMS[j]:
+                gather(b, "ou%d" % TEAMS[j][0], N * b - T0[j], AGAIN[j])
+                scans("gb%d" % b, "mx%d" % b, "mn%d" % b, 0, [w for _q, w in AGAIN[j]])
+                fin(A(BANKS[b][0], 0, N), less(t, N * b, N)[:2], A("mx%d" % b, 15, 16 * N, 16), A("mn%d" % b, 15, 16 * N, 16), [],
+                    A("xw%d" % b, ZO, ZO + N))
+            return
+        copy("g", A("t15" + s), A("ga" + s, 15, 16 * n, 16))
+        for lo in (0, n):
+            mm(A(b1, lo, lo + n), ht, A("idn", 0, n, 1, n), True, True)
+        lo = min(EK[j])
+        tt(A("dn" + s), A(b1, 0, 2 * n), A("ek" + u, lo, lo + 2 * n), OP.mult)
+        W = sixteens(256 * (j % 2), 2 * n)
+        mms(W, [(I, A("mk", lo, lo + 2 * n)), (A("blk"), A("dn" + s))])
+        greatest(A("xl" + s, 0, n // 8), W)
+        xl, pl = [A("xl" + s, (i - lo) // 16, (i - lo + n) // 16) for i in EK[j]]
+        vcp(IND(A("ga" + s), pl), A("t15" + s))
+        tt(A("ga" + s, 15, 16 * n, 16), IND(A(win, ZO), xl), team("xs" + u, j), OP.subtract)
+        act(A("gk" + s), IND(A(win, 0, XE), xl), AF.Copy)
+        for b in TEAMS[j]:
+            lo = 16 * (N * b - T0[j])
+            scans("ga" + s, "m0" + s, "n0" + s, lo, TSCANS)
+            fin(A(BANKS[b][0], 0, N), less(t, N * b, N), A("m0" + s, lo + 15, lo + 16 * N, 16), A("n0" + s, lo + 15, lo + 16 * N, 16), [],
+                A("xw%d" % b, ZO, ZO + N))
+
+    def stay(t, j):
+        n, s = TN[j], str(j)
+        xs = team("xs%d" % (t % 2), j)
+        at, late = 15, []
+        if AGAIN[j]:
+            scans("ga" + s, "m0" + s, "n0" + s, 0, TSCANS * len(TEAMS[j]))
         else:
-            copy("g", A("t15" + s), A("ga" + s, 15, 16 * n, 16))
-            H = A(b1, 0, 2 * n)
-            for lo in (0, n):
-                mm(A(b1, lo, lo + n), ht, A("idn", 0, n, 1, n), True, True)
-            mm(part(KEEP, b), ht, A("idn" if t < 4 else "i1152", 0, n, 1, n), True, True)
-            tt(A("dn" + s), H, part("ek" + u, b, 2), OP.mult)
-            W = sixteens(256, 2 * n)
-            mms(W, [(I, A("mk")), (A("blk"), A("dn" + s))])
-            greatest(A("xl" + s, 0, n // 8), W)
-            xl, pl = A("xl" + s, 0, n // 16), A("xl" + s, n // 16, n // 8)
-            vcp(IND(A("ga" + s), pl), A("t15" + s))
-            tt(A("ga" + s, 15, 16 * n, 16), IND(A("xw" + s, ZO), xl), xs, OP.subtract)
-            act(A("gk" + s), IND(A("xw" + s, 0, XE), xl), AF.Copy)
-            scans("ga" + s, b, [n // 2] * 2)
-            fin(b0, b, less + [(I, xs)], 15, [], z)
-            mms(A(b2, 0, n), [(I, A("gk" + s)), (NEG, xs), (NEG, A("mx" + s, 14, 16 * n, 16))])
-            mms(A(b2, n, 2 * n), [(NEG, A("gk" + s)), (I, xs), (I, A("mn" + s, 14, 16 * n, 16))])
-            act(A("rl" + s), A(b2, 0, 2 * n), AF.Relu)
-            fin(b2, b, less + [(I, xs)], 14, [(HALF, A("rl" + s, 0, n)), (A("nhalf"), A("rl" + s, n, 2 * n))], part("f0", b))
-        mms(A(KEEP, NJ + U0[b], NJ + U0[b] + n), [(NEG, part("f0", b)), (I, z)])
+            at, late = 14, [(HALF, A("rl" + s, 0, n)), (A("nhalf"), A("rl" + s, n, 2 * n))]
+            mms(A(KEEP, NJ, NJ + n), [(I, A("gk" + s)), (NEG, xs), (NEG, A("m0" + s, at, 16 * n, 16))])
+            mms(A(KEEP, NJ + n, NJ + 2 * n), [(NEG, A("gk" + s)), (I, xs), (I, A("n0" + s, at, 16 * n, 16))])
+            act(A("rl" + s), A(KEEP, NJ, NJ + 2 * n), AF.Relu)
+        fin(A(KEEP, NJ, NJ + n), less(t, T0[j], n), A("m0" + s, at, 16 * n, 16), A("n0" + s, at, 16 * n, 16), late, team("f0", j))
+        for b in TEAMS[j]:
+            mms(part(KEEP, b), [(NEG, part("f0", b)), (I, A("xw%d" % b, ZO, ZO + N))])
 
     def hop(t, h, b):
-        n, s = NS[b], str(b)
-        b0, b1, b2 = BANKS[b]
-        z = A("xw" + s, ZO + n * (h - 1), ZO + n * h)
-        was, wl = [A("wl" + s, 8 * i, 8 * i + n // 16) for i in ((h - 2) % 3, h - 1)]
-        cm = A("cm", 0, n)
-        F = A(b1, 0, n)
-        mms(F, [(I, A("yc96", 0, n)), (A("b16"), z), (I, cm), (NEG, cm), (A("nb16"), z),
+        s = str(b)
+        b0, b1 = BANKS[b]
+        z = A("xw" + s, ZO + N * (h - 1), ZO + N * h)
+        was, wl = [A("wl" + s, 8 * i, 8 * i + N // 16) for i in ((h - 2) % 3, h - 1)]
+        cm = A("cm", 0, N)
+        F = A(b1, 0, N)
+        mms(F, [(I, A("yc96")), (A("b16"), z), (I, cm), (NEG, cm), (A("nb16"), z),
                 (A("i32k"), part("w1%d" % (t % 2), b) if h == 1 else A("ww" + s))])
         act(A("hot" + s), F, AF.Relu, A("p1c"), 2.0 ** 15)
-        W = sixteens(128 * b, n)
-        mms(W, [(I, A("mq", 0, n)), (A("blk"), A("hot" + s))])
-        tt(A("pq" + s), A("uq", *cls(t, b)) if h == 1 else IND(A("uq"), was), A("hot" + s), OP.min)
-        Q = A(b1, 0, n)
-        mms(Q, [(I, A("jc", 0, n)), (A("f8k"), A("pq" + s))])
+        W = sixteens(128 * b, N)
+        mms(W, [(I, A("mq")), (A("blk"), A("hot" + s))])
+        tt(A("pq" + s), A("uq", *cls(t, N * b, N)) if h == 1 else IND(A("uq"), was), A("hot" + s), OP.min)
+        Q = A(b0, 0, N)
+        mms(Q, [(I, A("jc")), (A("f8k"), A("pq" + s))])
         act(A("aa" + s), Q, AF.Abs, A("bc", h - 1, h))
         greatest(wl, W)
-        tt(A("ou" + s, n * (h - 1), n * h), IND(A("entt"), wl), A("aa" + s), OP.min)
+        lo = N * (h - 1)
+        tt(A("ou" + s, lo, lo + N), IND(A("entt"), wl), A("aa" + s), OP.min)
         act(A("bw" + s), IND(A("bt"), wl), AF.Identity, A("c25"))
-        gather("gb" + s, b, "ou" + s, n * (h - 1), HOP[h - 1][b])
-        scans("gb" + s, b, SCANS)
-        fin(b0, b, [(NEG, A("bw" + s))], 15, [], A("xw" + s, ZO + n * h, ZO + n * (h + 1)) if h < 3 else A("z3" + s))
+        gather(b, "ou" + s, lo, HOP[h - 1][b])
+        scans("gb" + s, "mx" + s, "mn" + s, 0, SCANS)
+        fin(A(b0, 0, N), [(NEG, A("bw" + s))], A("mx" + s, 15, 16 * N, 16), A("mn" + s, 15, 16 * N, 16), [],
+            A("xw" + s, ZO + N * h, ZO + N * (h + 1)) if h < 3 else A("z3" + s))
         if h < 3:
             act(A("ww" + s), IND(A("uw"), wl), AF.Identity, A("cw"), 0.0625)
         else:
             act(A("xv" + s), IND(A("xw" + s, XO, XG), wl), AF.Copy)
             ts(A("cl" + s), A("ou" + s), ZO - 1.0, XO - 1.0, OP.max, OP.min)
-            cl = [A("cl" + s, n * i, n * i + n) for i in range(3)]
-            mms(A(b2, 0, n), [(A("i15"), A("one", 0, n)), (A("b1m"), part("ct%d" % (t % 2), b)), (I, A("cm3", 0, n)),
-                              (NEG, A("cm3", 0, n)), (A("i8k"), A("ca"))] + [(A("nf8k"), c) for c in cl]
-                + [(I, A("cm2", 0, n)), (NEG, A("cm2", 0, n))] + [(A("f8k"), c) for c in cl]
+            cl = [A("cl" + s, N * i, N * i + N) for i in range(3)]
+            none = [(A("i15"), A("one", 0, N)), (A("b1m"), part("ct%d" % (t % 2), b)), (I, A("cm3")), (NEG, A("cm3"))]
+            mms(F, none * (not [a for j, a in zip(TEAMS, AGAIN) if b in j][0]) + [(A("i8k"), A("ca"))] + [(A("nf8k"), c) for c in cl]
+                + [(I, A("cm2")), (NEG, A("cm2"))] + [(A("f8k"), c) for c in cl]
                 + [(A("i8k"), A("cb")), (A("nb1"), A("xv" + s))], True, False)
 
     def effect(t, b):
-        n, s = NS[b], str(b)
-        D = A(BANKS[b][2], 0, n)
-        X = A(BANKS[b][1], 0, n)
-        mm(X, I, A("xv" + s), True, True)
-        tt(A("mz" + s), X, A("z3" + s), OP.max)
+        s = str(b)
+        D = A(BANKS[b][1], 0, N)
+        tt(A("mz" + s), A("xv" + s), A("z3" + s), OP.max)
         mms(D, [(A("nb1"), A("z3" + s)), (A("b2"), A("mz" + s))], False, True)
         ts(part("st", b), D, A("thc", t, t + 1), None, OP.is_le)
-        tt(part("sd", b), A(KEEP, NJ + U0[b], NJ + U0[b] + n), part("st", b), OP.mult)
+        tt(part("sd", b), part(KEEP, b), part("st", b), OP.mult)
+
+    def hits(by):
+        for j, n in enumerate(TN):
+            mm(team("p0", j), A("ht%d" % j, 0, 128, 1, n), A(by, 0, n, 1, n), True, True)
 
     def close(t):
         tt(A("gt%d" % t), IND(A("sd"), A("sndl", 6 * t, 6 * t + 6)), A("f0g"), OP.add)
-        ghosts = [A("xw%d" % b, XG + 96 * t, XG + 96 * (t + 1)) for b in range(NB)]
-        send(t, [A("gt%d" % t)], ghosts[0], (free(t, ghosts[0]),))
-        tt(A("xw0", *cls(t, None, XO)), A("f0"), A("sd"), OP.add)
-        tt(A("hs"), A(KEEP, 0, NJ), A("st"), OP.mult)
-        act(A("xw1", *cls(t, None, XO)), A("xw0", *cls(t, None, XO)), AF.Copy)
-        for bank, tab, by in (("p4", "entt", "ixo"), ("p5", "yef", "i1152")):
+        ghosts = A("xw0", XG + 96 * t, XG + 96 * (t + 1))
+        send(t, A("gt%d" % t), ghosts, (free(t, ghosts),))
+        tt(A("xw0", *cls(t, base=XO)), A("f0"), A("sd"), OP.add)
+        hits("idn")
+        tt(A("hs"), A("p0", 0, NJ), A("st"), OP.mult)
+        for b in range(1, NB):
+            copy("g", A("xw%d" % b, *cls(t, base=XO)), A("xw0", *cls(t, base=XO)))
+        for bank, tab, by in (("p1", "entt", "ixo"), ("p3", "yef", "i1152")):
             E = A(bank, 0, NJ)
             mms(E, [(A("idf"), A(tab, *cls(t))), (A(by), A("hs"))])
             act(A(tab, *cls(t)), E, AF.Copy)
@@ -749,68 +771,69 @@ def rank_program(g, core, T, topo):
         vcp(A("rri"), rr)
         ts(A("rrj"), A("rri"), 31, None, OP.bitwise_and)
         tt(A("thc", t + 1, t + 2), A("rrj"), A("tha", t + 1, t + 2), OP.add)
-        copy("g", ghosts[1], ghosts[0])
 
     def store(t, b):
-        n = NS[b]
-        tt(part("hs", b), part(KEEP, b), part("st", b), OP.mult)
-        tt(A("yef", *cls(t, b)), A("yef", *cls(t, b)), part("hs", b), OP.add)
-        tt(A("xw0", *cls(t, b, XO)), part("f0", b), part("sd", b), OP.add)
-        cols = slice(4 * U0[b], 4 * (U0[b] + n))
+        tt(part("hs", b), part("p0", b), part("st", b), OP.mult)
+        tt(A("yef", *cls(t, N * b, N)), A("yef", *cls(t, N * b, N)), part("hs", b), OP.add)
+        tt(A("xw0", *cls(t, N * b, N, XO)), part("f0", b), part("sd", b), OP.add)
+        cols = slice(4 * N * b, 4 * N * (b + 1))
         xc = slice(XO + cols.start, XO + cols.stop)
         add("s", lambda e: e.dma_start(out=T.yx[:, cols], in_=T.xw0[:, xc]),
             [("xw0", xc.start, xc.stop, 1)], [], (0.1, 0, False), 2.0, "o%d" % (NB + b), 16, True)
         add("y", lambda e: e.dma_start(out=T.ye[:, cols], in_=T.yef[:, cols]),
             [("yef", cols.start, cols.stop, 1)], [], (0.1, 0, False), 2.0, "o%d" % b, 16, True)
 
-    def rounds(which):
-        for t in which:
-            u = str(t % 2)
-            for b, n in enumerate(NS):
-                label("gather", b)
-                w = n // len(JUDGE[b])
-                for p, q in enumerate(JUDGE[b]):
-                    lo = U0[b] + w * p
-                    out, src = A("ga%d" % b, 16 * w * p, 16 * w * (p + 1)), IND(A("xw%d" % b, 0, XE), A("eu" + u, lo, lo + w))
-                    if q == "s":
-                        act(out, src, AF.Copy)
-                    else:
-                        tt(out, src, A("xr" + u, 16 * lo, 16 * (lo + w)), OP.subtract)
+    for t in range(5):
+        step[2] = t
+        u = str(t % 2)
+        label("landed")
+        lo, hi = (XG + 96 * (t - 1), XG + 96 * t) if t else (XG, XE)
+        for b in range(1, NB):
+            copy("g", A("xw%d" % b, lo, hi), A("xw0", lo, hi))
+        for j in range(len(TEAMS)):
+            label("gather", j)
+            lo = 0
+            for q, w in JUDGE[j]:
+                at = T0[j] + lo
+                out, what = A("ga%d" % j, 16 * lo, 16 * (lo + w)), IND(A("xw0", 0, XE), A("eu" + u, at, at + w))
+                if q == "s":
+                    act(out, what, AF.Copy)
+                else:
+                    tt(out, what, A("xr" + u, 16 * at, 16 * (at + w)), OP.subtract)
+                lo += w
+        for j in range(len(TEAMS)):
+            label("score", j)
+            score(t, j)
+            label("least", j)
+            trial(t, j)
+        for j in range(len(TEAMS)):
+            label("stay", j)
+            stay(t, j)
+        if t < 4:
+            label("ahead")
+            repeat(t + 1, "g")
+            lists(t + 1)
+            act(A("w1%d" % ((t + 1) % 2)), A("uw", *cls(t + 1)), AF.Identity, A("cw"), 0.0625)
+            act(A("f0g"), IND(A("f0"), A("sndl", 6 * t, 6 * t + 6)), AF.Copy)
+        for h in range(1, 4):
             for b in range(NB):
-                label("score", b)
-                score(t, b)
-                label("least", b)
-                trial(t, b)
-            if t < 4:
-                label("ahead")
-                repeat(t + 1, "g")
-                lists(t + 1)
-                act(A("w1%d" % ((t + 1) % 2)), A("uw", *cls(t + 1)), AF.Identity, A("cw"), 0.0625)
-                act(A("f0g"), IND(A("f0"), A("sndl", 6 * t, 6 * t + 6)), AF.Copy)
-            for h in range(1, 4):
-                for b in range(NB):
-                    label("hop", h, b)
-                    hop(t, h, b)
+                label("hop", h, b)
+                hop(t, h, b)
+        for b in range(NB):
+            label("effect", b)
+            effect(t, b)
+        if t < 4:
+            label("end")
+            close(t)
+        else:
+            label("out")
+            hits("i1152")
             for b in range(NB):
-                label("effect", b)
-                effect(t, b)
-            if t < 4:
-                label("end")
-                close(t)
-            else:
-                label("out")
-                for b in range(NB):
-                    store(t, b)
+                store(t, b)
 
+    _edges(ops)
     if "order" not in PLAN:
-        rounds((0, 1, 4))
-        few = [dict(o) for o in ops]
-        del ops[setup:]
-        rounds(range(5))
-        PLAN["order"] = _plan(few, ops)
-    else:
-        rounds(range(5))
-        _edges(ops)
+        PLAN["order"] = _plan(ops)
     needed = [False] * len(ops)
     for o in ops:
         for j in o["pre"]:

import math
import numpy as np
from concourse.bass import DstId, RemoteDMATransfer
from concourse.mybir import AluOpType as OP, ActivationFunctionType as AF, AxisListType as AX

V, NG, NJ = 768, 384, 192
NB, N = 3, 64
TEAMS = [(0,), (1,), (2,)]
TN = [N * len(_t) for _t in TEAMS]
T0 = [N * _t[0] for _t in TEAMS]
NM = max(TN)
JUDGE = [[("s", 32), ("v", 32)], [("v", 64)], [("v", 64)]]
AGAIN = [None, None, [("s", 32), ("s", 32)]]
CUTS = [2, 2, 2]
EK = []
for _j, _w in enumerate(TN):
    _lo = sum(_x * (1 if _a else 2) for _x, _a in zip(TN[:_j], AGAIN))
    EK.append((_lo, None) if AGAIN[_j] else (_lo + _w, _lo) if _j == 0 else (_lo, _lo + _w))
PARTS = [("s", 32), ("s", 22), ("v", 10)]
HOP = [[PARTS] * NB] * 3
SCANS = [32, 32]
TSCANS = [64]
FIRST = 2.0
LATE = ("i1152", "i15", "i8k", "nb1", "b2", "b1m", "nf8k", "nhalf")
START = "vsvgvs"
BANKS = [("p0", "p1"), ("p2", "p3"), ("p4", "p5")]
DBANKS = [("p1", "p5"), ("p3", "p5"), ("p5", "p5")]
KEEP, LIST = "p6", "p7"
ZO, XO = 1152, 1664
XG = XO + V
XE = XG + NG
GAP = XO - ZO
MAGIC = 12582912.0
WO = 1040.0
BF2 = "bfloat16"
SCRATCH = {}
WHERE = {}


def _buf(name, cols, dtype=BF2, where="sbuf", rows=128, pool=True):
    if not pool or where != "sbuf" or rows != 128 or cols > 384:
        SCRATCH[name] = (where, [rows, cols], dtype)
        WHERE[name] = (name, 0, cols, dtype)
        return
    p = "pool_" + dtype
    lo = SCRATCH[p][1][1] if p in SCRATCH else 0
    SCRATCH[p] = ("sbuf", [128, lo + (cols + 15) // 16 * 16], dtype)
    WHERE[name] = (p, lo, cols, dtype)


TWICE = [_t[0] for _t, _a in zip(TEAMS, AGAIN) if not _a]
for _b in range(NB):
    _buf("xw%d" % _b, XE + ZO if _b in TWICE else XE)
    for _n in ("gb", "mx", "mn"):
        _buf("%s%d" % (_n, _b), 16 * N)
    for _n in ("pq", "xv", "z3", "mz"):
        _buf("%s%d" % (_n, _b), N)
    for _n, _k in (("hot", 1), ("ww", 1), ("bw", 1), ("cl", 3)):
        _buf("%s%d" % (_n, _b), _k * N, "float16")
    _buf("aa%d" % _b, N, "float32")
    for _n, _k in (("ou", 3 * N), ("wl", 24)):
        _buf("%s%d" % (_n, _b), _k, "uint16")
for _b, _w in enumerate(TN):
    for _n in ("ga", "mt", "m0", "n0"):
        _buf("%s%d" % (_n, _b), 16 * _w)
    for _n, _k in (("t15", _w), ("gk", _w), ("rl", 2 * _w), ("ht", 128)):
        _buf("%s%d" % (_n, _b), _k)
    _buf("dn%d" % _b, 2 * _w, "float16")
    _buf("r1%d" % _b, 144, "float32")
    _buf("mb%d" % _b, 128, "float32")
    _buf("xl%d" % _b, 16, "uint16")
for _n in range(2):
    _buf("eu%d" % _n, NJ, "uint16")
    _buf("ct%d" % _n, NJ)
    _buf("xs%d" % _n, NJ)
    _buf("ek%d" % _n, 2 * NJ, "float16")
    _buf("w1%d" % _n, NJ, "float16")
    _buf("xr%d" % _n, 16 * NJ)
for _n in ("f0", "st", "sd", "hs"):
    _buf(_n, NJ)
for _n in ("enti", "usri", "uq"):
    _buf(_n, V, "int32")
for _n in ("entt", "yef", "uw"):
    _buf(_n, V, "float32")
for _n, _w in (("bt", V), ("lt", V), ("rm", 16 * max(SCANS + TSCANS)), ("rn", 16 * max(SCANS + TSCANS))):
    _buf(_n, _w)
_buf("sndi", 24, "int32", "sbuf", 128, False)
_buf("sndu", 24, "uint16")
_buf("sndl", 24, "uint16")
_buf("thi", 5, "int32", "sbuf", 8)
_buf("thf", 5, "float32", "sbuf", 8)
for _n, _w in (("tha", 5), ("thc", 5), ("rr", 1), ("pf", 4), ("bk", 4), ("py", 1), ("p1c", 1), ("c25", 1), ("mgc", 1), ("c256", 1), ("cw", 1),
               ("n1k", 1), ("cz", 1), ("pg", 1), ("c1k", 1), ("top", 128), ("cap", 128), ("idf", 128)):
    _buf(_n, _w, "float32")
for _n, _w in (("rri", 1), ("rrj", 1), ("ji", NM), ("jj", NM), ("pi", 4), ("pj", 4), ("pk", 1)):
    _buf(_n, _w, "int32")
for _n, _w, _d in (("ca", N, "float16"), ("cb", N, "float16"), ("bc", 4, "float32"), ("bi", 4, "float32"), ("mk", 2 * NJ, BF2)):
    _buf(_n, _w, _d)
_buf("gs0", NG, BF2, "sbuf", 128, False)
_buf("f0g", 96, BF2, "sbuf", 128, False)
for _n in range(4):
    _buf("gt%d" % _n, 96, BF2, "sbuf", 128, False)
for _n in ("one", "zero", "i1k", "idn", "half", "nhalf", "neg", "ict", "ik", "ig", "ixo", "ixe", "i1152", "i15", "blkh", "blk", "b16", "nb16",
           "nb1", "b2", "i32k", "w16", "b1m", "i8k", "f8k", "nf8k"):
    _buf(_n, 128)
for _n in ("oe", "ee0", "ee"):
    _buf(_n, 128, "float32", "sbuf", 8)
for _n in ("j16", "mask", "cm", "cq"):
    _buf(_n, NM)
for _n in ("yc96", "jc", "mq", "cm2", "cm3"):
    _buf(_n, N)
for _n in range(8):
    _buf("p%d" % _n, 512, "float32", "psum")
SCRATCH[LIST] = ("psum", [128, 32, 16], "float32")
LOADS = ["snd", "xa", "ent", "yc", "bn", "usr", "th"]
COPIES = [("yc", _b, XE) for _b in TWICE] + [(_n, _b, _c) for _b in range(1, NB) for _n, _c in (("xa", XO), ("yc", 0))]
SEMAPHORES = (["sv", "ss", "st", "sg"] + ["o%d" % n for n in range(2 * NB)] + ["ld_" + n for n in LOADS] + ["cp%d" % n for n in range(len(COPIES))]
              + ["arr%d" % t for t in range(5)] + ["left%d" % t for t in range(5)]
              + ["free%d" % t for t in range(4)] + ["told%d" % t for t in range(4)])
QS = {"v": "sv", "s": "ss", "t": "st", "g": "sg"}
PLAN = {}


def _overlap(a, b):
    if a[1] >= b[2] or b[1] >= a[2]:
        return False
    return not (a[3] > 1 and a[3] == b[3] and (a[1] - b[1]) % a[3])


def _bank(r):
    return r[0][0] == "p" and r[0][1:].isdigit()


def _edges(ops):
    hist = {}
    for i, o in enumerate(ops):
        pre = {}
        both = [(False, r) for r in o["rd"]] + [(True, r) for r in o["wr"]]
        for wr, r in both:
            for (r2, j, w2) in hist.get(r[0], ()):
                if j == i or not (_bank(r) or ((wr or w2) and _overlap(r, r2))):
                    continue
                pre[j] = pre.get(j, False) or ops[j]["q"] != o["q"] or ((wr or w2) and o["q"] != "t") or ops[j]["dma"]
        for j in o["after"]:
            pre[j] = True
        for wr, r in both:
            h = hist.setdefault(r[0], [])
            if _bank(r):
                if h and ops[h[-1][1]]["q"] != o["q"]:
                    h[:] = [e for e in h if e[1] == i or ops[e[1]]["q"] != o["q"]]
            elif wr:
                h[:] = [e for e in h if e[1] == i or not (r == e[0] or (r[3] == 1 and r[1] <= e[0][1] and e[0][2] <= r[2]))]
            h.append((r, i, wr))
        o["pre"] = pre


def _cost(o, m):
    f, n, gath = o["cost"]
    if o["q"] == "t":
        return m[5] * (0.02 * m[0] + n * 1e-3 * m[1])
    return f * m[0] + max(64, n * m[2] * gath if gath else n) * 1.0e-3 * m[1] if n else f


MODELS = [(1.05, 0.9, 1.4, 0.135, 0.95, 0.72), (1.0, 1.15, 1.1, 0.1, 0.9, 0.9), (1.05, 0.85, 1.9, 0.19, 0.9, 0.8)]
STEPS = {2: 260000, 0: 25000, 4: 15000}
HEAT = {2: 0.003, 0: 0.0007, 4: 0.0007}
SEED, LEAD = 3, 1.0


def _pieces(calls):
    head, ops = [], []
    for i, o in enumerate(calls):
        if o["q"] == "t" and i - 1 in o["pre"] and calls[i - 1]["q"] == "t" and all(
                not w or calls[j]["once"] or calls[j]["round"] < o["round"] or head[j] in ops[-1]["pre"] for j, w in o["pre"].items()):
            p = ops[-1]
        else:
            p = {"q": o["q"], "key": o["key"], "lag": o["lag"], "round": o["round"], "batch": o["batch"], "calls": [], "pre": {}}
            ops.append(p)
        head.append(len(ops) - 1)
        p["calls"].append(i)
        for j, w in o["pre"].items():
            if head[j] != len(ops) - 1:
                p["pre"][head[j]] = p["pre"].get(head[j], False) or w
    return ops


def _shop(calls, pieces, t, models):
    own = [i for i, o in enumerate(pieces) if o["round"] == t]
    at = dict((i, k) for k, i in enumerate(own))
    ops = [pieces[i] for i in own]
    s = {"ops": ops, "queue": ["vstgyxz".index(o["q"]) for o in ops], "succ": [[] for _ in ops],
         "pre": [[at[j] for j in o["pre"] if j in at] for o in ops],
         "wait": [[at[j] for j, w in o["pre"].items() if w and j in at] for o in ops],
         "cost": [[sum(_cost(calls[i], m) for i in o["calls"]) for o in ops] for m in models],
         "lag": [[o["lag"] * m[4] + m[3] for o in ops] for m in models]}
    for i, l in enumerate(s["pre"]):
        for j in l:
            s["succ"][j].append(i)
    return s


def _listed(s, known):
    ops, queue, cost, lag = s["ops"], s["queue"], s["cost"][0], s["lag"][0]
    n = len(ops)
    succ = [list(l) for l in s["succ"]]
    last = {}
    for i in sorted((i for i in range(n) if ops[i]["key"] in known), key=lambda i: known[ops[i]["key"]]):
        if queue[i] in last:
            succ[last[queue[i]]].append(i)
        last[queue[i]] = i
    pri = [0.0] * n
    for i in range(n - 1, -1, -1):
        pri[i] = -known[ops[i]["key"]] if ops[i]["key"] in known else cost[i] + lag[i] + max([pri[j] for j in s["succ"][i]] + [-99.0])
    if not known:
        pri = [p - LEAD * o["batch"] for p, o in zip(pri, ops)]
    left, rdy, free, order = [0] * n, [0.0] * n, [0.0] * 7, []
    for l in succ:
        for j in l:
            left[j] += 1
    cand = [i for i in range(n) if not left[i]]
    while cand:
        now, i = min((max(rdy[i], free[queue[i]]), i) for i in cand)
        q = queue[i]
        i = max((j for j in cand if queue[j] == q and rdy[j] <= now + 0.1), key=lambda j: pri[j])
        cand.remove(i)
        order.append(i)
        now = max(now, rdy[i])
        free[q] = now + cost[i]
        for j in succ[i]:
            rdy[j] = max(rdy[j], free[q] + lag[i] if i in s["wait"][j] else now)
            left[j] -= 1
            if not left[j]:
                cand.append(j)
    assert len(order) == n
    return order


def _improve(s, order, steps, heat, rng):
    queue, pre, succ, wait, cost, lag = [s[k] for k in ("queue", "pre", "succ", "wait", "cost", "lag")]
    n, nm = len(order), len(cost)
    work = [list(zip(range(n), wait, cost[m], lag[m])) for m in range(nm)]
    prev, nxt = [n] * (n + 1), [n] * (n + 1)

    def link(seg, last, tail):
        last = dict(last)
        for x in seg:
            p = last[queue[x]]
            prev[x], nxt[p], last[queue[x]] = p, x, x
        for q, x in tail.items():
            nxt[last[q]], prev[x] = x, last[q]

    def run(a, m, end, fin):
        w = work[m]
        for x in order[a:]:
            i, js, c, l = w[x]
            t = end[prev[i]]
            for j in js:
                if fin[j] > t:
                    t = fin[j]
            end[i] = t = t + c
            fin[i] = t + l
        return end, fin

    def held(m):
        end, fin = times[m]
        i, out = fin.index(max(fin)), []
        while i < n:
            at, j = end[i] - cost[m][i] - 1e-9, prev[i]
            if j < n and end[j] >= at:
                if j not in pre[i]:
                    out.append((j, i))
                i = j
            else:
                i = ([j for j in wait[i] if fin[j] >= at] + [n])[0]
        return out

    link(order, dict((q, n) for q in queue), dict((q, n) for q in queue))
    times = [run(0, m, [0.0] * (n + 1), [0.0] * n) for m in range(nm)]
    unit = [max(x[1]) for x in times]
    vals, best, kept, arcs = [1.0] * nm, float(nm), list(order), None
    for step in range(steps):
        if step % 1000 == 0:
            dice = rng.rand(1000, 6).tolist()
        d = dice[step % 1000]
        arcs = arcs or [held(m) for m in range(nm)]
        up, pairs = d[0] < 0.5, arcs[int(d[1] * nm)]
        if pairs and d[2] < 0.8:
            u, v = pairs[int(d[3] * len(pairs))]
            far = int(d[4] * 10) + 1 if d[4] < 0.3 else 0
        else:
            u = v = int(d[3] * n)
            far = 1 + int(d[4] * 2)
        for _k in range(far):
            u, v = (prev[u] if u < n else n, v) if up else (u, nxt[v] if v < n else n)
        if u == n or v == n:
            continue
        a, b = order.index(u), order.index(v)
        seg = order[a:b + 1]
        edges = pre if up else succ
        x = v if up else u
        take, need = set([x]), set(edges[x])
        for x in (seg[-2::-1] if up else seg[1:]):
            if x in need:
                take.add(x)
                need.update(edges[x])
        if u in take and v in take:
            continue
        new = [x for x in seg if (x in take) == up] + [x for x in seg if (x in take) != up]
        tail = dict((queue[x], nxt[x]) for x in seg)
        head = dict((queue[x], prev[x]) for x in seg[::-1])
        order[a:b + 1] = new
        link(new, head, tail)
        bar = -heat * nm * (1 - step / steps) ** 2 * math.log(d[5] + 1e-300) + 1e-12
        tot, got, got_vals = 0.0, [], []
        for m in range(nm):
            x = run(a, m, times[m][0][:], times[m][1][:])
            got.append(x)
            got_vals.append(max(x[1]) / unit[m])
            tot += got_vals[m] - vals[m]
            if tot > bar + (0.004 if m < nm - 1 else 0.0):
                order[a:b + 1] = seg
                link(seg, head, tail)
                break
        else:
            times, vals, arcs = got, got_vals, None
            if sum(vals) < best:
                best, kept = sum(vals), list(order)
    order[:] = kept
    link(order, dict((q, n) for q in queue), dict((q, n) for q in queue))
    end = run(0, 0, [0.0] * (n + 1), [0.0] * n)[0]
    return kept, dict((s["ops"][i]["key"], end[i] - cost[0][i] + 1e-7 * k) for k, i in enumerate(kept))


def _plan(calls):
    pieces = _pieces(calls)
    rng = np.random.RandomState(SEED)
    known, orders = {}, {}
    for t in (2, 0, 4, 1, 3):
        s = _shop(calls, pieces, t, MODELS)
        order = _listed(s, known)
        if t in STEPS:
            order, starts = _improve(s, order, STEPS[t], HEAT[t], rng)
            known = known or starts
        orders[t] = [i for p in order for i in s["ops"][p]["calls"]]
    return [i for t in range(5) for i in orders[t]]


def rank_program(g, core, T, topo):
    rank = T.rank_of(core)
    if rank is None:
        return
    ops = []
    names = {}
    step = [None, 0, 0]
    eng = {"v": g.vector, "s": g.scalar, "t": g.tensor, "g": g, "y": g.sync}

    def label(*x):
        step[:2] = [x, 0]

    def add(q, fn, rd, wr, cost, lag=0.0, sem=None, amount=1, dma=False, after=()):
        key = names.setdefault((step[0], step[1]), len(names))
        step[1] += 1
        ops.append({"q": q, "fn": fn, "key": key, "once": step[0] is None, "round": step[2],
                    "batch": step[0][-1] if step[0] and len(step[0]) > 1 else 0, "rd": rd, "wr": wr,
                    "cost": cost, "lag": lag, "sem": sem, "amount": amount, "dma": dma, "after": list(after), "remote": False})
        return len(ops) - 1

    def A(name, lo=0, hi=None, step=1, rows=None):
        buf, o, cols, _d = WHERE[name]
        if hi is None:
            hi = cols
        c = slice(o + lo, o + hi) if step == 1 else slice(o + lo, o + hi, step)
        ap = T[buf][:, c] if rows is None else T[buf][0:rows, c]
        return (ap, [(name, lo, hi, step)], (hi - lo + step - 1) // step, False)

    def IND(w, off):
        return (w[0].indirect(off[0]), w[1] + off[1], 16 * off[2], True)

    def regs(*xs):
        out = []
        for x in xs:
            if isinstance(x, tuple):
                out += x[1]
        return out

    def val(x):
        return x[0] if isinstance(x, tuple) else x

    def kind(x):
        return WHERE[x[1][0][0]][3]

    def half(*xs):
        return 0.5 if all(kind(x) in ("bfloat16", "float16", "uint16") for x in xs) else 1

    def vc(n, gath=False):
        return (0.055, n, gath)

    def tt(out, a, b, op):
        n = out[2] * (1 if a[3] or _bank(a[1][0]) or _bank(b[1][0]) else 2)
        return add("v", lambda e: e.tensor_tensor(out=out[0], in0=a[0], in1=b[0], op=op), regs(a, b), regs(out), vc(n, a[3]))

    def ts(out, a, s1, s2, op0, op1=None):
        if op1 is None:
            fn = lambda e: e.tensor_scalar(out=out[0], in0=a[0], scalar1=val(s1), scalar2=None, op0=op0)
        else:
            fn = lambda e: e.tensor_scalar(out=out[0], in0=a[0], scalar1=val(s1), scalar2=val(s2), op0=op0, op1=op1)
        return add("v", fn, regs(a, s1, s2), regs(out), vc(out[2] * half(out, a)))

    def vcp(out, a):
        fn = lambda e: e.tensor_copy(out=out[0], in_=a[0])
        if out[3]:
            return add("v", fn, regs(a) + out[1][1:], out[1][:1], vc(out[2], 2.4))
        return add("v", fn, regs(a), regs(out), vc(out[2], True) if a[3] else vc(out[2] * half(out, a)))

    def scan(out, d0, d1, op0, op1):
        return add("v", lambda e: e.tensor_tensor_scan(out=out[0], data0=d0[0], data1=d1[0], initial=0.0, op0=op0, op1=op1),
                   regs(d0, d1), regs(out), vc(out[2] * half(out, d0, d1)))

    def sixteens(lo, n):
        return (T[LIST][:, lo // 16:(lo + n) // 16, :], [(LIST, lo, lo + n, 1)], n, False)

    def greatest(out, a):
        return add("v", lambda e: e.tensor_reduce(out=out[0], in_=a[0], axis=AX.X, op=OP.max), regs(a), regs(out), vc(a[2]))

    def fill(out, x):
        return add("v", lambda e: e.memset(out[0], x), [], regs(out), vc(out[2] * half(out)))

    def act(out, a, func, bias=None, scale=1.0):
        if bias is None:
            fn = lambda e: e.activation(out=out[0], in_=a[0], func=func, scale=val(scale))
        else:
            fn = lambda e: e.activation(out=out[0], in_=a[0], func=func, bias=val(bias), scale=val(scale))
        return add("s", fn, regs(a, bias, scale), regs(out), (0.065, out[2], a[3]))

    def mm(out, l, r, start, stop):
        return add("t", lambda e: e.matmul(out[0], l[0], r[0], start, stop), regs(l, r), regs(out),
                   (0.03, max(64, r[2]) * (4 if kind(r) == "float32" else 1), False))

    def mms(out, pairs, start=True, stop=True):
        for i, (l, r) in enumerate(pairs):
            mm(out, l, r, start and i == 0, stop and i == len(pairs) - 1)

    def sel(out, a, pattern, op, base, cm, other=0.0):
        return add("g", lambda e: e.affine_select(out=out[0], in_=a[0], pattern=pattern, compare_op=op, fill=other, base=base,
                                                 channel_multiplier=cm), regs(a), regs(out), (0.17, 2 * out[2], False))

    def copy(q, out, a):
        if q == "g":
            return sel(out, a, [[0, out[2]]], OP.is_ge, 0, 0)
        return vcp(out, a) if q == "v" else act(out, a, AF.Copy)

    def iota(out, pattern, base, cm):
        if kind(out) != "int32":
            fn = lambda e: e.iota(out[0], pattern=pattern, base=base, channel_multiplier=cm, allow_small_or_imprecise_dtypes=True)
        else:
            fn = lambda e: e.iota(out[0], pattern=pattern, base=base, channel_multiplier=cm)
        return add("g", fn, [], regs(out), (0.13, 2 * out[2], False))

    def load(q, name, out, lag, sem=None, after=()):
        return add(q, lambda e: e.dma_start(out=out[0], in_=T[name][:, :]), [], regs(out), (0.1, 0, False), lag,
                   sem or "ld_" + name, 16, True, after)

    dst = T.cores[(rank - 1) % len(T.cores)]
    src = T.cores[(rank + 1) % len(T.cores)]
    rid, pid = topo.addr(dst, core)
    es = topo.engines(core, dst)
    mask = topo.mask(core, dst)
    n_in = len(topo.engines(src, core))

    back, bid = topo.addr(src, core)
    one_engine = 1 << topo.engines(core, src)[0]

    def free(slot, land):
        j = add("g", lambda e: e.remote_sem_update(T.sem["free%d" % slot], T.sem["told%d" % slot], bid, back, one_engine),
                [], regs(land), (0.3, 0, False), 1.0, "told%d" % slot, 1)
        ops[j]["remote"] = True
        return add("z", None, [], [], (0.0, 0, False), 1.0, "free%d" % slot, 1, True, (j,))

    def send(slot, what, land, after=()):
        j = add("g", lambda e: e.remote_dma(land[0], what[0], T.sem["arr%d" % slot], T.sem["left%d" % slot], pid, rid, mask),
                regs(what), [], (0.3, 0, False), 1.0, "left%d" % slot, len(es), False, after)
        ops[j]["remote"] = True
        add("x", None, [], regs(land), (0.0, 0, False), 1.5 + FIRST * (slot == 4), "arr%d" % slot, n_in, True, (j,))
        return j

    def cls(t, lo=0, n=NJ, base=0):
        return base + 4 * lo + t % 4, base + 4 * (lo + n), 4

    def part(name, b):
        return A(name, N * b, N * b + N)

    def team(name, j):
        return A(name, T0[j], T0[j] + TN[j])

    own0 = A("xw0", XO, XG)
    load("y", "snd", A("sndi"), 1.5)
    xa = load("s", "xa", own0, 2.0)
    load("y", "ent", A("enti"), 3.0)
    load("y", "yc", A("xw0", 0, ZO), 2.0, None, (xa,))
    for c in range(4):
        ts(A("sndu", 6 * c, 6 * c + 6), A("sndi", 6 * c, 6 * c + 6), 4, c, OP.mult, OP.add)
    act(A("gs0"), IND(own0, A("sndu")), AF.Copy)
    first = send(4, A("gs0"), A("xw0", XG, XE))
    vcp(A("sndl"), A("sndi"))
    fill(A("one"), 1.0)
    for name, out, lag in (("usr", A("usri"), 2.5), ("bn", A("bt"), 3.2), ("th", A("thi"), 3.3)):
        load("y", name, out, lag, None, (first,))
    for i, (name, b, lo) in enumerate(COPIES):
        load("y", name, A("xw%d" % b, lo, lo + (V if name == "xa" else ZO)), 4.0 + 0.6 * i, "cp%d" % i, (first,))
    for b in TWICE:
        fill(A("xw%d" % b, ZO, XO), 0.0)

    iota(A("oe"), [[0, 128]], 1, 0)
    sel(A("idn"), A("one"), [[-1, 128]], OP.is_equal, 0, 1)
    sel(A("blkh"), A("one"), [[-16, 8], [0, 16]], OP.is_ge, 0, 1)
    sel(A("blk"), A("blkh"), [[16, 8], [0, 16]], OP.is_ge, 15, -1)
    sel(A("ee0"), A("oe"), [[1, 128]], OP.is_ge, 0, -16)
    sel(A("ee"), A("ee0"), [[-1, 128]], OP.is_ge, 15, 16)
    iota(A("ji"), [[1, NM]], 128, -1)
    iota(A("jc"), [[1, N]], 0, 0)
    iota(A("pi"), [[0, 4]], 0, 1)
    for name, x in (("top", 131071.0), ("cap", 65535.0)):
        act(A(name), A("one"), AF.Identity, None, 0.0)
        ts(A(name, 0, 128, 16), A("jc", 0, 8), 131072.0, x, OP.mult, OP.add)
    ts(A("pj"), A("pi"), 15, None, OP.bitwise_and)
    vcp(A("pf"), A("pj"))
    ts(A("pk"), A("pi", 0, 1), 112, None, OP.bitwise_and)
    ts(A("pg"), A("pk"), 8192.0, 32768.0, OP.mult, OP.add)
    for name, of, x in (("neg", "idn", -1.0), ("ict", "idn", -32768.0), ("ixe", "idn", -XE / 2), ("idf", "idn", 1.0),
                        ("ik", "idn", A("pf", 0, 1)), ("ig", "idn", A("pg")), ("w16", "blk", 16.0)):
        act(A(name), A(of), AF.Identity, None, x)
    iota(A("zero"), [[0, 128]], 0, 0)
    for name, x in (("i1k", 1024.0), ("half", 0.5), ("nhalf", -0.5), ("i1152", 1152.0), ("ixo", -float(XO)), ("i15", 2.0 ** 19),
                    ("i32k", 2.0 ** -15), ("i8k", 8192.0)):
        if name in LATE:
            sel(A(name), A("zero"), [[-1, 128]], OP.not_equal, 0, 1, x)
        else:
            ts(A(name), A("idn"), x, None, OP.mult)
    for name, x in (("b16", 0.0625), ("nb16", -0.0625), ("nb1", -1.0), ("b2", 2.0), ("b1m", -2.0 ** 19), ("f8k", 8192.0),
                    ("nf8k", -8192.0)):
        if name in LATE:
            sel(A(name), A("zero"), [[16, 8], [0, 16]], OP.is_gt, 0, -1, x)
            sel(A(name), A(name), [[16, 8], [0, 16]], OP.is_ge, 15, -1)
        else:
            ts(A(name), A("blk"), x, None, OP.mult)
    ts(A("py"), A("pf", 0, 1), -0.0625, -15.0 / 32, OP.mult, OP.add)
    act(A("p1c"), A("pf", 0, 1), AF.Identity, None, 2048.0)
    ts(A("bk", 0, 1), A("pf", 0, 1), -8192.0, None, OP.mult)
    ts(A("jj"), A("ji"), 15, None, OP.bitwise_and)
    ts(A("mask"), A("jj"), 0, -4096.0, OP.not_equal, OP.mult)
    iota(A("j16"), [[16, NM]], 0, 0)
    iota(A("bi"), [[N, 4]], ZO, 0)
    act(A("bc"), A("bi"), AF.Identity, A("bk", 0, 1))
    c0 = (48 * (ZO - 1) + 3 * N + 3) % GAP
    ts(A("ca"), A("jc"), 3.0, c0 - (GAP - 1) / 2, OP.mult, OP.add)
    ts(A("cb"), A("jc"), -3.0, -float(c0), OP.mult, OP.add)
    for j, n in enumerate(TN):
        iota(A("r1%d" % j, 128, 144), [[0, 16]], 1048576, 0)
        mid, lo = EK[j]
        if not AGAIN[j]:
            for i in range(2):
                act(A("ek%d" % i, lo, lo + n), A("one", 0, n), AF.Identity, None, A("pf", 0, 1))
            mms(A("p6", lo, lo + n), [(A("idn"), A("mask", 0, n)), (A("idn"), A("j16", 0, n))])
            mms(A("p6", mid, mid + n), [(A("idn"), A("mask", 0, n)), (A("i1k"), A("one", 0, n))])
    wide = 2 * sum(n for n, a in zip(TN, AGAIN) if not a)
    act(A("mk", 0, wide), A("p6", 0, wide), AF.Copy)
    ts(A("mq"), A("mask", 0, N), -WO, None, OP.add)
    act(A("yc96"), A("one", 0, N), AF.Identity, None, A("py"))
    for name, x in (("cm", MAGIC), ("cm2", MAGIC * 8192 * GAP), ("cm3", MAGIC * 2 ** 24), ("cq", -0.25)):
        n = WHERE[name][2]
        sel(A(name), A("one", 0, n), [[0, n]], OP.is_gt, 0, 0, x)
    for name, x in (("c256", 256.0), ("cz", 0.5 - ZO), ("mgc", -MAGIC), ("n1k", -1024.0), ("cw", WO - 15.0 / 32), ("c25", 0.25),
                    ("c1k", 1024.0)):
        act(A(name), A("one", 0, 1), AF.Identity, None, x)
    for name, x in (("rm", -512.0), ("rn", 512.0)):
        fill(A(name), 0.0)
        act(A(name, 0, WHERE[name][2], 16), A("one", 0, WHERE[name][2] // 16), AF.Identity, None, x)
    I, NEG, HALF = A("idn"), A("neg"), A("half")

    def lists(t):
        copy("g" if t else "v", A("eu%d" % (t % 2)), A("entt", *cls(t)))
        act(A("ct%d" % (t % 2)), A("entt", *cls(t)), AF.Sign, A("cz"))
        runs = []
        for j, n in enumerate(TN):
            if runs and runs[-1][0] + runs[-1][2] == EK[j][0]:
                runs[-1][2] += n
            else:
                runs.append([EK[j][0], T0[j], n])
        for lo, at, n in runs:
            act(A("ek%d" % (t % 2), lo, lo + n), A("entt", *cls(t, at, n)), AF.Identity, A("n1k"))

    def repeat(t, queues):
        for r in range(16):
            copy(queues[r % len(queues)], A("xr%d" % (t % 2), r, 16 * NJ, 16), A("xw0", *cls(t, base=XO)))
        for j, n in enumerate(TN):
            sel(team("xs%d" % (t % 2), j), A("xw0", *cls(t, T0[j], n, XO)), [[1, n]], OP.is_ge,
                -sum(w for q, w in JUDGE[j] if q == "s"), 0)

    for c in range(4):
        vcp(A("yef", *cls(c)), A("enti", *cls(c)))
        act(A("lt", NJ * c, NJ * c + NJ), A("yef", *cls(c)), AF.Sign, A("cz"))
        E = A(("p0", "p2", "p4", "p3")[c], 0, NJ)
        mms(E, [(A("idf"), A("yef", *cls(c))), (A("ixe"), A("lt", NJ * c, NJ * c + NJ))])
        act(A("entt", *cls(c)), E, AF.Identity, A("c256"))
    lists(0)
    repeat(0, START)
    copy("g", A("uw"), A("usri"))
    ts(A("uq"), A("usri"), 15, None, OP.bitwise_and)
    act(A("w10"), A("uw", *cls(0)), AF.Identity, A("cw"), 0.0625)
    vcp(A("thf"), A("thi"))
    mm(A(KEEP, 0, 5), A("ee"), A("thf"), True, True)
    act(A("tha"), A(KEEP, 0, 5), AF.Copy)
    act(A("thc", 0, 1), A("tha", 0, 1), AF.Copy)

    def gather(b, off, lo, parts):
        at = 0
        for q, w in parts:
            copy(q, A("gb%d" % b, 16 * at, 16 * (at + w)), IND(A("xw%d" % b, 0, XE), A(off, lo + at, lo + at + w)))
            at += w

    def scans(G, mx, mn, lo, parts):
        for w in parts:
            hi = lo + 16 * w
            scan(A(mx, lo, hi), A("rm", 0, 16 * w), A(G, lo, hi), OP.add, OP.max)
            scan(A(mn, lo, hi), A("rn", 0, 16 * w), A(G, lo, hi), OP.add, OP.min)
            lo = hi

    def fin(p, early, mx, mn, late, out):
        mms(p, early + [(HALF, mx), (HALF, mn)] + late + [(I, A("cm", 0, p[2]))])
        act(out, p, AF.Abs, A("mgc"))

    def less(t, lo, n):
        return [(NEG, A("bt", *cls(t, lo, n))), (I, A("cq", 0, n)), (I, A("xs%d" % (t % 2), lo, lo + n))]

    def score(t, j):
        n, s, u, cut = TN[j], str(j), str(t % 2), CUTS[j]
        keys = BANKS[TEAMS[j][0]][0]
        mms(A(keys, 0, 128, 1, n), [(team("ct" + u, j), A("ict")), (A("one", 0, n), A("ik")), (A("one", 0, n), A("ig"))], True, False)
        per = 16 // cut
        turn = 0
        for m in range(cut):
            hi = n
            for q, w in reversed(JUDGE[j]):
                lo = hi - w
                d = A("ga" + s, 16 * lo + m, 16 * hi, cut)
                if q == "s":
                    gm, d = d, A(DBANKS[j][turn % 2], 0, per * w)
                    turn += 1
                    mms(d, [(NEG, A("xr" + u, 16 * (T0[j] + lo) + m, 16 * (T0[j] + hi), cut)), (I, gm)])
                act(A("mt" + s, per * (n * m + lo), per * (n * m + hi)), d, AF.Abs)
                hi = lo
            for e in range(per):
                mm(A(keys, cut * e + m, 128, 16, n), A("mt" + s, per * n * m + e, per * n * (m + 1), per), A("w16", 0, 128, 16),
                   False, (m, e) == (cut - 1, per - 1))

    def trial(t, j):
        n, s, u = TN[j], str(j), str(t % 2)
        b0, b1 = BANKS[TEAMS[j][0]]
        win = "xw%d" % TEAMS[j][0]
        K, top = A(b0, 0, 128, 1, n), A("cap" if AGAIN[j] else "top", 0, 128, 1, n)
        scan(A("r1" + s, 0, 128, 1, n), top, K, OP.max, OP.min)
        scan(A("mb" + s, 0, 128, 1, n), top, A("r1" + s, 15, 143, 1, n), OP.max, OP.min)
        ht = A("ht" + s, 0, 128, 1, n)
        tt(ht, K, A("mb" + s, 0, 128, 1, n), OP.is_equal)
        if AGAIN[j]:
            E = A(b1, 0, n)
            mms(E, [(I, A("ek" + u, EK[j][0], EK[j][0] + n)), (ht, A("ixo", 0, n, 1, n))])
            act(A("ou%d" % TEAMS[j][0], 0, n), E, AF.Relu, A("c1k"))
            for b in TEAMS[j]:
                gather(b, "ou%d" % TEAMS[j][0], N * b - T0[j], AGAIN[j])
                scans("gb%d" % b, "mx%d" % b, "mn%d" % b, 0, [w for _q, w in AGAIN[j]])
                fin(A(BANKS[b][0], 0, N), less(t, N * b, N)[:2], A("mx%d" % b, 15, 16 * N, 16), A("mn%d" % b, 15, 16 * N, 16), [],
                    A("xw%d" % b, ZO, ZO + N))
            return
        copy("g", A("t15" + s), A("ga" + s, 15, 16 * n, 16))
        for lo in (0, n):
            mm(A(b1, lo, lo + n), ht, A("idn", 0, n, 1, n), True, True)
        lo = min(EK[j])
        tt(A("dn" + s), A(b1, 0, 2 * n), A("ek" + u, lo, lo + 2 * n), OP.mult)
        W = sixteens(256 * (j % 2), 2 * n)
        mms(W, [(I, A("mk", lo, lo + 2 * n)), (A("blk"), A("dn" + s))])
        greatest(A("xl" + s, 0, n // 8), W)
        xl, pl = [A("xl" + s, (i - lo) // 16, (i - lo + n) // 16) for i in EK[j]]
        vcp(IND(A("ga" + s), pl), A("t15" + s))
        tt(A("ga" + s, 15, 16 * n, 16), IND(A(win, ZO), xl), team("xs" + u, j), OP.subtract)
        act(A("gk" + s), IND(A(win, 0, XE), xl), AF.Copy)
        for b in TEAMS[j]:
            lo = 16 * (N * b - T0[j])
            scans("ga" + s, "m0" + s, "n0" + s, lo, TSCANS)
            fin(A(BANKS[b][0], 0, N), less(t, N * b, N), A("m0" + s, lo + 15, lo + 16 * N, 16), A("n0" + s, lo + 15, lo + 16 * N, 16), [],
                A("xw%d" % b, ZO, ZO + N))

    def stay(t, j):
        n, s = TN[j], str(j)
        xs = team("xs%d" % (t % 2), j)
        at, late = 15, []
        if AGAIN[j]:
            scans("ga" + s, "m0" + s, "n0" + s, 0, TSCANS * len(TEAMS[j]))
        else:
            at, late = 14, [(HALF, A("rl" + s, 0, n)), (A("nhalf"), A("rl" + s, n, 2 * n))]
            mms(A(KEEP, NJ, NJ + n), [(I, A("gk" + s)), (NEG, xs), (NEG, A("m0" + s, at, 16 * n, 16))])
            mms(A(KEEP, NJ + n, NJ + 2 * n), [(NEG, A("gk" + s)), (I, xs), (I, A("n0" + s, at, 16 * n, 16))])
            act(A("rl" + s), A(KEEP, NJ, NJ + 2 * n), AF.Relu)
        fin(A(KEEP, NJ, NJ + n), less(t, T0[j], n), A("m0" + s, at, 16 * n, 16), A("n0" + s, at, 16 * n, 16), late, team("f0", j))
        for b in TEAMS[j]:
            mms(part(KEEP, b), [(NEG, part("f0", b)), (I, A("xw%d" % b, ZO, ZO + N))])

    def hop(t, h, b):
        s = str(b)
        b0, b1 = BANKS[b]
        z = A("xw" + s, ZO + N * (h - 1), ZO + N * h)
        was, wl = [A("wl" + s, 8 * i, 8 * i + N // 16) for i in ((h - 2) % 3, h - 1)]
        cm = A("cm", 0, N)
        F = A(b1, 0, N)
        mms(F, [(I, A("yc96")), (A("b16"), z), (I, cm), (NEG, cm), (A("nb16"), z),
                (A("i32k"), part("w1%d" % (t % 2), b) if h == 1 else A("ww" + s))])
        act(A("hot" + s), F, AF.Relu, A("p1c"), 2.0 ** 15)
        W = sixteens(128 * b, N)
        mms(W, [(I, A("mq")), (A("blk"), A("hot" + s))])
        tt(A("pq" + s), A("uq", *cls(t, N * b, N)) if h == 1 else IND(A("uq"), was), A("hot" + s), OP.min)
        Q = A(b0, 0, N)
        mms(Q, [(I, A("jc")), (A("f8k"), A("pq" + s))])
        act(A("aa" + s), Q, AF.Abs, A("bc", h - 1, h))
        greatest(wl, W)
        lo = N * (h - 1)
        tt(A("ou" + s, lo, lo + N), IND(A("entt"), wl), A("aa" + s), OP.min)
        act(A("bw" + s), IND(A("bt"), wl), AF.Identity, A("c25"))
        gather(b, "ou" + s, lo, HOP[h - 1][b])
        scans("gb" + s, "mx" + s, "mn" + s, 0, SCANS)
        fin(A(b0, 0, N), [(NEG, A("bw" + s))], A("mx" + s, 15, 16 * N, 16), A("mn" + s, 15, 16 * N, 16), [],
            A("xw" + s, ZO + N * h, ZO + N * (h + 1)) if h < 3 else A("z3" + s))
        if h < 3:
            act(A("ww" + s), IND(A("uw"), wl), AF.Identity, A("cw"), 0.0625)
        else:
            act(A("xv" + s), IND(A("xw" + s, XO, XG), wl), AF.Copy)
            ts(A("cl" + s), A("ou" + s), ZO - 1.0, XO - 1.0, OP.max, OP.min)
            cl = [A("cl" + s, N * i, N * i + N) for i in range(3)]
            none = [(A("i15"), A("one", 0, N)), (A("b1m"), part("ct%d" % (t % 2), b)), (I, A("cm3")), (NEG, A("cm3"))]
            mms(F, none * (not [a for j, a in zip(TEAMS, AGAIN) if b in j][0]) + [(A("i8k"), A("ca"))] + [(A("nf8k"), c) for c in cl]
                + [(I, A("cm2")), (NEG, A("cm2"))] + [(A("f8k"), c) for c in cl]
                + [(A("i8k"), A("cb")), (A("nb1"), A("xv" + s))], True, False)

    def effect(t, b):
        s = str(b)
        D = A(BANKS[b][1], 0, N)
        tt(A("mz" + s), A("xv" + s), A("z3" + s), OP.max)
        mms(D, [(A("nb1"), A("z3" + s)), (A("b2"), A("mz" + s))], False, True)
        ts(part("st", b), D, A("thc", t, t + 1), None, OP.is_le)
        tt(part("sd", b), part(KEEP, b), part("st", b), OP.mult)

    def hits(by):
        for j, n in enumerate(TN):
            mm(team("p0", j), A("ht%d" % j, 0, 128, 1, n), A(by, 0, n, 1, n), True, True)

    def close(t):
        tt(A("gt%d" % t), IND(A("sd"), A("sndl", 6 * t, 6 * t + 6)), A("f0g"), OP.add)
        ghosts = A("xw0", XG + 96 * t, XG + 96 * (t + 1))
        send(t, A("gt%d" % t), ghosts, (free(t, ghosts),))
        tt(A("xw0", *cls(t, base=XO)), A("f0"), A("sd"), OP.add)
        hits("idn")
        tt(A("hs"), A("p0", 0, NJ), A("st"), OP.mult)
        for b in range(1, NB):
            copy("g", A("xw%d" % b, *cls(t, base=XO)), A("xw0", *cls(t, base=XO)))
        for bank, tab, by in (("p1", "entt", "ixo"), ("p3", "yef", "i1152")):
            E = A(bank, 0, NJ)
            mms(E, [(A("idf"), A(tab, *cls(t))), (A(by), A("hs"))])
            act(A(tab, *cls(t)), E, AF.Copy)
        C, rr = A("p2", 0, NJ), A("rr")
        mm(C, A("one"), A("hs"), True, True)
        add("v", lambda e: e.tensor_reduce(out=rr[0], in_=C[0], axis=AX.X, op=OP.add), regs(C), regs(rr), vc(NJ))
        vcp(A("rri"), rr)
        ts(A("rrj"), A("rri"), 31, None, OP.bitwise_and)
        tt(A("thc", t + 1, t + 2), A("rrj"), A("tha", t + 1, t + 2), OP.add)

    def store(t, b):
        tt(part("hs", b), part("p0", b), part("st", b), OP.mult)
        tt(A("yef", *cls(t, N * b, N)), A("yef", *cls(t, N * b, N)), part("hs", b), OP.add)
        tt(A("xw0", *cls(t, N * b, N, XO)), part("f0", b), part("sd", b), OP.add)
        cols = slice(4 * N * b, 4 * N * (b + 1))
        xc = slice(XO + cols.start, XO + cols.stop)
        add("s", lambda e: e.dma_start(out=T.yx[:, cols], in_=T.xw0[:, xc]),
            [("xw0", xc.start, xc.stop, 1)], [], (0.1, 0, False), 2.0, "o%d" % (NB + b), 16, True)
        add("y", lambda e: e.dma_start(out=T.ye[:, cols], in_=T.yef[:, cols]),
            [("yef", cols.start, cols.stop, 1)], [], (0.1, 0, False), 2.0, "o%d" % b, 16, True)

    for t in range(5):
        step[2] = t
        u = str(t % 2)
        label("landed")
        lo, hi = (XG + 96 * (t - 1), XG + 96 * t) if t else (XG, XE)
        for b in range(1, NB):
            copy("g", A("xw%d" % b, lo, hi), A("xw0", lo, hi))
        for j in range(len(TEAMS)):
            label("gather", j)
            lo = 0
            for q, w in JUDGE[j]:
                at = T0[j] + lo
                out, what = A("ga%d" % j, 16 * lo, 16 * (lo + w)), IND(A("xw0", 0, XE), A("eu" + u, at, at + w))
                if q == "s":
                    act(out, what, AF.Copy)
                else:
                    tt(out, what, A("xr" + u, 16 * at, 16 * (at + w)), OP.subtract)
                lo += w
        for j in range(len(TEAMS)):
            label("score", j)
            score(t, j)
            label("least", j)
            trial(t, j)
        for j in range(len(TEAMS)):
            label("stay", j)
            stay(t, j)
        if t < 4:
            label("ahead")
            repeat(t + 1, "g")
            lists(t + 1)
            act(A("w1%d" % ((t + 1) % 2)), A("uw", *cls(t + 1)), AF.Identity, A("cw"), 0.0625)
            act(A("f0g"), IND(A("f0"), A("sndl", 6 * t, 6 * t + 6)), AF.Copy)
        for h in range(1, 4):
            for b in range(NB):
                label("hop", h, b)
                hop(t, h, b)
        for b in range(NB):
            label("effect", b)
            effect(t, b)
        if t < 4:
            label("end")
            close(t)
        else:
            label("out")
            hits("i1152")
            for b in range(NB):
                store(t, b)

    _edges(ops)
    if "order" not in PLAN:
        PLAN["order"] = _plan(ops)
    needed = [False] * len(ops)
    for o in ops:
        for j in o["pre"]:
            needed[j] = needed[j] or o["pre"][j]
    know = {}
    count = {}
    for i in PLAN["order"]:
        o = ops[i]
        q = o["q"]
        if q in "xz":
            count[o["sem"]] = o["amount"]
            o["done"] = (o["sem"], o["amount"])
            o["snap"] = {}
            continue
        kq = know.setdefault(q, {})
        want = sorted((j for j in o["pre"] if o["pre"][j]), key=lambda j: -j)
        for j in want:
            sm, c = ops[j]["done"]
            if kq.get(sm, 0) < c:
                same = [j2 for j2 in want if ops[j2]["done"][0] == sm]
                c = max(ops[j2]["done"][1] for j2 in same)
                eng[q].wait_ge(T.sem[sm], c)
                kq[sm] = c
                for j2 in same:
                    for a in ops[j2]["snap"]:
                        kq[a] = max(kq.get(a, 0), ops[j2]["snap"][a])
        ins = o["fn"](eng[q])
        o["snap"] = dict(kq)
        if o["sem"] or needed[i]:
            sm = o["sem"] or QS[q]
            count[sm] = count.get(sm, 0) + o["amount"]
            if not o["remote"]:
                ins.then_inc(T.sem[sm], o["amount"])
            o["done"] = (sm, count[sm])
            if not o["sem"]:
                o["snap"][sm] = count[sm]
    for sm in sorted(count):
        g.wait_ge(T.sem[sm], count[sm])
